import numpy as np
import ml_dtypes


def mxq(x, axis, fmt="e4m3"):
    dtype, down = {"e4m3": (ml_dtypes.float8_e4m3fn, 7), "e5m2": (ml_dtypes.float8_e5m2, 14)}[fmt]
    v = np.moveaxis(np.asarray(x, np.float32).astype(ml_dtypes.bfloat16).astype(np.float64), axis, -1)
    blocks = v.reshape(v.shape[:-1] + (-1, 32))
    amax = np.abs(blocks).max(-1, keepdims=True)
    byte = np.maximum(np.where(amax > 0, np.frexp(amax)[1] - 1 + 127, 0) - down, 1)
    scale = np.exp2(byte - 127.0)
    codes = (blocks / scale).astype(np.float32).astype(dtype).astype(np.float64)
    return np.moveaxis((codes * scale).reshape(v.shape), -1, axis)


WIDE = False


def mx_kscale(k):
    if not WIDE:
        return np.ones(k)
    levels = np.array([24, -24, 12, -12, 0])
    if k % 512:
        return np.exp2(np.random.permutation(np.resize(levels, k // 32))).repeat(32)
    a = np.empty((k // 512, 16))
    for p in range(k // 512):
        a[p, :8] = np.random.permutation(np.resize(levels, 8))
        for g in range(8):
            far = levels[np.abs(levels - a[p, g]) >= 10]
            a[p, g + 8] = far[np.random.randint(len(far))]
    return np.exp2(a.ravel()).repeat(32)


def f64(x):
    return np.asarray(x).astype(np.float64)


def striped(idx):
    return np.tile(idx.reshape(-1, 16).T, (8, 1)).astype(np.uint16)


def unstriped(offs):
    return offs[:16].T.reshape(-1).astype(np.int64)


E2M1 = np.array([0.0, 0.5, 1.0, 1.5, 2.0, 3.0, 4.0, 6.0, -0.0, -0.5, -1.0, -1.5, -2.0, -3.0, -4.0, -6.0])


def pack_weight(w, fmt):
    k, n = w.shape
    w = f64(np.asarray(w, np.float32).astype(ml_dtypes.bfloat16)).reshape(k // 32, 32, n)
    amax = np.abs(w).max(1)
    if fmt == "e4m3":
        byte = np.frexp(amax)[1] - 1 + 127 - 7
    else:
        mant, ex = np.frexp(amax / 6.0)
        byte = np.where(mant > 0.5, ex, ex - 1) + 127
    byte = np.clip(np.where(amax > 0, byte, 1), 1, 254)
    scaled = (w * np.exp2(127.0 - byte)[:, None, :]).reshape(k, n).astype(np.float32)
    by_word = np.ascontiguousarray(scaled.reshape(k // 512, 128, 4, n).transpose(0, 1, 3, 2))
    if fmt == "e4m3":
        words = by_word.astype(ml_dtypes.float8_e4m3fn).view(np.uint8)
    else:
        c = by_word.astype(ml_dtypes.float4_e2m1fn).view(np.uint8) & 0xF
        words = (c[..., 0::2] | (c[..., 1::2] << 4)).reshape(k // 512, 128, 2 * n)
    return np.ascontiguousarray(words), np.ascontiguousarray(byte.astype(np.uint8).reshape(k // 512, 16, n))


def unpack_weight(words, scales, fmt):
    g, _, n = scales.shape
    words = np.ascontiguousarray(words).reshape(g, 128, n, -1)
    if fmt == "e4m3":
        vals = words.view(ml_dtypes.float8_e4m3fn).astype(np.float64)
    else:
        nib = np.empty((g, 128, n, 4), np.uint8)
        nib[..., 0::2] = words & 0xF
        nib[..., 1::2] = words >> 4
        vals = E2M1[nib]
    vals = vals * np.repeat(np.exp2(scales.astype(np.float64) - 127.0), 8, axis=1)[..., None]
    return vals.transpose(0, 1, 3, 2).reshape(g * 512, n)


def pack_table4(v):
    words, scales = pack_weight(v, "e2m1")
    g, t = words.shape[0] // 2, v.shape[1]
    return np.ascontiguousarray(words.reshape(g, 2, 128, t, 2).transpose(0, 2, 3, 1, 4).reshape(g, 128, t, 4)), scales


def unpack_table4(words, scales):
    g, _, t, _ = words.shape
    return unpack_weight(words.reshape(g, 128, t, 2, 2).transpose(0, 3, 1, 2, 4).reshape(2 * g, 128, 2 * t), scales, "e2m1")


K, L, N, T, J = 1024, 512, 1024, 2048, 1024


def setup_inputs():
    n = np.random.standard_normal
    s = mx_kscale(K)[:, None]
    s2 = mx_kscale(L)[:, None]
    p_tab = pack_table4(n((K, T)) * s)
    return {
        "tab_words": p_tab[0],
        "tab_scales": p_tab[1],
        "wt": (n((K, N)) / np.sqrt(K) / s).astype(np.float32),
        "x": (n((L, J)) * s2).astype(np.float32),
        "wx": (n((L, N)) / np.sqrt(L) / s2).astype(np.float32),
        "rT": (n((N, T))).astype(np.float32),
        "offs": striped(np.random.permutation(T)[:J]),
    }


def reference(tab_words, tab_scales, wt, x, wx, rT, offs):
    idx = unstriped(offs)
    tab_ = unpack_table4(tab_words, tab_scales)[:, idx]
    wt_q_ = mxq(f64(wt), 0, "e4m3")
    wt_r_ = mxq(f64(wt) - wt_q_, 0, "e4m3")
    x_ = mxq(f64(x), 0, "e4m3")
    wx_ = mxq(f64(wx), 0, "e4m3")
    y = wt_q_.T @ tab_ + wt_r_.T @ tab_ + wx_.T @ x_
    return y + f64(rT)[:, idx]

@@ -1,0 +1,224 @@
+from contextlib import ExitStack
+
+import concourse.mybir as mybir
+from concourse.masks import make_identity
+
+K, L, N, T, J = 1024, 512, 1024, 2048, 1024
+FLOPS = 2 * (2 * K + L) * N * J + 2 * 512 * K * N
+
+F32 = mybir.dt.float32
+BF16 = mybir.dt.bfloat16
+I32 = mybir.dt.int32
+U32 = mybir.dt.uint32
+U16 = mybir.dt.uint16
+U8 = mybir.dt.uint8
+FP8X4 = mybir.dt.float8_e4m3fn_x4
+FP4X4 = mybir.dt.float4_e2m1fn_x4
+ALU = mybir.AluOpType
+
+P = 128
+PACK = 4
+K_PASS = P * PACK
+HALF = 512
+RUN = 2
+
+
+def tile_list_tiert_resL_kernel(tc, tab_words, tab_scales, wt, x, wx, rT, offs, out):
+    nc = tc.nc
+    with ExitStack() as ctx:
+        keep = ctx.enter_context(tc.tile_pool(name="keep", bufs=1))
+        big = ctx.enter_context(tc.tile_pool(name="big", bufs=16))
+        cast_pool = ctx.enter_context(tc.tile_pool(name="cast", bufs=3))
+        rest_pool = ctx.enter_context(tc.tile_pool(name="rest", bufs=2))
+        sums_pool = ctx.enter_context(tc.tile_pool(name="sums", bufs=2))
+        deq_psum = ctx.enter_context(tc.psum_pool(name="deq", bufs=4))
+        acc_psum = ctx.enter_context(tc.psum_pool(name="acc", bufs=4))
+
+        offsets = keep.tile([P, J // 16], U16, name="offsets")
+        nc.sync.dma_start(offsets[:], offs)
+
+        scale_window = keep.tile([P, T], U8, name="scale_window", align_bytes=64)
+        nc.vector.memset(scale_window[:].bitcast(I32), 0)
+        for q in range(4):
+            nc.sync.dma_start(
+                out=scale_window[32 * q : 32 * q + 8, :].bitcast(I32),
+                in_=tab_scales[:, 4 * q : 4 * q + 4, :].bitcast(I32),
+            )
+
+        raw = {}
+
+        def load_rows(name, src, a, h):
+            piece = big.tile([P, PACK, HALF], F32, name="piece", tag="big")
+            rows = src[a * K_PASS : (a + 1) * K_PASS, :].rearrange("(p t) n -> p t n", t=PACK)
+            nc.sync.dma_start(out=piece[:], in_=rows[:, :, h * HALF : (h + 1) * HALF])
+            raw[(name, a, h)] = piece
+
+        def load_record(m):
+            window = big.tile([P, T], F32, name="record", tag="big")
+            nc.sync.dma_start(out=window[:], in_=rT[m * P : (m + 1) * P, :])
+            raw[("rT", m)] = window
+
+        word_window = big.tile([P, T], I32, name="word_window", tag="big")
+        nc.sync.dma_start(out=word_window[:], in_=tab_words[0].rearrange("p t b -> p (t b)").bitcast(I32))
+        load_rows("wt", wt, 0, 0)
+        load_record(0)
+        load_rows("wt", wt, 1, 0)
+        load_rows("x", x, 0, 0)
+        load_record(1)
+        load_rows("x", x, 0, 1)
+        load_rows("wx", wx, 0, 0)
+        load_record(2)
+        load_rows("wt", wt, 0, 1)
+        load_record(3)
+        load_rows("wt", wt, 1, 1)
+        load_rows("wx", wx, 0, 1)
+        load_record(4)
+        load_record(5)
+        load_record(6)
+        load_record(7)
+
+        identity = keep.tile([P, P], BF16, name="identity")
+        make_identity(nc, identity[:])
+        eye = keep.tile([P, PACK * K_PASS], BF16, name="eye", align_bytes=64)
+        nc.vector.memset(eye[:].bitcast(I32), 0)
+        for t in range(PACK):
+            nc.scalar.copy(out=eye[:, t * K_PASS + t : (t + 1) * K_PASS : PACK], in_=identity[:])
+
+        codes = {}
+
+        def quantise(key, grouped):
+            words = keep.tile([P, HALF], U32, name="codes_%s%d%d" % key, align_bytes=64)
+            scales = keep.tile([P, HALF], U8, name="scales_%s%d%d" % key, align_bytes=64)
+            nc.vector.quantize_mx(out=words[:].bitcast(FP8X4), scales=scales[:], in_=grouped)
+            codes[key] = (words, scales)
+
+        picked_scales = keep.tile([P, J], U8, name="picked_scales", align_bytes=64)
+        nc.vector.tensor_copy(picked_scales[:], scale_window[:].indirect(offsets[:]))
+        second_scales = keep.tile([P, J], U8, name="second_scales", align_bytes=64)
+        nc.vector.memset(second_scales[:].bitcast(I32), 0)
+        nc.scalar.dma_start(out=second_scales[0:112, :].bitcast(I32), in_=picked_scales[4:116, :].bitcast(I32))
+        table_scales = [picked_scales, second_scales]
+        picked_words = keep.tile([P, J], U32, name="picked_words", align_bytes=64)
+        nc.vector.tensor_copy(picked_words[:], word_window[:].bitcast(U32).indirect(offsets[:]))
+        quantise(("eye", 0, 0), eye[:])
+        table_words = keep.tile([P, 2 * 2 * J], U8, name="table_words", align_bytes=64)
+        nc.vector.tensor_copy(
+            out=table_words[:].bitcast(U16).rearrange("p (d j) -> p d j", d=2),
+            in_=picked_words[:].bitcast(U16).rearrange("p (j d) -> p d j", d=2),
+        )
+
+        rounded = {}
+
+        def cast(key):
+            grouped = cast_pool.tile([P, HALF, PACK], BF16, name="grouped", align_bytes=64)
+            nc.scalar.copy(
+                out=grouped[:].rearrange("p (c i) t -> p c t i", i=RUN),
+                in_=raw[key][:].rearrange("p t (c i) -> p c t i", i=RUN),
+            )
+            rounded[key] = grouped
+
+        def quantise_cast(key):
+            quantise(key, rounded[key][:].rearrange("p n t -> p (n t)"))
+
+        def leftover(a, h):
+            eye_words, eye_scales = codes[("eye", 0, 0)]
+            words, scales = codes[("wt", a, h)]
+            rest = rest_pool.tile([P, HALF, PACK], BF16, name="rest", align_bytes=64)
+            for b in range(HALF // P):
+                cols = slice(b * P, (b + 1) * P)
+                bank = deq_psum.tile([P, PACK, P], F32, name="deq")
+                for t in range(PACK):
+                    sel = slice(t * P, (t + 1) * P)
+                    nc.tensor.matmul_mx(
+                        out=bank[:, t, :], lhsT=eye_words[:, sel].bitcast(FP8X4), lhsT_scale=eye_scales[:, sel],
+                        rhs=words[:, cols].bitcast(FP8X4), rhs_scale=scales[:, cols], start=True, stop=True,
+                    )
+                nc.vector.tensor_tensor(
+                    out=rest[:, cols, :].rearrange("p (c i) t -> p c t i", i=RUN),
+                    in0=raw[("wt", a, h)][:, :, cols].rearrange("p t (c i) -> p c t i", i=RUN),
+                    in1=bank[:].rearrange("p t (c i) -> p c t i", i=RUN),
+                    op=ALU.subtract,
+                )
+            rounded[("wr", a, h)] = rest
+
+        results = {}
+
+        def gather_record(m):
+            result = keep.tile([P, J], F32, name="result%d" % m)
+            nc.vector.tensor_copy(result[:], raw[("rT", m)][:].indirect(offsets[:]))
+            results[m] = result
+
+        def product(m):
+            h, cols = m // 4, slice((m % 4) * P, (m % 4 + 1) * P)
+            banks = [acc_psum.tile([P, HALF], F32, name="acc") for jh in range(2)]
+            terms = [("wx", 0), ("wt", 0), ("wt", 1), ("wr", 0), ("wr", 1)]
+            for s, (name, a) in enumerate(terms):
+                words, scales = codes[(name, a, h)]
+                for jh in range(2):
+                    if name == "wx":
+                        rhs, rhs_scale = codes[("x", 0, jh)][0][:].bitcast(FP8X4), codes[("x", 0, jh)][1][:]
+                    else:
+                        first = a * J + jh * HALF
+                        rhs = table_words[:, 2 * first : 2 * (first + HALF)].bitcast(FP4X4)
+                        rhs_scale = table_scales[a][:, jh * HALF : (jh + 1) * HALF]
+                    nc.tensor.matmul_mx(
+                        out=banks[jh][:], lhsT=words[:, cols].bitcast(FP8X4), lhsT_scale=scales[:, cols],
+                        rhs=rhs, rhs_scale=rhs_scale, start=(s == 0), stop=(s == len(terms) - 1),
+                    )
+            return banks
+
+        def finish_vector(m, banks):
+            result = results[m]
+            for jh in range(2):
+                half = result[:, jh * HALF : (jh + 1) * HALF]
+                nc.vector.tensor_tensor(out=half, in0=banks[jh][:], in1=half, op=ALU.add)
+            nc.sync.dma_start(out=out[m * P : (m + 1) * P, :], in_=result[:])
+
+        def finish_pool(m, banks):
+            result = results[m]
+            sums = sums_pool.tile([P, J], F32, name="sums")
+            for jh in range(2):
+                nc.scalar.copy(out=sums[:, jh * HALF : (jh + 1) * HALF], in_=banks[jh][:])
+            nc.gpsimd.tensor_tensor(out=result[:], in0=result[:], in1=sums[:], op=ALU.add)
+            nc.sync.dma_start(out=out[m * P : (m + 1) * P, :], in_=result[:])
+
+        cast(("wt", 0, 0))
+        quantise_cast(("wt", 0, 0))
+        gather_record(0)
+        leftover(0, 0)
+        cast(("wt", 1, 0))
+        quantise_cast(("wt", 1, 0))
+        quantise_cast(("wr", 0, 0))
+        leftover(1, 0)
+        cast(("x", 0, 0))
+        quantise_cast(("x", 0, 0))
+        quantise_cast(("wr", 1, 0))
+        gather_record(1)
+        cast(("x", 0, 1))
+        quantise_cast(("x", 0, 1))
+        cast(("wx", 0, 0))
+        quantise_cast(("wx", 0, 0))
+        gather_record(2)
+        finish_vector(0, product(0))
+        cast(("wt", 0, 1))
+        gather_record(3)
+        quantise_cast(("wt", 0, 1))
+        finish_vector(1, product(1))
+        leftover(0, 1)
+        cast(("wt", 1, 1))
+        quantise_cast(("wt", 1, 1))
+        quantise_cast(("wr", 0, 1))
+        finish_vector(2, product(2))
+        leftover(1, 1)
+        cast(("wx", 0, 1))
+        quantise_cast(("wx", 0, 1))
+        quantise_cast(("wr", 1, 1))
+        finish_vector(3, product(3))
+        gather_record(4)
+        gather_record(5)
+        finish_vector(4, product(4))
+        gather_record(6)
+        finish_vector(5, product(5))
+        gather_record(7)
+        finish_vector(6, product(6))
+        finish_vector(7, product(7))

@@ -20,17 +20,18 @@ P = 128
 PACK = 4
 K_PASS = P * PACK
 HALF = 512
-RUN = 2
+RUN_CAST = 2
+RUN_REST = 2
 
 
 def tile_list_tiert_resL_kernel(tc, tab_words, tab_scales, wt, x, wx, rT, offs, out):
     nc = tc.nc
     with ExitStack() as ctx:
         keep = ctx.enter_context(tc.tile_pool(name="keep", bufs=1))
-        big = ctx.enter_context(tc.tile_pool(name="big", bufs=16))
-        cast_pool = ctx.enter_context(tc.tile_pool(name="cast", bufs=3))
+        loads = ctx.enter_context(tc.tile_pool(name="loads", bufs=15))
+        cast_pool = ctx.enter_context(tc.tile_pool(name="cast", bufs=4))
         rest_pool = ctx.enter_context(tc.tile_pool(name="rest", bufs=2))
-        sums_pool = ctx.enter_context(tc.tile_pool(name="sums", bufs=2))
+        picked_pool = ctx.enter_context(tc.tile_pool(name="picked", bufs=3))
         deq_psum = ctx.enter_context(tc.psum_pool(name="deq", bufs=4))
         acc_psum = ctx.enter_context(tc.psum_pool(name="acc", bufs=4))
 
@@ -38,44 +39,48 @@ def tile_list_tiert_resL_kernel(tc, tab_words, tab_scales, wt, x, wx, rT, offs, 
         nc.sync.dma_start(offsets[:], offs)
 
         scale_window = keep.tile([P, T], U8, name="scale_window", align_bytes=64)
-        nc.vector.memset(scale_window[:].bitcast(I32), 0)
+        nc.gpsimd.memset(scale_window[:].bitcast(I32), 0)
         for q in range(4):
             nc.sync.dma_start(
                 out=scale_window[32 * q : 32 * q + 8, :].bitcast(I32),
                 in_=tab_scales[:, 4 * q : 4 * q + 4, :].bitcast(I32),
             )
 
+        sources = {"wt0": wt[0:K_PASS, :], "wt1": wt[K_PASS:K, :], "x": x, "wx": wx}
         raw = {}
 
-        def load_rows(name, src, a, h):
-            piece = big.tile([P, PACK, HALF], F32, name="piece", tag="big")
-            rows = src[a * K_PASS : (a + 1) * K_PASS, :].rearrange("(p t) n -> p t n", t=PACK)
-            nc.sync.dma_start(out=piece[:], in_=rows[:, :, h * HALF : (h + 1) * HALF])
-            raw[(name, a, h)] = piece
+        def load_piece(name, first, width):
+            piece = loads.tile([P, PACK, width], F32, name="piece", tag="load")
+            rows = sources[name].rearrange("(p t) n -> p t n", t=PACK)
+            nc.sync.dma_start(out=piece[:], in_=rows[:, :, first : first + width])
+            raw[(name, first)] = piece
 
         def load_record(m):
-            window = big.tile([P, T], F32, name="record", tag="big")
+            window = loads.tile([P, T], F32, name="record", tag="load")
             nc.sync.dma_start(out=window[:], in_=rT[m * P : (m + 1) * P, :])
             raw[("rT", m)] = window
 
-        word_window = big.tile([P, T], I32, name="word_window", tag="big")
+        load_piece("wt0", 0, 256)
+        word_window = loads.tile([P, T], I32, name="word_window", tag="load")
         nc.sync.dma_start(out=word_window[:], in_=tab_words[0].rearrange("p t b -> p (t b)").bitcast(I32))
-        load_rows("wt", wt, 0, 0)
-        load_record(0)
-        load_rows("wt", wt, 1, 0)
-        load_rows("x", x, 0, 0)
-        load_record(1)
-        load_rows("x", x, 0, 1)
-        load_rows("wx", wx, 0, 0)
-        load_record(2)
-        load_rows("wt", wt, 0, 1)
-        load_record(3)
-        load_rows("wt", wt, 1, 1)
-        load_rows("wx", wx, 0, 1)
-        load_record(4)
-        load_record(5)
-        load_record(6)
-        load_record(7)
+        load_piece("wt0", 256, 256)
+        load_piece("wt1", 0, HALF)
+        load_piece("wt0", HALF, HALF)
+
+        picked_scales = keep.tile([P, J], U8, name="picked_scales", align_bytes=64)
+        nc.vector.tensor_copy(picked_scales[:], scale_window[:].indirect(offsets[:]))
+        second_scales = keep.tile([P, J], U8, name="second_scales", align_bytes=64)
+        nc.vector.memset(second_scales[:].bitcast(I32), 0)
+        nc.sync.dma_start(out=second_scales[0:112, :].bitcast(I32), in_=picked_scales[4:116, :].bitcast(I32))
+        table_scales = [picked_scales, second_scales]
+
+        load_piece("wt1", HALF, HALF)
+        load_piece("x", 0, HALF)
+        load_piece("wx", 0, HALF)
+        load_piece("x", HALF, HALF)
+        load_piece("wx", HALF, HALF)
+        for m in range(N // P):
+            load_record(m)
 
         identity = keep.tile([P, P], BF16, name="identity")
         make_identity(nc, identity[:])
@@ -84,141 +89,115 @@ def tile_list_tiert_resL_kernel(tc, tab_words, tab_scales, wt, x, wx, rT, offs, 
         for t in range(PACK):
             nc.scalar.copy(out=eye[:, t * K_PASS + t : (t + 1) * K_PASS : PACK], in_=identity[:])
 
-        codes = {}
+        words, scales = {}, {}
+        for name, width in (("eye", PACK * P), ("wt0", N), ("wt1", N), ("wr0", N), ("wr1", N), ("x", J), ("wx", N)):
+            words[name] = keep.tile([P, width], U32, name="words_" + name, align_bytes=64)
+            scales[name] = keep.tile([P, width], U8, name="scales_" + name, align_bytes=64)
 
-        def quantise(key, grouped):
-            words = keep.tile([P, HALF], U32, name="codes_%s%d%d" % key, align_bytes=64)
-            scales = keep.tile([P, HALF], U8, name="scales_%s%d%d" % key, align_bytes=64)
-            nc.vector.quantize_mx(out=words[:].bitcast(FP8X4), scales=scales[:], in_=grouped)
-            codes[key] = (words, scales)
+        def quantise(name, first, grouped):
+            cols = slice(first, first + grouped.shape[1] // PACK)
+            nc.vector.quantize_mx(out=words[name][:, cols].bitcast(FP8X4), scales=scales[name][:, cols], in_=grouped)
 
-        picked_scales = keep.tile([P, J], U8, name="picked_scales", align_bytes=64)
-        nc.vector.tensor_copy(picked_scales[:], scale_window[:].indirect(offsets[:]))
-        second_scales = keep.tile([P, J], U8, name="second_scales", align_bytes=64)
-        nc.vector.memset(second_scales[:].bitcast(I32), 0)
-        nc.scalar.dma_start(out=second_scales[0:112, :].bitcast(I32), in_=picked_scales[4:116, :].bitcast(I32))
-        table_scales = [picked_scales, second_scales]
-        picked_words = keep.tile([P, J], U32, name="picked_words", align_bytes=64)
-        nc.vector.tensor_copy(picked_words[:], word_window[:].bitcast(U32).indirect(offsets[:]))
-        quantise(("eye", 0, 0), eye[:])
-        table_words = keep.tile([P, 2 * 2 * J], U8, name="table_words", align_bytes=64)
-        nc.vector.tensor_copy(
-            out=table_words[:].bitcast(U16).rearrange("p (d j) -> p d j", d=2),
-            in_=picked_words[:].bitcast(U16).rearrange("p (j d) -> p d j", d=2),
-        )
+        quantise("eye", 0, eye[:])
 
-        rounded = {}
-
-        def cast(key):
-            grouped = cast_pool.tile([P, HALF, PACK], BF16, name="grouped", align_bytes=64)
+        def cast_and_quantise(name, first):
+            piece = raw[(name, first)]
+            grouped = cast_pool.tile([P, piece.shape[2], PACK], BF16, name="grouped", align_bytes=64)
             nc.scalar.copy(
-                out=grouped[:].rearrange("p (c i) t -> p c t i", i=RUN),
-                in_=raw[key][:].rearrange("p t (c i) -> p c t i", i=RUN),
+                out=grouped[:].rearrange("p (c i) t -> p c t i", i=RUN_CAST),
+                in_=piece[:].rearrange("p t (c i) -> p c t i", i=RUN_CAST),
             )
-            rounded[key] = grouped
+            quantise(name, first, grouped[:].rearrange("p n t -> p (n t)"))
 
-        def quantise_cast(key):
-            quantise(key, rounded[key][:].rearrange("p n t -> p (n t)"))
+        rests = {}
 
-        def leftover(a, h):
-            eye_words, eye_scales = codes[("eye", 0, 0)]
-            words, scales = codes[("wt", a, h)]
+        def leftover(a, first):
+            name = "wt%d" % a
             rest = rest_pool.tile([P, HALF, PACK], BF16, name="rest", align_bytes=64)
-            for b in range(HALF // P):
-                cols = slice(b * P, (b + 1) * P)
+            for b in range(0, HALF, P):
+                col = first + b
+                start = max(s for n, s in raw if n == name and s <= col)
                 bank = deq_psum.tile([P, PACK, P], F32, name="deq")
                 for t in range(PACK):
                     sel = slice(t * P, (t + 1) * P)
                     nc.tensor.matmul_mx(
-                        out=bank[:, t, :], lhsT=eye_words[:, sel].bitcast(FP8X4), lhsT_scale=eye_scales[:, sel],
-                        rhs=words[:, cols].bitcast(FP8X4), rhs_scale=scales[:, cols], start=True, stop=True,
+                        out=bank[:, t, :],
+                        lhsT=words["eye"][:, sel].bitcast(FP8X4), lhsT_scale=scales["eye"][:, sel],
+                        rhs=words[name][:, col : col + P].bitcast(FP8X4), rhs_scale=scales[name][:, col : col + P],
+                        start=True, stop=True,
                     )
                 nc.vector.tensor_tensor(
-                    out=rest[:, cols, :].rearrange("p (c i) t -> p c t i", i=RUN),
-                    in0=raw[("wt", a, h)][:, :, cols].rearrange("p t (c i) -> p c t i", i=RUN),
-                    in1=bank[:].rearrange("p t (c i) -> p c t i", i=RUN),
+                    out=rest[:, b : b + P, :].rearrange("p (c i) t -> p c t i", i=RUN_REST),
+                    in0=raw[(name, start)][:, :, col - start : col - start + P].rearrange("p t (c i) -> p c t i", i=RUN_REST),
+                    in1=bank[:].rearrange("p t (c i) -> p c t i", i=RUN_REST),
                     op=ALU.subtract,
                 )
-            rounded[("wr", a, h)] = rest
+            rests[(a, first)] = rest
 
-        results = {}
+        def quantise_leftover(a, first):
+            quantise("wr%d" % a, first, rests[(a, first)][:].rearrange("p n t -> p (n t)"))
 
-        def gather_record(m):
-            result = keep.tile([P, J], F32, name="result%d" % m)
-            nc.vector.tensor_copy(result[:], raw[("rT", m)][:].indirect(offsets[:]))
-            results[m] = result
+        picked_words = keep.tile([P, J], U32, name="picked_words", align_bytes=64)
+        table_words = keep.tile([P, 2 * 2 * J], U8, name="table_words", align_bytes=64)
 
-        def product(m):
-            h, cols = m // 4, slice((m % 4) * P, (m % 4 + 1) * P)
-            banks = [acc_psum.tile([P, HALF], F32, name="acc") for jh in range(2)]
-            terms = [("wx", 0), ("wt", 0), ("wt", 1), ("wr", 0), ("wr", 1)]
-            for s, (name, a) in enumerate(terms):
-                words, scales = codes[(name, a, h)]
-                for jh in range(2):
+        cast_and_quantise("wt0", 0)
+        nc.vector.tensor_copy(picked_words[:], word_window[:].bitcast(U32).indirect(offsets[:]))
+        cast_and_quantise("wt0", 256)
+        leftover(0, 0)
+        cast_and_quantise("wt1", 0)
+        nc.vector.tensor_copy(
+            out=table_words[:].bitcast(U16).rearrange("p (d j) -> p d j", d=2),
+            in_=picked_words[:].bitcast(U16).rearrange("p (j d) -> p d j", d=2),
+        )
+        quantise_leftover(0, 0)
+        leftover(1, 0)
+        cast_and_quantise("wt0", HALF)
+        quantise_leftover(1, 0)
+        cast_and_quantise("x", 0)
+        cast_and_quantise("wx", 0)
+        cast_and_quantise("x", HALF)
+        leftover(0, HALF)
+        cast_and_quantise("wt1", HALF)
+        quantise_leftover(0, HALF)
+        leftover(1, HALF)
+        quantise_leftover(1, HALF)
+        cast_and_quantise("wx", HALF)
+
+        terms = ("wt0", "wt1", "wr0", "wr1", "wx")
+        halves = [slice(0, HALF), slice(HALF, J)]
+        tiles = N // P
+        for m in range(tiles):
+            rows = slice(m * P, (m + 1) * P)
+            window = raw[("rT", m)]
+            picked = picked_pool.tile([P, J], F32, name="picked")
+            if m < tiles - 1:
+                nc.vector.tensor_copy(picked[:], window[:].indirect(offsets[:]))
+            else:
+                for half in halves:
+                    nc.vector.tensor_copy(picked[:, half], window[:].indirect(offsets[:, half.start // 16 : half.stop // 16]))
+
+            banks = [acc_psum.tile([P, HALF], F32, name="acc") for half in halves]
+            for s, name in enumerate(terms):
+                for bank, half in zip(banks, halves):
                     if name == "wx":
-                        rhs, rhs_scale = codes[("x", 0, jh)][0][:].bitcast(FP8X4), codes[("x", 0, jh)][1][:]
+                        rhs, rhs_scale = words["x"][:, half].bitcast(FP8X4), scales["x"][:, half]
                     else:
-                        first = a * J + jh * HALF
-                        rhs = table_words[:, 2 * first : 2 * (first + HALF)].bitcast(FP4X4)
-                        rhs_scale = table_scales[a][:, jh * HALF : (jh + 1) * HALF]
+                        a = int(name[2])
+                        rhs = table_words[:, 2 * (a * J + half.start) : 2 * (a * J + half.stop)].bitcast(FP4X4)
+                        rhs_scale = table_scales[a][:, half]
                     nc.tensor.matmul_mx(
-                        out=banks[jh][:], lhsT=words[:, cols].bitcast(FP8X4), lhsT_scale=scales[:, cols],
+                        out=bank[:], lhsT=words[name][:, rows].bitcast(FP8X4), lhsT_scale=scales[name][:, rows],
                         rhs=rhs, rhs_scale=rhs_scale, start=(s == 0), stop=(s == len(terms) - 1),
                     )
-            return banks
 
-        def finish_vector(m, banks):
-            result = results[m]
-            for jh in range(2):
-                half = result[:, jh * HALF : (jh + 1) * HALF]
-                nc.vector.tensor_tensor(out=half, in0=banks[jh][:], in1=half, op=ALU.add)
-            nc.sync.dma_start(out=out[m * P : (m + 1) * P, :], in_=result[:])
-
-        def finish_pool(m, banks):
-            result = results[m]
-            sums = sums_pool.tile([P, J], F32, name="sums")
-            for jh in range(2):
-                nc.scalar.copy(out=sums[:, jh * HALF : (jh + 1) * HALF], in_=banks[jh][:])
-            nc.gpsimd.tensor_tensor(out=result[:], in0=result[:], in1=sums[:], op=ALU.add)
-            nc.sync.dma_start(out=out[m * P : (m + 1) * P, :], in_=result[:])
-
-        cast(("wt", 0, 0))
-        quantise_cast(("wt", 0, 0))
-        gather_record(0)
-        leftover(0, 0)
-        cast(("wt", 1, 0))
-        quantise_cast(("wt", 1, 0))
-        quantise_cast(("wr", 0, 0))
-        leftover(1, 0)
-        cast(("x", 0, 0))
-        quantise_cast(("x", 0, 0))
-        quantise_cast(("wr", 1, 0))
-        gather_record(1)
-        cast(("x", 0, 1))
-        quantise_cast(("x", 0, 1))
-        cast(("wx", 0, 0))
-        quantise_cast(("wx", 0, 0))
-        gather_record(2)
-        finish_vector(0, product(0))
-        cast(("wt", 0, 1))
-        gather_record(3)
-        quantise_cast(("wt", 0, 1))
-        finish_vector(1, product(1))
-        leftover(0, 1)
-        cast(("wt", 1, 1))
-        quantise_cast(("wt", 1, 1))
-        quantise_cast(("wr", 0, 1))
-        finish_vector(2, product(2))
-        leftover(1, 1)
-        cast(("wx", 0, 1))
-        quantise_cast(("wx", 0, 1))
-        quantise_cast(("wr", 1, 1))
-        finish_vector(3, product(3))
-        gather_record(4)
-        gather_record(5)
-        finish_vector(4, product(4))
-        gather_record(6)
-        finish_vector(5, product(5))
-        gather_record(7)
-        finish_vector(6, product(6))
-        finish_vector(7, product(7))
+            result = keep.tile([P, J], F32, name="result%d" % m)
+            if m < tiles - 1:
+                for bank, half in zip(banks, halves):
+                    nc.scalar.copy(out=result[:, half], in_=bank[:])
+                for part in halves if m == tiles - 2 else [slice(0, J)]:
+                    nc.gpsimd.tensor_tensor(out=result[:, part], in0=result[:, part], in1=picked[:, part], op=ALU.add)
+                    nc.sync.dma_start(out=out[rows, part], in_=result[:, part])
+            else:
+                for bank, half in zip(banks, halves):
+                    nc.vector.tensor_tensor(out=result[:, half], in0=bank[:], in1=picked[:, half], op=ALU.add)
+                    nc.sync.dma_start(out=out[rows, half], in_=result[:, half])

@@ -20,6 +20,7 @@ P = 128
 PACK = 4
 K_PASS = P * PACK
 HALF = 512
+QUARTER = 256
 RUN_CAST = 2
 RUN_REST = 2
 
@@ -29,17 +30,15 @@ def tile_list_tiert_resL_kernel(tc, tab_words, tab_scales, wt, x, wx, rT, offs, 
     with ExitStack() as ctx:
         keep = ctx.enter_context(tc.tile_pool(name="keep", bufs=1))
         loads = ctx.enter_context(tc.tile_pool(name="loads", bufs=15))
-        cast_pool = ctx.enter_context(tc.tile_pool(name="cast", bufs=4))
-        rest_pool = ctx.enter_context(tc.tile_pool(name="rest", bufs=2))
         picked_pool = ctx.enter_context(tc.tile_pool(name="picked", bufs=3))
-        deq_psum = ctx.enter_context(tc.psum_pool(name="deq", bufs=4))
-        acc_psum = ctx.enter_context(tc.psum_pool(name="acc", bufs=4))
+        decoded_pool = ctx.enter_context(tc.tile_pool(name="decoded", bufs=2))
+        psum = ctx.enter_context(tc.psum_pool(name="psum", bufs=1))
 
         offsets = keep.tile([P, J // 16], U16, name="offsets")
         nc.sync.dma_start(offsets[:], offs)
 
         scale_window = keep.tile([P, T], U8, name="scale_window", align_bytes=64)
-        nc.gpsimd.memset(scale_window[:].bitcast(I32), 0)
+        nc.vector.memset(scale_window[:].bitcast(I32), 0)
         for q in range(4):
             nc.sync.dma_start(
                 out=scale_window[32 * q : 32 * q + 8, :].bitcast(I32),
@@ -60,25 +59,30 @@ def tile_list_tiert_resL_kernel(tc, tab_words, tab_scales, wt, x, wx, rT, offs, 
             nc.sync.dma_start(out=window[:], in_=rT[m * P : (m + 1) * P, :])
             raw[("rT", m)] = window
 
-        load_piece("wt0", 0, 256)
         word_window = loads.tile([P, T], I32, name="word_window", tag="load")
-        nc.sync.dma_start(out=word_window[:], in_=tab_words[0].rearrange("p t b -> p (t b)").bitcast(I32))
-        load_piece("wt0", 256, 256)
-        load_piece("wt1", 0, HALF)
-        load_piece("wt0", HALF, HALF)
-
         picked_scales = keep.tile([P, J], U8, name="picked_scales", align_bytes=64)
-        nc.vector.tensor_copy(picked_scales[:], scale_window[:].indirect(offsets[:]))
         second_scales = keep.tile([P, J], U8, name="second_scales", align_bytes=64)
-        nc.vector.memset(second_scales[:].bitcast(I32), 0)
-        nc.sync.dma_start(out=second_scales[0:112, :].bitcast(I32), in_=picked_scales[4:116, :].bitcast(I32))
         table_scales = [picked_scales, second_scales]
 
-        load_piece("wt1", HALF, HALF)
-        load_piece("x", 0, HALF)
-        load_piece("wx", 0, HALF)
-        load_piece("x", HALF, HALF)
-        load_piece("wx", HALF, HALF)
+        def load_words():
+            nc.sync.dma_start(out=word_window[:], in_=tab_words[0].rearrange("p t b -> p (t b)").bitcast(I32))
+
+        def shift_scales():
+            nc.vector.tensor_copy(picked_scales[:], scale_window[:].indirect(offsets[:]))
+            nc.gpsimd.memset(second_scales[:].bitcast(I32), 0)
+            nc.sync.dma_start(out=second_scales[0:112, :].bitcast(I32), in_=picked_scales[4:116, :].bitcast(I32))
+
+        load_piece("wt0", 0, 256)
+        load_piece("wt0", 256, 256)
+        load_words()
+        load_piece("wt1", 0, 512)
+        shift_scales()
+        load_piece("wt0", 512, 512)
+        load_piece("wt1", 512, 512)
+        load_piece("x", 0, 512)
+        load_piece("x", 512, 512)
+        load_piece("wx", 0, 512)
+        load_piece("wx", 512, 512)
         for m in range(N // P):
             load_record(m)
 
@@ -100,24 +104,25 @@ def tile_list_tiert_resL_kernel(tc, tab_words, tab_scales, wt, x, wx, rT, offs, 
 
         quantise("eye", 0, eye[:])
 
-        def cast_and_quantise(name, first):
+        stage = [keep.tile([P, HALF * PACK], BF16, name="stage%d" % i, align_bytes=64) for i in range(5)]
+        banks = [psum.tile([P, HALF], F32, name="bank%d" % i) for i in range(8)]
+
+        def cast_and_quantise(name, first, tile):
             piece = raw[(name, first)]
-            grouped = cast_pool.tile([P, piece.shape[2], PACK], BF16, name="grouped", align_bytes=64)
+            lo = first % HALF * PACK
+            grouped = tile[:, lo : lo + piece.shape[2] * PACK]
             nc.scalar.copy(
-                out=grouped[:].rearrange("p (c i) t -> p c t i", i=RUN_CAST),
+                out=grouped.rearrange("p (c i t) -> p c t i", i=RUN_CAST, t=PACK),
                 in_=piece[:].rearrange("p t (c i) -> p c t i", i=RUN_CAST),
             )
-            quantise(name, first, grouped[:].rearrange("p n t -> p (n t)"))
+            quantise(name, first, grouped)
 
-        rests = {}
-
-        def leftover(a, first):
+        def leftover(a, first, tile, on_gpsimd, turn=0):
             name = "wt%d" % a
-            rest = rest_pool.tile([P, HALF, PACK], BF16, name="rest", align_bytes=64)
-            for b in range(0, HALF, P):
-                col = first + b
+            for b in range(HALF // P):
+                col = first + b * P
                 start = max(s for n, s in raw if n == name and s <= col)
-                bank = deq_psum.tile([P, PACK, P], F32, name="deq")
+                bank = banks[4 + b][:].rearrange("p (t n) -> p t n", t=PACK)
                 for t in range(PACK):
                     sel = slice(t * P, (t + 1) * P)
                     nc.tensor.matmul_mx(
@@ -126,47 +131,42 @@ def tile_list_tiert_resL_kernel(tc, tab_words, tab_scales, wt, x, wx, rT, offs, 
                         rhs=words[name][:, col : col + P].bitcast(FP8X4), rhs_scale=scales[name][:, col : col + P],
                         start=True, stop=True,
                     )
-                nc.vector.tensor_tensor(
-                    out=rest[:, b : b + P, :].rearrange("p (c i) t -> p c t i", i=RUN_REST),
-                    in0=raw[(name, start)][:, :, col - start : col - start + P].rearrange("p t (c i) -> p c t i", i=RUN_REST),
-                    in1=bank[:].rearrange("p t (c i) -> p c t i", i=RUN_REST),
-                    op=ALU.subtract,
-                )
-            rests[(a, first)] = rest
-
-        def quantise_leftover(a, first):
-            quantise("wr%d" % a, first, rests[(a, first)][:].rearrange("p n t -> p (n t)"))
+                weights = raw[(name, start)][:, :, col - start : col - start + P]
+                place = (b * P + turn) % HALF * PACK
+                rest = tile[:, place : place + K_PASS]
+                if b < on_gpsimd:
+                    decoded = decoded_pool.tile([P, P, PACK], F32, name="decoded")
+                    nc.scalar.copy(out=decoded[:], in_=bank.rearrange("p t n -> p n t"))
+                    nc.gpsimd.tensor_tensor(
+                        out=rest.rearrange("p (n t) -> p n t", t=PACK),
+                        in0=weights.rearrange("p t n -> p n t"), in1=decoded[:], op=ALU.subtract,
+                    )
+                else:
+                    nc.vector.tensor_tensor(
+                        out=rest.rearrange("p (c i t) -> p c t i", i=RUN_REST, t=PACK),
+                        in0=weights.rearrange("p t (c i) -> p c t i", i=RUN_REST),
+                        in1=bank.rearrange("p t (c i) -> p c t i", i=RUN_REST),
+                        op=ALU.subtract,
+                    )
+            for part in range(0, HALF, QUARTER):
+                place = (part + turn) % HALF * PACK
+                quantise("wr%d" % a, first + part, tile[:, place : place + QUARTER * PACK])
 
         picked_words = keep.tile([P, J], U32, name="picked_words", align_bytes=64)
         table_words = keep.tile([P, 2 * 2 * J], U8, name="table_words", align_bytes=64)
 
-        cast_and_quantise("wt0", 0)
-        nc.vector.tensor_copy(picked_words[:], word_window[:].bitcast(U32).indirect(offsets[:]))
-        cast_and_quantise("wt0", 256)
-        leftover(0, 0)
-        cast_and_quantise("wt1", 0)
-        nc.vector.tensor_copy(
-            out=table_words[:].bitcast(U16).rearrange("p (d j) -> p d j", d=2),
-            in_=picked_words[:].bitcast(U16).rearrange("p (j d) -> p d j", d=2),
-        )
-        quantise_leftover(0, 0)
-        leftover(1, 0)
-        cast_and_quantise("wt0", HALF)
-        quantise_leftover(1, 0)
-        cast_and_quantise("x", 0)
-        cast_and_quantise("wx", 0)
-        cast_and_quantise("x", HALF)
-        leftover(0, HALF)
-        cast_and_quantise("wt1", HALF)
-        quantise_leftover(0, HALF)
-        leftover(1, HALF)
-        quantise_leftover(1, HALF)
-        cast_and_quantise("wx", HALF)
+        def pick_words():
+            nc.vector.tensor_copy(picked_words[:], word_window[:].bitcast(U32).indirect(offsets[:]))
+            nc.vector.tensor_copy(
+                out=table_words[:].bitcast(U16).rearrange("p (d j) -> p d j", d=2),
+                in_=picked_words[:].bitcast(U16).rearrange("p (j d) -> p d j", d=2),
+            )
 
-        terms = ("wt0", "wt1", "wr0", "wr1", "wx")
+        terms = ("wr1", "wt0", "wt1", "wr0", "wx")
         halves = [slice(0, HALF), slice(HALF, J)]
         tiles = N // P
-        for m in range(tiles):
+
+        def row_tile(m):
             rows = slice(m * P, (m + 1) * P)
             window = raw[("rT", m)]
             picked = picked_pool.tile([P, J], F32, name="picked")
@@ -176,9 +176,9 @@ def tile_list_tiert_resL_kernel(tc, tab_words, tab_scales, wt, x, wx, rT, offs, 
                 for half in halves:
                     nc.vector.tensor_copy(picked[:, half], window[:].indirect(offsets[:, half.start // 16 : half.stop // 16]))
 
-            banks = [acc_psum.tile([P, HALF], F32, name="acc") for half in halves]
+            sums = banks[2 * m % 8 : 2 * m % 8 + 2]
             for s, name in enumerate(terms):
-                for bank, half in zip(banks, halves):
+                for bank, half in zip(sums, halves):
                     if name == "wx":
                         rhs, rhs_scale = words["x"][:, half].bitcast(FP8X4), scales["x"][:, half]
                     else:
@@ -192,12 +192,29 @@ def tile_list_tiert_resL_kernel(tc, tab_words, tab_scales, wt, x, wx, rT, offs, 
 
             result = keep.tile([P, J], F32, name="result%d" % m)
             if m < tiles - 1:
-                for bank, half in zip(banks, halves):
+                for bank, half in zip(sums, halves):
                     nc.scalar.copy(out=result[:, half], in_=bank[:])
                 for part in halves if m == tiles - 2 else [slice(0, J)]:
                     nc.gpsimd.tensor_tensor(out=result[:, part], in0=result[:, part], in1=picked[:, part], op=ALU.add)
                     nc.sync.dma_start(out=out[rows, part], in_=result[:, part])
             else:
-                for bank, half in zip(banks, halves):
+                for bank, half in zip(sums, halves):
                     nc.vector.tensor_tensor(out=result[:, half], in0=bank[:], in1=picked[:, half], op=ALU.add)
                     nc.sync.dma_start(out=out[rows, half], in_=result[:, half])
+
+        cast_and_quantise("wt0", 0, stage[0])
+        cast_and_quantise("wt0", 256, stage[0])
+        leftover(0, 0, stage[0], 0, QUARTER)
+        pick_words()
+        cast_and_quantise("wt1", 0, stage[1])
+        cast_and_quantise("wt0", 512, stage[2])
+        leftover(1, 0, stage[2], 0)
+        cast_and_quantise("wt1", 512, stage[3])
+        leftover(0, 512, stage[3], 0)
+        cast_and_quantise("x", 0, stage[4])
+        leftover(1, 512, stage[4], 0)
+        cast_and_quantise("x", 512, stage[1])
+        cast_and_quantise("wx", 0, stage[0])
+        cast_and_quantise("wx", 512, stage[2])
+        for m in range(tiles):
+            row_tile(m)

@@ -1,7 +1,6 @@
 from contextlib import ExitStack
 
 import concourse.mybir as mybir
-from concourse.masks import make_identity
 
 K, L, N, T, J = 1024, 512, 1024, 2048, 1024
 FLOPS = 2 * (2 * K + L) * N * J + 2 * 512 * K * N
@@ -31,19 +30,36 @@ def tile_list_tiert_resL_kernel(tc, tab_words, tab_scales, wt, x, wx, rT, offs, 
         keep = ctx.enter_context(tc.tile_pool(name="keep", bufs=1))
         loads = ctx.enter_context(tc.tile_pool(name="loads", bufs=15))
         picked_pool = ctx.enter_context(tc.tile_pool(name="picked", bufs=3))
-        decoded_pool = ctx.enter_context(tc.tile_pool(name="decoded", bufs=2))
         psum = ctx.enter_context(tc.psum_pool(name="psum", bufs=1))
 
         offsets = keep.tile([P, J // 16], U16, name="offsets")
         nc.sync.dma_start(offsets[:], offs)
 
         scale_window = keep.tile([P, T], U8, name="scale_window", align_bytes=64)
-        nc.vector.memset(scale_window[:].bitcast(I32), 0)
+        eye = keep.tile([P, PACK * (K_PASS + 1)], BF16, name="eye", align_bytes=64)
+        ones = keep.tile([P, P], F32, name="ones")
+        ramp = keep.tile([P, P], F32, name="ramp", align_bytes=64)
+        turned = keep.tile([P, P], F32, name="turned", align_bytes=64)
+        nc.gpsimd.memset(ones[:], 1.0)
+        nc.gpsimd.memset(eye[:].bitcast(I32), 0)
+        nc.gpsimd.memset(scale_window[:].bitcast(I32), 0)
+        nc.vector.tensor_tensor_scan(out=ramp[:], data0=ones[:], data1=ones[:], initial=0.0, op0=ALU.mult, op1=ALU.add)
+        nc.vector.transpose(out=turned[:], in_=ramp[:])
         for q in range(4):
-            nc.sync.dma_start(
-                out=scale_window[32 * q : 32 * q + 8, :].bitcast(I32),
-                in_=tab_scales[:, 4 * q : 4 * q + 4, :].bitcast(I32),
+            rows = slice(32 * q, 32 * q + 32)
+            nc.vector.tensor_tensor(
+                out=eye[rows, :].rearrange("p (t u) -> p t u", t=PACK)[:, :, P * q : P * (q + 1) : PACK],
+                in0=ramp[rows, :].rearrange("p (t j) -> p t j", t=PACK),
+                in1=turned[rows, :].rearrange("p (t j) -> p t j", t=PACK),
+                op=ALU.is_equal,
             )
+
+        def load_scales():
+            for q in range(4):
+                nc.sync.dma_start(
+                    out=scale_window[32 * q : 32 * q + 8, :].bitcast(I32),
+                    in_=tab_scales[:, 4 * q : 4 * q + 4, :].bitcast(I32),
+                )
 
         sources = {"wt0": wt[0:K_PASS, :], "wt1": wt[K_PASS:K, :], "x": x, "wx": wx}
         raw = {}
@@ -72,113 +88,132 @@ def tile_list_tiert_resL_kernel(tc, tab_words, tab_scales, wt, x, wx, rT, offs, 
             nc.gpsimd.memset(second_scales[:].bitcast(I32), 0)
             nc.sync.dma_start(out=second_scales[0:112, :].bitcast(I32), in_=picked_scales[4:116, :].bitcast(I32))
 
+        load_words()
+        load_scales()
         load_piece("wt0", 0, 256)
         load_piece("wt0", 256, 256)
-        load_words()
         load_piece("wt1", 0, 512)
-        shift_scales()
         load_piece("wt0", 512, 512)
+        shift_scales()
         load_piece("wt1", 512, 512)
         load_piece("x", 0, 512)
         load_piece("x", 512, 512)
         load_piece("wx", 0, 512)
         load_piece("wx", 512, 512)
-        for m in range(N // P):
+        for m in range(0, N // P):
             load_record(m)
-
-        identity = keep.tile([P, P], BF16, name="identity")
-        make_identity(nc, identity[:])
-        eye = keep.tile([P, PACK * K_PASS], BF16, name="eye", align_bytes=64)
-        nc.vector.memset(eye[:].bitcast(I32), 0)
-        for t in range(PACK):
-            nc.scalar.copy(out=eye[:, t * K_PASS + t : (t + 1) * K_PASS : PACK], in_=identity[:])
 
         words, scales = {}, {}
         for name, width in (("eye", PACK * P), ("wt0", N), ("wt1", N), ("wr0", N), ("wr1", N), ("x", J), ("wx", N)):
             words[name] = keep.tile([P, width], U32, name="words_" + name, align_bytes=64)
             scales[name] = keep.tile([P, width], U8, name="scales_" + name, align_bytes=64)
 
+        moved = {}
+
+        def codes(name, first, width):
+            if (name, first // HALF) in moved:
+                return moved[(name, first // HALF)][:, first % HALF : first % HALF + width].bitcast(FP8X4)
+            return words[name][:, first : first + width].bitcast(FP8X4)
+
         def quantise(name, first, grouped):
-            cols = slice(first, first + grouped.shape[1] // PACK)
-            nc.vector.quantize_mx(out=words[name][:, cols].bitcast(FP8X4), scales=scales[name][:, cols], in_=grouped)
+            width = grouped.shape[1] // PACK
+            nc.vector.quantize_mx(out=codes(name, first, width), scales=scales[name][:, first : first + width], in_=grouped)
 
-        quantise("eye", 0, eye[:])
+        quantise("eye", 0, eye[:, 0 : PACK * K_PASS])
 
-        stage = [keep.tile([P, HALF * PACK], BF16, name="stage%d" % i, align_bytes=64) for i in range(5)]
+        stage = [keep.tile([P, HALF * PACK], BF16, name="stage%d" % i, tag="stage%d" % i, align_bytes=64) for i in range(6)]
+        results = [keep.tile([P, J], F32, name="result%d" % m) for m in range(N // P)]
         banks = [psum.tile([P, HALF], F32, name="bank%d" % i) for i in range(8)]
 
-        def cast_and_quantise(name, first, tile):
+        casts = {}
+
+        def cast(name, first, tile, on_vector=False):
             piece = raw[(name, first)]
             lo = first % HALF * PACK
             grouped = tile[:, lo : lo + piece.shape[2] * PACK]
-            nc.scalar.copy(
+            (nc.vector.tensor_copy if on_vector else nc.scalar.copy)(
                 out=grouped.rearrange("p (c i t) -> p c t i", i=RUN_CAST, t=PACK),
                 in_=piece[:].rearrange("p t (c i) -> p c t i", i=RUN_CAST),
             )
-            quantise(name, first, grouped)
+            casts[(name, first)] = grouped
 
-        def leftover(a, first, tile, on_gpsimd, turn=0):
+        def quantise_cast(name, first, tile=None):
+            quantise(name, first, casts[(name, first)] if tile is None else tile[:])
+
+        def decode(a, first):
             name = "wt%d" % a
             for b in range(HALF // P):
                 col = first + b * P
-                start = max(s for n, s in raw if n == name and s <= col)
-                bank = banks[4 + b][:].rearrange("p (t n) -> p t n", t=PACK)
                 for t in range(PACK):
                     sel = slice(t * P, (t + 1) * P)
                     nc.tensor.matmul_mx(
-                        out=bank[:, t, :],
+                        out=banks[4 + b][:, sel],
                         lhsT=words["eye"][:, sel].bitcast(FP8X4), lhsT_scale=scales["eye"][:, sel],
                         rhs=words[name][:, col : col + P].bitcast(FP8X4), rhs_scale=scales[name][:, col : col + P],
                         start=True, stop=True,
                     )
-                weights = raw[(name, start)][:, :, col - start : col - start + P]
-                place = (b * P + turn) % HALF * PACK
-                rest = tile[:, place : place + K_PASS]
-                if b < on_gpsimd:
-                    decoded = decoded_pool.tile([P, P, PACK], F32, name="decoded")
-                    nc.scalar.copy(out=decoded[:], in_=bank.rearrange("p t n -> p n t"))
-                    nc.gpsimd.tensor_tensor(
-                        out=rest.rearrange("p (n t) -> p n t", t=PACK),
-                        in0=weights.rearrange("p t n -> p n t"), in1=decoded[:], op=ALU.subtract,
-                    )
-                else:
-                    nc.vector.tensor_tensor(
-                        out=rest.rearrange("p (c i t) -> p c t i", i=RUN_REST, t=PACK),
-                        in0=weights.rearrange("p t (c i) -> p c t i", i=RUN_REST),
-                        in1=bank.rearrange("p t (c i) -> p c t i", i=RUN_REST),
-                        op=ALU.subtract,
-                    )
+
+        def subtract(a, first, b, tile, turn=0, spare=None):
+            name = "wt%d" % a
+            col = first + b * P
+            start = max(s for n, s in raw if n == name and s <= col)
+            bank = banks[4 + b][:].rearrange("p (t n) -> p t n", t=PACK)
+            weights = raw[(name, start)][:, :, col - start : col - start + P]
+            place = (b * P + turn) % HALF * PACK
+            rest = tile[:, place : place + K_PASS]
+            if spare is None:
+                nc.vector.tensor_tensor(
+                    out=rest.rearrange("p (c i t) -> p c t i", i=RUN_REST, t=PACK),
+                    in0=weights.rearrange("p t (c i) -> p c t i", i=RUN_REST),
+                    in1=bank.rearrange("p t (c i) -> p c t i", i=RUN_REST),
+                    op=ALU.subtract,
+                )
+            else:
+                decoded = spare.rearrange("p (n t) -> p n t", t=PACK)
+                nc.scalar.copy(out=decoded, in_=bank.rearrange("p t n -> p n t"))
+                nc.gpsimd.tensor_tensor(
+                    out=rest.rearrange("p (n t) -> p n t", t=PACK),
+                    in0=weights.rearrange("p t n -> p n t"), in1=decoded, op=ALU.subtract,
+                )
+
+        def quantise_halves(name, first):
             for part in range(0, HALF, QUARTER):
+                quantise(name, first + part, casts[(name, first)][:, part * PACK : (part + QUARTER) * PACK])
+
+        def quantise_rest(a, first, tile, turn=0, width=QUARTER):
+            for part in range(0, HALF, width):
                 place = (part + turn) % HALF * PACK
-                quantise("wr%d" % a, first + part, tile[:, place : place + QUARTER * PACK])
+                quantise("wr%d" % a, first + part, tile[:, place : place + width * PACK])
 
         picked_words = keep.tile([P, J], U32, name="picked_words", align_bytes=64)
-        table_words = keep.tile([P, 2 * 2 * J], U8, name="table_words", align_bytes=64)
+        table_words = keep.tile([P, 2 * 2 * J], U8, name="table_words", tag="stage0", align_bytes=64)
 
         def pick_words():
             nc.vector.tensor_copy(picked_words[:], word_window[:].bitcast(U32).indirect(offsets[:]))
+
+        def part_words():
             nc.vector.tensor_copy(
                 out=table_words[:].bitcast(U16).rearrange("p (d j) -> p d j", d=2),
                 in_=picked_words[:].bitcast(U16).rearrange("p (j d) -> p d j", d=2),
             )
 
-        terms = ("wr1", "wt0", "wt1", "wr0", "wx")
         halves = [slice(0, HALF), slice(HALF, J)]
-        tiles = N // P
+        picked = {}
 
-        def row_tile(m):
+        def gather(m, parts=1):
+            picked[m] = picked_pool.tile([P, J], F32, name="picked")
+            for lo in range(0, J, J // parts):
+                hi = lo + J // parts
+                nc.vector.tensor_copy(picked[m][:, lo:hi], raw[("rT", m)][:].indirect(offsets[:, lo // 16 : hi // 16]))
+
+        begun = {}
+
+        def products(m, pair, names):
             rows = slice(m * P, (m + 1) * P)
-            window = raw[("rT", m)]
-            picked = picked_pool.tile([P, J], F32, name="picked")
-            if m < tiles - 1:
-                nc.vector.tensor_copy(picked[:], window[:].indirect(offsets[:]))
-            else:
-                for half in halves:
-                    nc.vector.tensor_copy(picked[:, half], window[:].indirect(offsets[:, half.start // 16 : half.stop // 16]))
-
-            sums = banks[2 * m % 8 : 2 * m % 8 + 2]
-            for s, name in enumerate(terms):
-                for bank, half in zip(sums, halves):
+            for name in names:
+                count = begun.get(m, 0)
+                begun[m] = count + 1
+                for h, half in enumerate(halves):
                     if name == "wx":
                         rhs, rhs_scale = words["x"][:, half].bitcast(FP8X4), scales["x"][:, half]
                     else:
@@ -186,35 +221,121 @@ def tile_list_tiert_resL_kernel(tc, tab_words, tab_scales, wt, x, wx, rT, offs, 
                         rhs = table_words[:, 2 * (a * J + half.start) : 2 * (a * J + half.stop)].bitcast(FP4X4)
                         rhs_scale = table_scales[a][:, half]
                     nc.tensor.matmul_mx(
-                        out=bank[:], lhsT=words[name][:, rows].bitcast(FP8X4), lhsT_scale=scales[name][:, rows],
-                        rhs=rhs, rhs_scale=rhs_scale, start=(s == 0), stop=(s == len(terms) - 1),
+                        out=banks[2 * pair + h][:], lhsT=codes(name, m * P, P), lhsT_scale=scales[name][:, rows],
+                        rhs=rhs, rhs_scale=rhs_scale, start=(count == 0), stop=(count == 4),
                     )
 
-            result = keep.tile([P, J], F32, name="result%d" % m)
-            if m < tiles - 1:
-                for bank, half in zip(sums, halves):
-                    nc.scalar.copy(out=result[:, half], in_=bank[:])
-                for part in halves if m == tiles - 2 else [slice(0, J)]:
-                    nc.gpsimd.tensor_tensor(out=result[:, part], in0=result[:, part], in1=picked[:, part], op=ALU.add)
-                    nc.sync.dma_start(out=out[rows, part], in_=result[:, part])
-            else:
-                for bank, half in zip(sums, halves):
-                    nc.vector.tensor_tensor(out=result[:, half], in0=bank[:], in1=picked[:, half], op=ALU.add)
-                    nc.sync.dma_start(out=out[rows, half], in_=result[:, half])
+        def empty(m, pair, which=(0, 1)):
+            for h in which:
+                nc.scalar.copy(out=results[m][:, halves[h]], in_=banks[2 * pair + h][:])
 
-        cast_and_quantise("wt0", 0, stage[0])
-        cast_and_quantise("wt0", 256, stage[0])
-        leftover(0, 0, stage[0], 0, QUARTER)
+        def add(m, part):
+            nc.gpsimd.tensor_tensor(out=results[m][:, part], in0=results[m][:, part], in1=picked[m][:, part], op=ALU.add)
+
+        def add_from_bank(m, pair, h):
+            nc.vector.tensor_tensor(out=results[m][:, halves[h]], in0=banks[2 * pair + h][:], in1=picked[m][:, halves[h]], op=ALU.add)
+
+        def store(m, part):
+            nc.sync.dma_start(out=out[m * P : (m + 1) * P, part], in_=results[m][:, part])
+
+        whole = slice(0, J)
         pick_words()
-        cast_and_quantise("wt1", 0, stage[1])
-        cast_and_quantise("wt0", 512, stage[2])
-        leftover(1, 0, stage[2], 0)
-        cast_and_quantise("wt1", 512, stage[3])
-        leftover(0, 512, stage[3], 0)
-        cast_and_quantise("x", 0, stage[4])
-        leftover(1, 512, stage[4], 0)
-        cast_and_quantise("x", 512, stage[1])
-        cast_and_quantise("wx", 0, stage[0])
-        cast_and_quantise("wx", 512, stage[2])
-        for m in range(tiles):
-            row_tile(m)
+        cast("wt0", 0, stage[0])
+        cast("wt0", 256, stage[0])
+        quantise_cast("wt0", 0, stage[0])
+        part_words()
+        decode(0,0)
+        subtract(0,0, 0, stage[5], 0)
+        subtract(0,0, 1, stage[5], 0)
+        subtract(0,0, 2, stage[5], 0)
+        subtract(0,0, 3, stage[5], 0)
+        cast("wt1", 0, stage[1])
+        quantise_cast("wt1", 0)
+        quantise_rest(0,0, stage[5], 0)
+        cast("wt0", 512, stage[2])
+        quantise_halves("wt0", 512)
+        decode(1,0)
+        subtract(1,0, 0, stage[2], 0)
+        subtract(1,0, 1, stage[2], 0)
+        subtract(1,0, 2, stage[2], 0)
+        subtract(1,0, 3, stage[2], 0)
+        quantise_rest(1,0, stage[2], 0)
+        cast("wt1", 512, stage[3])
+        quantise_halves("wt1", 512)
+        decode(0,512)
+        subtract(0,512, 0, stage[3], 0)
+        subtract(0,512, 1, stage[3], 0)
+        subtract(0,512, 2, stage[3], 0)
+        subtract(0,512, 3, stage[3], 0)
+        quantise_rest(0,512, stage[3], 0)
+        cast("x", 0, stage[4])
+        quantise_halves("x", 0)
+        decode(1,512)
+        subtract(1,512, 0, stage[4], 0)
+        subtract(1,512, 1, stage[4], 0)
+        subtract(1,512, 2, stage[4], 0)
+        subtract(1,512, 3, stage[4], 0)
+        quantise_rest(1,512, stage[4], 0)
+        cast("x", 512, stage[1])
+        quantise_cast("x", 512)
+        cast("wx", 0, stage[5])
+        quantise_cast("wx", 0)
+        cast("wx", 512, stage[2])
+        quantise_cast("wx", 512)
+        gather(0, 1)
+        products(0, 0, ("wr1", "wt0", "wt1", "wr0", "wx", ))
+        empty(0, 0)
+        add(0, whole)
+        store(0, whole)
+        gather(1, 1)
+        products(1, 1, ("wr1", "wt0", "wt1", "wr0", "wx", ))
+        empty(1, 1)
+        add(1, whole)
+        store(1, whole)
+        gather(2, 1)
+        products(2, 2, ("wr1", "wt0", "wt1", "wr0", "wx", ))
+        empty(2, 2)
+        add(2, whole)
+        store(2, whole)
+        gather(3, 1)
+        products(3, 3, ("wr1", "wt0", "wt1", "wr0", "wx", ))
+        empty(3, 3)
+        add(3, whole)
+        store(3, whole)
+        gather(4, 1)
+        products(4, 0, ("wr1", "wt0", "wt1", "wr0", "wx", ))
+        empty(4, 0)
+        add(4, whole)
+        store(4, whole)
+        gather(5, 1)
+        products(5, 1, ("wr1", "wt0", "wt1", "wr0", "wx", ))
+        empty(5, 1)
+        add(5, whole)
+        store(5, whole)
+        gather(6, 2)
+        products(6, 2, ("wr1", "wt0", "wt1", "wr0", "wx", ))
+        empty(6, 2, (0,))
+        empty(6, 2, (1,))
+        add(6, halves[0])
+        store(6, halves[0])
+        add(6, halves[1])
+        store(6, halves[1])
+        last = N // P - 1
+        picked[last] = picked_pool.tile([P, J], F32, name="picked")
+        products(last, 3, ("wr1", "wt0", "wt1", "wr0", "wx"))
+        parts = [slice(0, HALF), slice(HALF, HALF + QUARTER), slice(HALF + QUARTER, J)]
+
+        def gather_last(part):
+            nc.vector.tensor_copy(picked[last][:, part], raw[("rT", last)][:].indirect(offsets[:, part.start // 16 : part.stop // 16]))
+
+        def add_last(part):
+            bank = banks[6 + part.start // HALF][:, part.start % HALF : (part.stop - 1) % HALF + 1]
+            nc.vector.tensor_tensor(out=results[last][:, part], in0=bank, in1=picked[last][:, part], op=ALU.add)
+            store(last, part)
+
+        gather_last(parts[0])
+        gather_last(parts[1])
+        add_last(parts[0])
+        gather_last(parts[2])
+        add_last(parts[1])
+        add_last(parts[2])

@@ -18,21 +18,28 @@ ALU = mybir.AluOpType
 P = 128
 PACK = 4
 K_PASS = P * PACK
+QUAD = 32
+LIST_ROWS = 16
 HALF = 512
-QUARTER = 256
-RUN_CAST = 2
-RUN_REST = 2
+QUARTER = HALF // 2
+RUN = 2
+ROW_TILES = N // P
+LOAD_SLOTS = 15
+PICKED_SLOTS = 3
+STAGE_TILES = 6
+DECODE_BANK = 4
+TERMS = ("wr1", "wt0", "wt1", "wr0", "wx")
 
 
 def tile_list_tiert_resL_kernel(tc, tab_words, tab_scales, wt, x, wx, rT, offs, out):
     nc = tc.nc
     with ExitStack() as ctx:
         keep = ctx.enter_context(tc.tile_pool(name="keep", bufs=1))
-        loads = ctx.enter_context(tc.tile_pool(name="loads", bufs=15))
-        picked_pool = ctx.enter_context(tc.tile_pool(name="picked", bufs=3))
+        loads = ctx.enter_context(tc.tile_pool(name="loads", bufs=LOAD_SLOTS))
+        picked_pool = ctx.enter_context(tc.tile_pool(name="picked", bufs=PICKED_SLOTS))
         psum = ctx.enter_context(tc.psum_pool(name="psum", bufs=1))
 
-        offsets = keep.tile([P, J // 16], U16, name="offsets")
+        offsets = keep.tile([P, J // LIST_ROWS], U16, name="offsets")
         nc.sync.dma_start(offsets[:], offs)
 
         scale_window = keep.tile([P, T], U8, name="scale_window", align_bytes=64)
@@ -45,62 +52,55 @@ def tile_list_tiert_resL_kernel(tc, tab_words, tab_scales, wt, x, wx, rT, offs, 
         nc.gpsimd.memset(scale_window[:].bitcast(I32), 0)
         nc.vector.tensor_tensor_scan(out=ramp[:], data0=ones[:], data1=ones[:], initial=0.0, op0=ALU.mult, op1=ALU.add)
         nc.vector.transpose(out=turned[:], in_=ramp[:])
-        for q in range(4):
-            rows = slice(32 * q, 32 * q + 32)
+        for q in range(P // QUAD):
+            quadrant = slice(QUAD * q, QUAD * (q + 1))
             nc.vector.tensor_tensor(
-                out=eye[rows, :].rearrange("p (t u) -> p t u", t=PACK)[:, :, P * q : P * (q + 1) : PACK],
-                in0=ramp[rows, :].rearrange("p (t j) -> p t j", t=PACK),
-                in1=turned[rows, :].rearrange("p (t j) -> p t j", t=PACK),
+                out=eye[quadrant, :].rearrange("p (t u) -> p t u", t=PACK)[:, :, P * q : P * (q + 1) : PACK],
+                in0=ramp[quadrant, :].rearrange("p (t j) -> p t j", t=PACK),
+                in1=turned[quadrant, :].rearrange("p (t j) -> p t j", t=PACK),
                 op=ALU.is_equal,
             )
 
-        def load_scales():
-            for q in range(4):
-                nc.sync.dma_start(
-                    out=scale_window[32 * q : 32 * q + 8, :].bitcast(I32),
-                    in_=tab_scales[:, 4 * q : 4 * q + 4, :].bitcast(I32),
-                )
-
         sources = {"wt0": wt[0:K_PASS, :], "wt1": wt[K_PASS:K, :], "x": x, "wx": wx}
-        raw = {}
+        pieces, records = {}, {}
 
-        def load_piece(name, first, width):
+        def load_piece(name, first, width=HALF):
             piece = loads.tile([P, PACK, width], F32, name="piece", tag="load")
             rows = sources[name].rearrange("(p t) n -> p t n", t=PACK)
             nc.sync.dma_start(out=piece[:], in_=rows[:, :, first : first + width])
-            raw[(name, first)] = piece
+            pieces[(name, first)] = piece
 
         def load_record(m):
-            window = loads.tile([P, T], F32, name="record", tag="load")
-            nc.sync.dma_start(out=window[:], in_=rT[m * P : (m + 1) * P, :])
-            raw[("rT", m)] = window
+            records[m] = loads.tile([P, T], F32, name="record", tag="load")
+            nc.sync.dma_start(out=records[m][:], in_=rT[m * P : (m + 1) * P, :])
 
         word_window = loads.tile([P, T], I32, name="word_window", tag="load")
         picked_scales = keep.tile([P, J], U8, name="picked_scales", align_bytes=64)
         second_scales = keep.tile([P, J], U8, name="second_scales", align_bytes=64)
         table_scales = [picked_scales, second_scales]
 
-        def load_words():
-            nc.sync.dma_start(out=word_window[:], in_=tab_words[0].rearrange("p t b -> p (t b)").bitcast(I32))
+        nc.sync.dma_start(out=word_window[:], in_=tab_words[0].rearrange("p t b -> p (t b)").bitcast(I32))
+        for q in range(P // QUAD):
+            nc.sync.dma_start(
+                out=scale_window[QUAD * q : QUAD * q + 8, :].bitcast(I32),
+                in_=tab_scales[:, 4 * q : 4 * q + 4, :].bitcast(I32),
+            )
+        load_piece("wt0", 0, QUARTER)
+        load_piece("wt0", QUARTER, QUARTER)
+        load_piece("wt1", 0)
+        load_piece("wt0", HALF)
 
-        def shift_scales():
-            nc.vector.tensor_copy(picked_scales[:], scale_window[:].indirect(offsets[:]))
-            nc.gpsimd.memset(second_scales[:].bitcast(I32), 0)
-            nc.sync.dma_start(out=second_scales[0:112, :].bitcast(I32), in_=picked_scales[4:116, :].bitcast(I32))
+        nc.vector.tensor_copy(picked_scales[:], scale_window[:].indirect(offsets[:]))
+        nc.gpsimd.memset(second_scales[:].bitcast(I32), 0)
+        nc.sync.dma_start(out=second_scales[0:112, :].bitcast(I32), in_=picked_scales[4:116, :].bitcast(I32))
 
-        load_words()
-        load_scales()
-        load_piece("wt0", 0, 256)
-        load_piece("wt0", 256, 256)
-        load_piece("wt1", 0, 512)
-        load_piece("wt0", 512, 512)
-        shift_scales()
-        load_piece("wt1", 512, 512)
-        load_piece("x", 0, 512)
-        load_piece("x", 512, 512)
-        load_piece("wx", 0, 512)
-        load_piece("wx", 512, 512)
-        for m in range(0, N // P):
+        load_piece("wt1", HALF)
+        load_piece("x", 0)
+        load_piece("x", HALF)
+        load_piece("wx", 0)
+        load_record(0)
+        load_piece("wx", HALF)
+        for m in range(1, ROW_TILES):
             load_record(m)
 
         words, scales = {}, {}
@@ -108,112 +108,73 @@ def tile_list_tiert_resL_kernel(tc, tab_words, tab_scales, wt, x, wx, rT, offs, 
             words[name] = keep.tile([P, width], U32, name="words_" + name, align_bytes=64)
             scales[name] = keep.tile([P, width], U8, name="scales_" + name, align_bytes=64)
 
-        moved = {}
-
-        def codes(name, first, width):
-            if (name, first // HALF) in moved:
-                return moved[(name, first // HALF)][:, first % HALF : first % HALF + width].bitcast(FP8X4)
-            return words[name][:, first : first + width].bitcast(FP8X4)
-
-        def quantise(name, first, grouped):
-            width = grouped.shape[1] // PACK
-            nc.vector.quantize_mx(out=codes(name, first, width), scales=scales[name][:, first : first + width], in_=grouped)
+        def quantise(name, first, interleaved, parts=1):
+            width = interleaved.shape[1] // PACK // parts
+            for part in range(parts):
+                cols = slice(first + part * width, first + (part + 1) * width)
+                nc.vector.quantize_mx(
+                    out=words[name][:, cols].bitcast(FP8X4), scales=scales[name][:, cols],
+                    in_=interleaved[:, part * width * PACK : (part + 1) * width * PACK],
+                )
 
         quantise("eye", 0, eye[:, 0 : PACK * K_PASS])
 
-        stage = [keep.tile([P, HALF * PACK], BF16, name="stage%d" % i, tag="stage%d" % i, align_bytes=64) for i in range(6)]
-        results = [keep.tile([P, J], F32, name="result%d" % m) for m in range(N // P)]
+        stage = [
+            keep.tile([P, HALF * PACK], BF16, name="stage%d" % i, tag="stage%d" % i, align_bytes=64)
+            for i in range(STAGE_TILES)
+        ]
+        results = [keep.tile([P, J], F32, name="result%d" % m) for m in range(ROW_TILES)]
         banks = [psum.tile([P, HALF], F32, name="bank%d" % i) for i in range(8)]
 
-        casts = {}
-
-        def cast(name, first, tile, on_vector=False):
-            piece = raw[(name, first)]
+        def cast(name, first, tile):
+            piece = pieces[(name, first)]
             lo = first % HALF * PACK
-            grouped = tile[:, lo : lo + piece.shape[2] * PACK]
-            (nc.vector.tensor_copy if on_vector else nc.scalar.copy)(
-                out=grouped.rearrange("p (c i t) -> p c t i", i=RUN_CAST, t=PACK),
-                in_=piece[:].rearrange("p t (c i) -> p c t i", i=RUN_CAST),
+            nc.scalar.copy(
+                out=tile[:, lo : lo + piece.shape[2] * PACK].rearrange("p (c i t) -> p c t i", i=RUN, t=PACK),
+                in_=piece[:].rearrange("p t (c i) -> p c t i", i=RUN),
             )
-            casts[(name, first)] = grouped
 
-        def quantise_cast(name, first, tile=None):
-            quantise(name, first, casts[(name, first)] if tile is None else tile[:])
-
-        def decode(a, first):
+        def leftover(a, first, tile):
             name = "wt%d" % a
             for b in range(HALF // P):
-                col = first + b * P
+                cols = slice(first + b * P, first + (b + 1) * P)
                 for t in range(PACK):
                     sel = slice(t * P, (t + 1) * P)
                     nc.tensor.matmul_mx(
-                        out=banks[4 + b][:, sel],
+                        out=banks[DECODE_BANK + b][:, sel],
                         lhsT=words["eye"][:, sel].bitcast(FP8X4), lhsT_scale=scales["eye"][:, sel],
-                        rhs=words[name][:, col : col + P].bitcast(FP8X4), rhs_scale=scales[name][:, col : col + P],
+                        rhs=words[name][:, cols].bitcast(FP8X4), rhs_scale=scales[name][:, cols],
                         start=True, stop=True,
                     )
-
-        def subtract(a, first, b, tile, turn=0, spare=None):
-            name = "wt%d" % a
-            col = first + b * P
-            start = max(s for n, s in raw if n == name and s <= col)
-            bank = banks[4 + b][:].rearrange("p (t n) -> p t n", t=PACK)
-            weights = raw[(name, start)][:, :, col - start : col - start + P]
-            place = (b * P + turn) % HALF * PACK
-            rest = tile[:, place : place + K_PASS]
-            if spare is None:
+            for b in range(HALF // P):
+                col = first + b * P
+                start = max(s for n, s in pieces if n == name and s <= col)
+                weights = pieces[(name, start)][:, :, col - start : col - start + P]
                 nc.vector.tensor_tensor(
-                    out=rest.rearrange("p (c i t) -> p c t i", i=RUN_REST, t=PACK),
-                    in0=weights.rearrange("p t (c i) -> p c t i", i=RUN_REST),
-                    in1=bank.rearrange("p t (c i) -> p c t i", i=RUN_REST),
+                    out=tile[:, b * K_PASS : (b + 1) * K_PASS].rearrange("p (c i t) -> p c t i", i=RUN, t=PACK),
+                    in0=weights.rearrange("p t (c i) -> p c t i", i=RUN),
+                    in1=banks[DECODE_BANK + b][:].rearrange("p (t c i) -> p c t i", t=PACK, i=RUN),
                     op=ALU.subtract,
                 )
-            else:
-                decoded = spare.rearrange("p (n t) -> p n t", t=PACK)
-                nc.scalar.copy(out=decoded, in_=bank.rearrange("p t n -> p n t"))
-                nc.gpsimd.tensor_tensor(
-                    out=rest.rearrange("p (n t) -> p n t", t=PACK),
-                    in0=weights.rearrange("p t n -> p n t"), in1=decoded, op=ALU.subtract,
-                )
-
-        def quantise_halves(name, first):
-            for part in range(0, HALF, QUARTER):
-                quantise(name, first + part, casts[(name, first)][:, part * PACK : (part + QUARTER) * PACK])
-
-        def quantise_rest(a, first, tile, turn=0, width=QUARTER):
-            for part in range(0, HALF, width):
-                place = (part + turn) % HALF * PACK
-                quantise("wr%d" % a, first + part, tile[:, place : place + width * PACK])
 
         picked_words = keep.tile([P, J], U32, name="picked_words", align_bytes=64)
         table_words = keep.tile([P, 2 * 2 * J], U8, name="table_words", tag="stage0", align_bytes=64)
-
-        def pick_words():
-            nc.vector.tensor_copy(picked_words[:], word_window[:].bitcast(U32).indirect(offsets[:]))
-
-        def part_words():
-            nc.vector.tensor_copy(
-                out=table_words[:].bitcast(U16).rearrange("p (d j) -> p d j", d=2),
-                in_=picked_words[:].bitcast(U16).rearrange("p (j d) -> p d j", d=2),
-            )
-
         halves = [slice(0, HALF), slice(HALF, J)]
         picked = {}
 
-        def gather(m, parts=1):
-            picked[m] = picked_pool.tile([P, J], F32, name="picked")
-            for lo in range(0, J, J // parts):
-                hi = lo + J // parts
-                nc.vector.tensor_copy(picked[m][:, lo:hi], raw[("rT", m)][:].indirect(offsets[:, lo // 16 : hi // 16]))
+        def gather(m, part):
+            if part.start == 0:
+                picked[m] = picked_pool.tile([P, J], F32, name="picked")
+            listed = offsets[:, part.start // LIST_ROWS : part.stop // LIST_ROWS]
+            nc.vector.tensor_copy(picked[m][:, part], records[m][:].indirect(listed))
 
-        begun = {}
+        def sum_bank(m, column):
+            return banks[2 * m % len(banks) + column // HALF]
 
-        def products(m, pair, names):
+        def products(m):
             rows = slice(m * P, (m + 1) * P)
-            for name in names:
-                count = begun.get(m, 0)
-                begun[m] = count + 1
-                for h, half in enumerate(halves):
+            for s, name in enumerate(TERMS):
+                for half in halves:
                     if name == "wx":
                         rhs, rhs_scale = words["x"][:, half].bitcast(FP8X4), scales["x"][:, half]
                     else:
@@ -221,121 +182,68 @@ def tile_list_tiert_resL_kernel(tc, tab_words, tab_scales, wt, x, wx, rT, offs, 
                         rhs = table_words[:, 2 * (a * J + half.start) : 2 * (a * J + half.stop)].bitcast(FP4X4)
                         rhs_scale = table_scales[a][:, half]
                     nc.tensor.matmul_mx(
-                        out=banks[2 * pair + h][:], lhsT=codes(name, m * P, P), lhsT_scale=scales[name][:, rows],
-                        rhs=rhs, rhs_scale=rhs_scale, start=(count == 0), stop=(count == 4),
+                        out=sum_bank(m, half.start)[:],
+                        lhsT=words[name][:, rows].bitcast(FP8X4), lhsT_scale=scales[name][:, rows],
+                        rhs=rhs, rhs_scale=rhs_scale, start=(s == 0), stop=(s == len(TERMS) - 1),
                     )
-
-        def empty(m, pair, which=(0, 1)):
-            for h in which:
-                nc.scalar.copy(out=results[m][:, halves[h]], in_=banks[2 * pair + h][:])
-
-        def add(m, part):
-            nc.gpsimd.tensor_tensor(out=results[m][:, part], in0=results[m][:, part], in1=picked[m][:, part], op=ALU.add)
-
-        def add_from_bank(m, pair, h):
-            nc.vector.tensor_tensor(out=results[m][:, halves[h]], in0=banks[2 * pair + h][:], in1=picked[m][:, halves[h]], op=ALU.add)
 
         def store(m, part):
             nc.sync.dma_start(out=out[m * P : (m + 1) * P, part], in_=results[m][:, part])
 
-        whole = slice(0, J)
-        pick_words()
+        nc.vector.tensor_copy(picked_words[:], word_window[:].bitcast(U32).indirect(offsets[:]))
         cast("wt0", 0, stage[0])
-        cast("wt0", 256, stage[0])
-        quantise_cast("wt0", 0, stage[0])
-        part_words()
-        decode(0,0)
-        subtract(0,0, 0, stage[5], 0)
-        subtract(0,0, 1, stage[5], 0)
-        subtract(0,0, 2, stage[5], 0)
-        subtract(0,0, 3, stage[5], 0)
+        cast("wt0", QUARTER, stage[0])
+        quantise("wt0", 0, stage[0][:])
+        nc.vector.tensor_copy(
+            out=table_words[:].bitcast(U16).rearrange("p (d j) -> p d j", d=2),
+            in_=picked_words[:].bitcast(U16).rearrange("p (j d) -> p d j", d=2),
+        )
+        leftover(0, 0, stage[5])
         cast("wt1", 0, stage[1])
-        quantise_cast("wt1", 0)
-        quantise_rest(0,0, stage[5], 0)
-        cast("wt0", 512, stage[2])
-        quantise_halves("wt0", 512)
-        decode(1,0)
-        subtract(1,0, 0, stage[2], 0)
-        subtract(1,0, 1, stage[2], 0)
-        subtract(1,0, 2, stage[2], 0)
-        subtract(1,0, 3, stage[2], 0)
-        quantise_rest(1,0, stage[2], 0)
-        cast("wt1", 512, stage[3])
-        quantise_halves("wt1", 512)
-        decode(0,512)
-        subtract(0,512, 0, stage[3], 0)
-        subtract(0,512, 1, stage[3], 0)
-        subtract(0,512, 2, stage[3], 0)
-        subtract(0,512, 3, stage[3], 0)
-        quantise_rest(0,512, stage[3], 0)
-        cast("x", 0, stage[4])
-        quantise_halves("x", 0)
-        decode(1,512)
-        subtract(1,512, 0, stage[4], 0)
-        subtract(1,512, 1, stage[4], 0)
-        subtract(1,512, 2, stage[4], 0)
-        subtract(1,512, 3, stage[4], 0)
-        quantise_rest(1,512, stage[4], 0)
-        cast("x", 512, stage[1])
-        quantise_cast("x", 512)
+        quantise("wt1", 0, stage[1][:])
+        quantise("wr0", 0, stage[5][:], parts=2)
+
+        following = [("wt1", 0), ("wt0", HALF), ("wt1", HALF), ("x", 0)]
+        for i in range(1, len(following)):
+            name, first = following[i]
+            tile = stage[i + 1]
+            cast(name, first, tile)
+            quantise(name, first, tile[:], parts=2)
+            before, before_first = following[i - 1]
+            leftover(int(before[2]), before_first, tile)
+            quantise("wr" + before[2], before_first, tile[:], parts=2)
+
+        whole = slice(0, J)
+        cast("x", HALF, stage[1])
+        quantise("x", HALF, stage[1][:])
         cast("wx", 0, stage[5])
-        quantise_cast("wx", 0)
-        cast("wx", 512, stage[2])
-        quantise_cast("wx", 512)
-        gather(0, 1)
-        products(0, 0, ("wr1", "wt0", "wt1", "wr0", "wx", ))
-        empty(0, 0)
-        add(0, whole)
-        store(0, whole)
-        gather(1, 1)
-        products(1, 1, ("wr1", "wt0", "wt1", "wr0", "wx", ))
-        empty(1, 1)
-        add(1, whole)
-        store(1, whole)
-        gather(2, 1)
-        products(2, 2, ("wr1", "wt0", "wt1", "wr0", "wx", ))
-        empty(2, 2)
-        add(2, whole)
-        store(2, whole)
-        gather(3, 1)
-        products(3, 3, ("wr1", "wt0", "wt1", "wr0", "wx", ))
-        empty(3, 3)
-        add(3, whole)
-        store(3, whole)
-        gather(4, 1)
-        products(4, 0, ("wr1", "wt0", "wt1", "wr0", "wx", ))
-        empty(4, 0)
-        add(4, whole)
-        store(4, whole)
-        gather(5, 1)
-        products(5, 1, ("wr1", "wt0", "wt1", "wr0", "wx", ))
-        empty(5, 1)
-        add(5, whole)
-        store(5, whole)
-        gather(6, 2)
-        products(6, 2, ("wr1", "wt0", "wt1", "wr0", "wx", ))
-        empty(6, 2, (0,))
-        empty(6, 2, (1,))
-        add(6, halves[0])
-        store(6, halves[0])
-        add(6, halves[1])
-        store(6, halves[1])
-        last = N // P - 1
-        picked[last] = picked_pool.tile([P, J], F32, name="picked")
-        products(last, 3, ("wr1", "wt0", "wt1", "wr0", "wx"))
+        quantise("wx", 0, stage[5][:])
+        gather(0, whole)
+        cast("wx", HALF, stage[2])
+        quantise("wx", HALF, stage[2][:])
+
+        last = ROW_TILES - 1
+        for m in range(last):
+            parts = halves if m == last - 1 else [whole]
+            if m > 0:
+                for part in parts:
+                    gather(m, part)
+            products(m)
+            for half in halves:
+                nc.scalar.copy(out=results[m][:, half], in_=sum_bank(m, half.start)[:])
+            for part in parts:
+                nc.gpsimd.tensor_tensor(out=results[m][:, part], in0=results[m][:, part], in1=picked[m][:, part], op=ALU.add)
+                store(m, part)
+
+        products(last)
         parts = [slice(0, HALF), slice(HALF, HALF + QUARTER), slice(HALF + QUARTER, J)]
-
-        def gather_last(part):
-            nc.vector.tensor_copy(picked[last][:, part], raw[("rT", last)][:].indirect(offsets[:, part.start // 16 : part.stop // 16]))
-
-        def add_last(part):
-            bank = banks[6 + part.start // HALF][:, part.start % HALF : (part.stop - 1) % HALF + 1]
-            nc.vector.tensor_tensor(out=results[last][:, part], in0=bank, in1=picked[last][:, part], op=ALU.add)
+        gather(last, parts[0])
+        for i, part in enumerate(parts):
+            if i + 1 < len(parts):
+                gather(last, parts[i + 1])
+            lo = part.start % HALF
+            nc.vector.tensor_tensor(
+                out=results[last][:, part], in0=sum_bank(last, part.start)[:, lo : lo + part.stop - part.start],
+                in1=picked[last][:, part], op=ALU.add,
+            )
             store(last, part)
-
-        gather_last(parts[0])
-        gather_last(parts[1])
-        add_last(parts[0])
-        gather_last(parts[2])
-        add_last(parts[1])
-        add_last(parts[2])

@@ -27,6 +27,7 @@ ROW_TILES = N // P
 LOAD_SLOTS = 15
 PICKED_SLOTS = 3
 STAGE_TILES = 6
+SECOND_ROWS = 16
 DECODE_BANK = 4
 TERMS = ("wr1", "wt0", "wt1", "wr0", "wx")
 
@@ -42,23 +43,22 @@ def tile_list_tiert_resL_kernel(tc, tab_words, tab_scales, wt, x, wx, rT, offs, 
         offsets = keep.tile([P, J // LIST_ROWS], U16, name="offsets")
         nc.sync.dma_start(offsets[:], offs)
 
-        scale_window = keep.tile([P, T], U8, name="scale_window", align_bytes=64)
+        scale_window = keep.tile([P, T + 4], U8, name="scale_window", align_bytes=64)
         eye = keep.tile([P, PACK * (K_PASS + 1)], BF16, name="eye", align_bytes=64)
         ones = keep.tile([P, P], F32, name="ones")
         ramp = keep.tile([P, P], F32, name="ramp", align_bytes=64)
-        turned = keep.tile([P, P], F32, name="turned", align_bytes=64)
+        turned = keep.tile([P, QUAD], F32, name="turned", align_bytes=64)
+        nc.vector.memset(scale_window[:].bitcast(I32), 0)
         nc.gpsimd.memset(ones[:], 1.0)
         nc.gpsimd.memset(eye[:].bitcast(I32), 0)
-        nc.gpsimd.memset(scale_window[:].bitcast(I32), 0)
-        nc.vector.tensor_tensor_scan(out=ramp[:], data0=ones[:], data1=ones[:], initial=0.0, op0=ALU.mult, op1=ALU.add)
-        nc.vector.transpose(out=turned[:], in_=ramp[:])
+        nc.vector.tensor_tensor_scan(out=ramp[:], data0=ones[:], data1=ones[:], initial=-1.0, op0=ALU.mult, op1=ALU.add)
+        nc.vector.transpose(out=turned[:], in_=ramp[:, 0:QUAD])
         for q in range(P // QUAD):
             quadrant = slice(QUAD * q, QUAD * (q + 1))
-            nc.vector.tensor_tensor(
-                out=eye[quadrant, :].rearrange("p (t u) -> p t u", t=PACK)[:, :, P * q : P * (q + 1) : PACK],
-                in0=ramp[quadrant, :].rearrange("p (t j) -> p t j", t=PACK),
-                in1=turned[quadrant, :].rearrange("p (t j) -> p t j", t=PACK),
-                op=ALU.is_equal,
+            nc.vector.tensor_scalar(
+                out=eye[quadrant, :].rearrange("p (t u) -> p t u", t=PACK)[:, :, P * q : P * (q + 1)],
+                in0=ramp[quadrant, :].unsqueeze(1).to_broadcast([QUAD, PACK, P]),
+                scalar1=1.0 / PACK, scalar2=turned[quadrant, 0:1], op0=ALU.mult, op1=ALU.is_equal,
             )
 
         sources = {"wt0": wt[0:K_PASS, :], "wt1": wt[K_PASS:K, :], "x": x, "wx": wx}
@@ -79,20 +79,18 @@ def tile_list_tiert_resL_kernel(tc, tab_words, tab_scales, wt, x, wx, rT, offs, 
         second_scales = keep.tile([P, J], U8, name="second_scales", align_bytes=64)
         table_scales = [picked_scales, second_scales]
 
-        nc.sync.dma_start(out=word_window[:], in_=tab_words[0].rearrange("p t b -> p (t b)").bitcast(I32))
-        for q in range(P // QUAD):
-            nc.sync.dma_start(
-                out=scale_window[QUAD * q : QUAD * q + 8, :].bitcast(I32),
-                in_=tab_scales[:, 4 * q : 4 * q + 4, :].bitcast(I32),
-            )
         load_piece("wt0", 0, QUARTER)
+        by_row = tab_scales.bitcast(I32).rearrange("a (q r) t -> r q a t", r=PACK)
+        for r in range(PACK):
+            nc.sync.dma_start(out=scale_window[r:P:SECOND_ROWS, 0:T].bitcast(I32), in_=by_row[r])
+        nc.sync.dma_start(out=word_window[:], in_=tab_words[0].rearrange("p t b -> p (t b)").bitcast(I32))
         load_piece("wt0", QUARTER, QUARTER)
         load_piece("wt1", 0)
         load_piece("wt0", HALF)
 
         nc.vector.tensor_copy(picked_scales[:], scale_window[:].indirect(offsets[:]))
         nc.gpsimd.memset(second_scales[:].bitcast(I32), 0)
-        nc.sync.dma_start(out=second_scales[0:112, :].bitcast(I32), in_=picked_scales[4:116, :].bitcast(I32))
+        nc.sync.dma_start(out=second_scales[0 : P - SECOND_ROWS, :].bitcast(I32), in_=picked_scales[SECOND_ROWS:P, :].bitcast(I32))
 
         load_piece("wt1", HALF)
         load_piece("x", 0)
@@ -188,7 +186,8 @@ def tile_list_tiert_resL_kernel(tc, tab_words, tab_scales, wt, x, wx, rT, offs, 
                     )
 
         def store(m, part):
-            nc.sync.dma_start(out=out[m * P : (m + 1) * P, part], in_=results[m][:, part])
+            queue = nc.scalar if m == ROW_TILES - 1 else nc.sync
+            queue.dma_start(out=out[m * P : (m + 1) * P, part], in_=results[m][:, part])
 
         nc.vector.tensor_copy(picked_words[:], word_window[:].bitcast(U32).indirect(offsets[:]))
         cast("wt0", 0, stage[0])

@@ -24,8 +24,8 @@ HALF = 512
 QUARTER = HALF // 2
 RUN = 2
 ROW_TILES = N // P
-LOAD_SLOTS = 15
-PICKED_SLOTS = 3
+LOAD_SLOTS = 13
+PICKED_SLOTS = 2
 STAGE_TILES = 6
 SECOND_ROWS = 16
 DECODE_BANK = 4
@@ -64,17 +64,17 @@ def tile_list_tiert_resL_kernel(tc, tab_words, tab_scales, wt, x, wx, rT, offs, 
         sources = {"wt0": wt[0:K_PASS, :], "wt1": wt[K_PASS:K, :], "x": x, "wx": wx}
         pieces, records = {}, {}
 
-        def load_piece(name, first, width=HALF):
-            piece = loads.tile([P, PACK, width], F32, name="piece", tag="load")
+        def load_piece(name, first, width=HALF, pool=loads, tag="load"):
+            piece = pool.tile([P, PACK, width], F32, name="piece", tag=tag, align_bytes=64)
             rows = sources[name].rearrange("(p t) n -> p t n", t=PACK)
             nc.sync.dma_start(out=piece[:], in_=rows[:, :, first : first + width])
             pieces[(name, first)] = piece
 
-        def load_record(m):
-            records[m] = loads.tile([P, T], F32, name="record", tag="load")
+        def load_record(m, pool=loads, tag="load"):
+            records[m] = pool.tile([P, T], F32, name="record", tag=tag, align_bytes=64)
             nc.sync.dma_start(out=records[m][:], in_=rT[m * P : (m + 1) * P, :])
 
-        word_window = loads.tile([P, T], I32, name="word_window", tag="load")
+        word_window = loads.tile([P, T], I32, name="word_window", tag="load", align_bytes=64)
         picked_scales = keep.tile([P, J], U8, name="picked_scales", align_bytes=64)
         second_scales = keep.tile([P, J], U8, name="second_scales", align_bytes=64)
         table_scales = [picked_scales, second_scales]
@@ -95,23 +95,29 @@ def tile_list_tiert_resL_kernel(tc, tab_words, tab_scales, wt, x, wx, rT, offs, 
         load_piece("wt1", HALF)
         load_piece("x", 0)
         load_piece("x", HALF)
-        load_piece("wx", 0)
+        load_piece("wx", 0, pool=keep, tag="shared")
         load_record(0)
         load_piece("wx", HALF)
-        for m in range(1, ROW_TILES):
+        load_record(1, pool=keep, tag="record1")
+        for m in range(2, ROW_TILES):
             load_record(m)
 
+        late = [("wx", HALF), ("wr1", HALF)]
+        late_words = keep.tile([P, len(late) * HALF], U32, name="late_words", tag="record1", align_bytes=64)
         words, scales = {}, {}
-        for name, width in (("eye", PACK * P), ("wt0", N), ("wt1", N), ("wr0", N), ("wr1", N), ("x", J), ("wx", N)):
-            words[name] = keep.tile([P, width], U32, name="words_" + name, align_bytes=64)
-            scales[name] = keep.tile([P, width], U8, name="scales_" + name, align_bytes=64)
+        for key in [("eye", 0)] + [(name, first) for name in TERMS + ("x",) for first in (0, HALF)]:
+            scales[key] = keep.tile([P, HALF], U8, name="scales_%s_%d" % key, align_bytes=64)
+            if key in late:
+                words[key] = late_words[:, late.index(key) * HALF : (late.index(key) + 1) * HALF]
+            else:
+                words[key] = keep.tile([P, HALF], U32, name="words_%s_%d" % key, align_bytes=64)
 
         def quantise(name, first, interleaved, parts=1):
-            width = interleaved.shape[1] // PACK // parts
+            width = HALF // parts
             for part in range(parts):
-                cols = slice(first + part * width, first + (part + 1) * width)
+                cols = slice(part * width, (part + 1) * width)
                 nc.vector.quantize_mx(
-                    out=words[name][:, cols].bitcast(FP8X4), scales=scales[name][:, cols],
+                    out=words[(name, first)][:, cols].bitcast(FP8X4), scales=scales[(name, first)][:, cols],
                     in_=interleaved[:, part * width * PACK : (part + 1) * width * PACK],
                 )
 
@@ -122,6 +128,8 @@ def tile_list_tiert_resL_kernel(tc, tab_words, tab_scales, wt, x, wx, rT, offs, 
             for i in range(STAGE_TILES)
         ]
         results = [keep.tile([P, J], F32, name="result%d" % m) for m in range(ROW_TILES)]
+        first_sum = keep.tile([P, J], F32, name="first_sum", tag="stage2", align_bytes=64)
+        decoded = keep.tile([P, HALF * PACK], F32, name="decoded", tag="shared", align_bytes=64)
         banks = [psum.tile([P, HALF], F32, name="bank%d" % i) for i in range(8)]
 
         def cast(name, first, tile):
@@ -132,18 +140,22 @@ def tile_list_tiert_resL_kernel(tc, tab_words, tab_scales, wt, x, wx, rT, offs, 
                 in_=piece[:].rearrange("p t (c i) -> p c t i", i=RUN),
             )
 
-        def leftover(a, first, tile):
-            name = "wt%d" % a
+        def decode(a, first, bank):
+            key = ("wt%d" % a, first)
             for b in range(HALF // P):
-                cols = slice(first + b * P, first + (b + 1) * P)
+                cols = slice(b * P, (b + 1) * P)
                 for t in range(PACK):
                     sel = slice(t * P, (t + 1) * P)
                     nc.tensor.matmul_mx(
-                        out=banks[DECODE_BANK + b][:, sel],
-                        lhsT=words["eye"][:, sel].bitcast(FP8X4), lhsT_scale=scales["eye"][:, sel],
-                        rhs=words[name][:, cols].bitcast(FP8X4), rhs_scale=scales[name][:, cols],
+                        out=banks[bank + b][:, sel],
+                        lhsT=words[("eye", 0)][:, sel].bitcast(FP8X4), lhsT_scale=scales[("eye", 0)][:, sel],
+                        rhs=words[key][:, cols].bitcast(FP8X4), rhs_scale=scales[key][:, cols],
                         start=True, stop=True,
                     )
+
+        def leftover(a, first, tile):
+            name = "wt%d" % a
+            decode(a, first, DECODE_BANK)
             for b in range(HALF // P):
                 col = first + b * P
                 start = max(s for n, s in pieces if n == name and s <= col)
@@ -155,39 +167,58 @@ def tile_list_tiert_resL_kernel(tc, tab_words, tab_scales, wt, x, wx, rT, offs, 
                     op=ALU.subtract,
                 )
 
+        def leftover_on_gpsimd(a, first, tile):
+            decode(a, first, 0)
+            for b in range(HALF // P):
+                part = slice(b * K_PASS, (b + 1) * K_PASS)
+                nc.scalar.copy(
+                    out=decoded[:, part].rearrange("p (n t) -> p n t", t=PACK),
+                    in_=banks[b][:].rearrange("p (t n) -> p n t", t=PACK),
+                )
+                nc.gpsimd.tensor_tensor(
+                    out=tile[:, part].rearrange("p (n t) -> p n t", t=PACK),
+                    in0=pieces[("wt%d" % a, first)][:, :, b * P : (b + 1) * P].rearrange("p t n -> p n t"),
+                    in1=decoded[:, part].rearrange("p (n t) -> p n t", t=PACK),
+                    op=ALU.subtract,
+                )
+
         picked_words = keep.tile([P, J], U32, name="picked_words", align_bytes=64)
         table_words = keep.tile([P, 2 * 2 * J], U8, name="table_words", tag="stage0", align_bytes=64)
         halves = [slice(0, HALF), slice(HALF, J)]
         picked = {}
 
         def gather(m, part):
-            if part.start == 0:
+            if part.start == 0 and m % 3 == 2:
+                picked[m] = keep.tile([P, J], F32, name="picked", tag="stage5", align_bytes=64)
+            elif part.start == 0:
                 picked[m] = picked_pool.tile([P, J], F32, name="picked")
             listed = offsets[:, part.start // LIST_ROWS : part.stop // LIST_ROWS]
             nc.vector.tensor_copy(picked[m][:, part], records[m][:].indirect(listed))
 
         def sum_bank(m, column):
-            return banks[2 * m % len(banks) + column // HALF]
+            return banks[(DECODE_BANK + 2 * m) % len(banks) + column // HALF]
 
         def products(m):
-            rows = slice(m * P, (m + 1) * P)
-            for s, name in enumerate(TERMS):
+            first = m * P // HALF * HALF
+            rows = slice(m * P - first, (m + 1) * P - first)
+            terms = TERMS if m < ROW_TILES // 2 else TERMS[1:] + TERMS[:1]
+            for s, name in enumerate(terms):
                 for half in halves:
                     if name == "wx":
-                        rhs, rhs_scale = words["x"][:, half].bitcast(FP8X4), scales["x"][:, half]
+                        rhs, rhs_scale = words[("x", half.start)][:].bitcast(FP8X4), scales[("x", half.start)][:]
                     else:
                         a = int(name[2])
                         rhs = table_words[:, 2 * (a * J + half.start) : 2 * (a * J + half.stop)].bitcast(FP4X4)
                         rhs_scale = table_scales[a][:, half]
                     nc.tensor.matmul_mx(
                         out=sum_bank(m, half.start)[:],
-                        lhsT=words[name][:, rows].bitcast(FP8X4), lhsT_scale=scales[name][:, rows],
+                        lhsT=words[(name, first)][:, rows].bitcast(FP8X4), lhsT_scale=scales[(name, first)][:, rows],
                         rhs=rhs, rhs_scale=rhs_scale, start=(s == 0), stop=(s == len(TERMS) - 1),
                     )
 
-        def store(m, part):
+        def store(m, part, source):
             queue = nc.scalar if m == ROW_TILES - 1 else nc.sync
-            queue.dma_start(out=out[m * P : (m + 1) * P, part], in_=results[m][:, part])
+            queue.dma_start(out=out[m * P : (m + 1) * P, part], in_=source[:, part])
 
         nc.vector.tensor_copy(picked_words[:], word_window[:].bitcast(U32).indirect(offsets[:]))
         cast("wt0", 0, stage[0])
@@ -202,7 +233,7 @@ def tile_list_tiert_resL_kernel(tc, tab_words, tab_scales, wt, x, wx, rT, offs, 
         quantise("wt1", 0, stage[1][:])
         quantise("wr0", 0, stage[5][:], parts=2)
 
-        following = [("wt1", 0), ("wt0", HALF), ("wt1", HALF), ("x", 0)]
+        following = [("wt1", 0), ("wt0", HALF), ("wt1", HALF)]
         for i in range(1, len(following)):
             name, first = following[i]
             tile = stage[i + 1]
@@ -213,26 +244,32 @@ def tile_list_tiert_resL_kernel(tc, tab_words, tab_scales, wt, x, wx, rT, offs, 
             quantise("wr" + before[2], before_first, tile[:], parts=2)
 
         whole = slice(0, J)
+        cast("x", 0, stage[4])
+        quantise("x", 0, stage[4][:])
         cast("x", HALF, stage[1])
         quantise("x", HALF, stage[1][:])
         cast("wx", 0, stage[5])
         quantise("wx", 0, stage[5][:])
+        leftover_on_gpsimd(1, HALF, stage[5])
         gather(0, whole)
+        gather(1, whole)
         cast("wx", HALF, stage[2])
         quantise("wx", HALF, stage[2][:])
+        quantise("wr1", HALF, stage[5][:])
 
         last = ROW_TILES - 1
         for m in range(last):
             parts = halves if m == last - 1 else [whole]
-            if m > 0:
+            if m > 1:
                 for part in parts:
                     gather(m, part)
             products(m)
             for half in halves:
                 nc.scalar.copy(out=results[m][:, half], in_=sum_bank(m, half.start)[:])
             for part in parts:
-                nc.gpsimd.tensor_tensor(out=results[m][:, part], in0=results[m][:, part], in1=picked[m][:, part], op=ALU.add)
-                store(m, part)
+                summed = first_sum if m == 0 else results[m]
+                nc.gpsimd.tensor_tensor(out=summed[:, part], in0=results[m][:, part], in1=picked[m][:, part], op=ALU.add)
+                store(m, part, summed)
 
         products(last)
         parts = [slice(0, HALF), slice(HALF, HALF + QUARTER), slice(HALF + QUARTER, J)]
@@ -245,4 +282,4 @@ def tile_list_tiert_resL_kernel(tc, tab_words, tab_scales, wt, x, wx, rT, offs, 
                 out=results[last][:, part], in0=sum_bank(last, part.start)[:, lo : lo + part.stop - part.start],
                 in1=picked[last][:, part], op=ALU.add,
             )
-            store(last, part)
+            store(last, part, results[last])

@@ -24,11 +24,11 @@ HALF = 512
 QUARTER = HALF // 2
 RUN = 2
 ROW_TILES = N // P
-LOAD_SLOTS = 13
-PICKED_SLOTS = 2
+LOAD_SLOTS = 14
+SUM_SLOTS = 3
 STAGE_TILES = 6
 SECOND_ROWS = 16
-DECODE_BANK = 4
+DECODE_BANKS = 4
 TERMS = ("wr1", "wt0", "wt1", "wr0", "wx")
 
 
@@ -37,7 +37,7 @@ def tile_list_tiert_resL_kernel(tc, tab_words, tab_scales, wt, x, wx, rT, offs, 
     with ExitStack() as ctx:
         keep = ctx.enter_context(tc.tile_pool(name="keep", bufs=1))
         loads = ctx.enter_context(tc.tile_pool(name="loads", bufs=LOAD_SLOTS))
-        picked_pool = ctx.enter_context(tc.tile_pool(name="picked", bufs=PICKED_SLOTS))
+        sum_pool = ctx.enter_context(tc.tile_pool(name="sums", bufs=SUM_SLOTS))
         psum = ctx.enter_context(tc.psum_pool(name="psum", bufs=1))
 
         offsets = keep.tile([P, J // LIST_ROWS], U16, name="offsets")
@@ -70,8 +70,8 @@ def tile_list_tiert_resL_kernel(tc, tab_words, tab_scales, wt, x, wx, rT, offs, 
             nc.sync.dma_start(out=piece[:], in_=rows[:, :, first : first + width])
             pieces[(name, first)] = piece
 
-        def load_record(m, pool=loads, tag="load"):
-            records[m] = pool.tile([P, T], F32, name="record", tag=tag, align_bytes=64)
+        def load_record(m):
+            records[m] = loads.tile([P, T], F32, name="record", tag="load", align_bytes=64)
             nc.sync.dma_start(out=records[m][:], in_=rT[m * P : (m + 1) * P, :])
 
         word_window = loads.tile([P, T], I32, name="word_window", tag="load", align_bytes=64)
@@ -79,12 +79,12 @@ def tile_list_tiert_resL_kernel(tc, tab_words, tab_scales, wt, x, wx, rT, offs, 
         second_scales = keep.tile([P, J], U8, name="second_scales", align_bytes=64)
         table_scales = [picked_scales, second_scales]
 
-        load_piece("wt0", 0, QUARTER)
+        load_piece("wt0", 0, QUARTER, pool=keep, tag="first")
         by_row = tab_scales.bitcast(I32).rearrange("a (q r) t -> r q a t", r=PACK)
         for r in range(PACK):
             nc.sync.dma_start(out=scale_window[r:P:SECOND_ROWS, 0:T].bitcast(I32), in_=by_row[r])
         nc.sync.dma_start(out=word_window[:], in_=tab_words[0].rearrange("p t b -> p (t b)").bitcast(I32))
-        load_piece("wt0", QUARTER, QUARTER)
+        load_piece("wt0", QUARTER, QUARTER, pool=keep, tag="second")
         load_piece("wt1", 0)
         load_piece("wt0", HALF)
 
@@ -95,22 +95,15 @@ def tile_list_tiert_resL_kernel(tc, tab_words, tab_scales, wt, x, wx, rT, offs, 
         load_piece("wt1", HALF)
         load_piece("x", 0)
         load_piece("x", HALF)
-        load_piece("wx", 0, pool=keep, tag="shared")
-        load_record(0)
+        load_piece("wx", 0)
         load_piece("wx", HALF)
-        load_record(1, pool=keep, tag="record1")
-        for m in range(2, ROW_TILES):
+        for m in range(ROW_TILES):
             load_record(m)
 
-        late = [("wx", HALF), ("wr1", HALF)]
-        late_words = keep.tile([P, len(late) * HALF], U32, name="late_words", tag="record1", align_bytes=64)
         words, scales = {}, {}
         for key in [("eye", 0)] + [(name, first) for name in TERMS + ("x",) for first in (0, HALF)]:
             scales[key] = keep.tile([P, HALF], U8, name="scales_%s_%d" % key, align_bytes=64)
-            if key in late:
-                words[key] = late_words[:, late.index(key) * HALF : (late.index(key) + 1) * HALF]
-            else:
-                words[key] = keep.tile([P, HALF], U32, name="words_%s_%d" % key, align_bytes=64)
+            words[key] = keep.tile([P, HALF], U32, name="words_%s_%d" % key, align_bytes=64)
 
         def quantise(name, first, interleaved, parts=1):
             width = HALF // parts
@@ -128,8 +121,6 @@ def tile_list_tiert_resL_kernel(tc, tab_words, tab_scales, wt, x, wx, rT, offs, 
             for i in range(STAGE_TILES)
         ]
         results = [keep.tile([P, J], F32, name="result%d" % m) for m in range(ROW_TILES)]
-        first_sum = keep.tile([P, J], F32, name="first_sum", tag="stage2", align_bytes=64)
-        decoded = keep.tile([P, HALF * PACK], F32, name="decoded", tag="shared", align_bytes=64)
         banks = [psum.tile([P, HALF], F32, name="bank%d" % i) for i in range(8)]
 
         def cast(name, first, tile):
@@ -155,7 +146,8 @@ def tile_list_tiert_resL_kernel(tc, tab_words, tab_scales, wt, x, wx, rT, offs, 
 
         def leftover(a, first, tile):
             name = "wt%d" % a
-            decode(a, first, DECODE_BANK)
+            bank = DECODE_BANKS * (1 - a)
+            decode(a, first, bank)
             for b in range(HALF // P):
                 col = first + b * P
                 start = max(s for n, s in pieces if n == name and s <= col)
@@ -163,40 +155,16 @@ def tile_list_tiert_resL_kernel(tc, tab_words, tab_scales, wt, x, wx, rT, offs, 
                 nc.vector.tensor_tensor(
                     out=tile[:, b * K_PASS : (b + 1) * K_PASS].rearrange("p (c i t) -> p c t i", i=RUN, t=PACK),
                     in0=weights.rearrange("p t (c i) -> p c t i", i=RUN),
-                    in1=banks[DECODE_BANK + b][:].rearrange("p (t c i) -> p c t i", t=PACK, i=RUN),
-                    op=ALU.subtract,
-                )
-
-        def leftover_on_gpsimd(a, first, tile):
-            decode(a, first, 0)
-            for b in range(HALF // P):
-                part = slice(b * K_PASS, (b + 1) * K_PASS)
-                nc.scalar.copy(
-                    out=decoded[:, part].rearrange("p (n t) -> p n t", t=PACK),
-                    in_=banks[b][:].rearrange("p (t n) -> p n t", t=PACK),
-                )
-                nc.gpsimd.tensor_tensor(
-                    out=tile[:, part].rearrange("p (n t) -> p n t", t=PACK),
-                    in0=pieces[("wt%d" % a, first)][:, :, b * P : (b + 1) * P].rearrange("p t n -> p n t"),
-                    in1=decoded[:, part].rearrange("p (n t) -> p n t", t=PACK),
+                    in1=banks[bank + b][:].rearrange("p (t c i) -> p c t i", t=PACK, i=RUN),
                     op=ALU.subtract,
                 )
 
         picked_words = keep.tile([P, J], U32, name="picked_words", align_bytes=64)
         table_words = keep.tile([P, 2 * 2 * J], U8, name="table_words", tag="stage0", align_bytes=64)
         halves = [slice(0, HALF), slice(HALF, J)]
-        picked = {}
-
-        def gather(m, part):
-            if part.start == 0 and m % 3 == 2:
-                picked[m] = keep.tile([P, J], F32, name="picked", tag="stage5", align_bytes=64)
-            elif part.start == 0:
-                picked[m] = picked_pool.tile([P, J], F32, name="picked")
-            listed = offsets[:, part.start // LIST_ROWS : part.stop // LIST_ROWS]
-            nc.vector.tensor_copy(picked[m][:, part], records[m][:].indirect(listed))
 
         def sum_bank(m, column):
-            return banks[(DECODE_BANK + 2 * m) % len(banks) + column // HALF]
+            return banks[(DECODE_BANKS + 2 * m) % len(banks) + column // HALF]
 
         def products(m):
             first = m * P // HALF * HALF
@@ -233,7 +201,7 @@ def tile_list_tiert_resL_kernel(tc, tab_words, tab_scales, wt, x, wx, rT, offs, 
         quantise("wt1", 0, stage[1][:])
         quantise("wr0", 0, stage[5][:], parts=2)
 
-        following = [("wt1", 0), ("wt0", HALF), ("wt1", HALF)]
+        following = [("wt1", 0), ("wt0", HALF), ("wt1", HALF), ("x", 0)]
         for i in range(1, len(following)):
             name, first = following[i]
             tile = stage[i + 1]
@@ -243,43 +211,27 @@ def tile_list_tiert_resL_kernel(tc, tab_words, tab_scales, wt, x, wx, rT, offs, 
             leftover(int(before[2]), before_first, tile)
             quantise("wr" + before[2], before_first, tile[:], parts=2)
 
-        whole = slice(0, J)
-        cast("x", 0, stage[4])
-        quantise("x", 0, stage[4][:])
-        cast("x", HALF, stage[1])
-        quantise("x", HALF, stage[1][:])
-        cast("wx", 0, stage[5])
-        quantise("wx", 0, stage[5][:])
-        leftover_on_gpsimd(1, HALF, stage[5])
-        gather(0, whole)
-        gather(1, whole)
-        cast("wx", HALF, stage[2])
-        quantise("wx", HALF, stage[2][:])
-        quantise("wr1", HALF, stage[5][:])
+        for name, first, tile in (("x", HALF, stage[1]), ("wx", 0, stage[5]), ("wx", HALF, stage[2])):
+            cast(name, first, tile)
+            quantise(name, first, tile[:])
 
         last = ROW_TILES - 1
-        for m in range(last):
-            parts = halves if m == last - 1 else [whole]
-            if m > 1:
-                for part in parts:
-                    gather(m, part)
+        for m in range(ROW_TILES):
+            parts = [slice(0, J)]
+            if m == 0:
+                parts = halves
+            if m == last:
+                parts = [slice(0, HALF), slice(HALF, HALF + QUARTER), slice(HALF + QUARTER, J)]
             products(m)
+            summed = sum_pool.tile([P, J], F32, name="summed", align_bytes=64)
             for half in halves:
-                nc.scalar.copy(out=results[m][:, half], in_=sum_bank(m, half.start)[:])
+                nc.scalar.copy(out=summed[:, half], in_=sum_bank(m, half.start)[:])
             for part in parts:
-                summed = first_sum if m == 0 else results[m]
-                nc.gpsimd.tensor_tensor(out=summed[:, part], in0=results[m][:, part], in1=picked[m][:, part], op=ALU.add)
-                store(m, part, summed)
-
-        products(last)
-        parts = [slice(0, HALF), slice(HALF, HALF + QUARTER), slice(HALF + QUARTER, J)]
-        gather(last, parts[0])
-        for i, part in enumerate(parts):
-            if i + 1 < len(parts):
-                gather(last, parts[i + 1])
-            lo = part.start % HALF
-            nc.vector.tensor_tensor(
-                out=results[last][:, part], in0=sum_bank(last, part.start)[:, lo : lo + part.stop - part.start],
-                in1=picked[last][:, part], op=ALU.add,
-            )
-            store(last, part, results[last])
+                listed = offsets[:, part.start // LIST_ROWS : part.stop // LIST_ROWS]
+                nc.vector.tensor_tensor(
+                    out=results[m][:, part], in0=records[m][:].indirect(listed), in1=summed[:, part], op=ALU.add,
+                )
+                if m == last:
+                    store(m, part, results[m])
+            if m < last:
+                store(m, slice(0, J), results[m])

@@ -24,12 +24,13 @@ HALF = 512
 QUARTER = HALF // 2
 RUN = 2
 ROW_TILES = N // P
-LOAD_SLOTS = 14
+LOAD_SLOTS = 8
 SUM_SLOTS = 3
 STAGE_TILES = 6
 SECOND_ROWS = 16
-DECODE_BANKS = 4
-TERMS = ("wr1", "wt0", "wt1", "wr0", "wx")
+DECODE_BANKS = (4, 5, 6, 7)
+LAST_DECODE_BANKS = (6, 7, 6, 7)
+TERMS = ("wt0", "wr0", "wt1", "wr1", "wx")
 
 
 def tile_list_tiert_resL_kernel(tc, tab_words, tab_scales, wt, x, wx, rT, offs, out):
@@ -62,13 +63,11 @@ def tile_list_tiert_resL_kernel(tc, tab_words, tab_scales, wt, x, wx, rT, offs, 
             )
 
         sources = {"wt0": wt[0:K_PASS, :], "wt1": wt[K_PASS:K, :], "x": x, "wx": wx}
-        pieces, records = {}, {}
+        operands, records = {}, {}
 
-        def load_piece(name, first, width=HALF, pool=loads, tag="load"):
-            piece = pool.tile([P, PACK, width], F32, name="piece", tag=tag, align_bytes=64)
-            rows = sources[name].rearrange("(p t) n -> p t n", t=PACK)
-            nc.sync.dma_start(out=piece[:], in_=rows[:, :, first : first + width])
-            pieces[(name, first)] = piece
+        def load_operand(name):
+            operands[name] = keep.tile([P, PACK, N], F32, name="operand_" + name, align_bytes=64)
+            nc.sync.dma_start(out=operands[name][:], in_=sources[name].rearrange("(p t) n -> p t n", t=PACK))
 
         def load_record(m):
             records[m] = loads.tile([P, T], F32, name="record", tag="load", align_bytes=64)
@@ -79,24 +78,21 @@ def tile_list_tiert_resL_kernel(tc, tab_words, tab_scales, wt, x, wx, rT, offs, 
         second_scales = keep.tile([P, J], U8, name="second_scales", align_bytes=64)
         table_scales = [picked_scales, second_scales]
 
-        load_piece("wt0", 0, QUARTER, pool=keep, tag="first")
+        nc.sync.dma_start(out=word_window[:], in_=tab_words[0].rearrange("p t b -> p (t b)").bitcast(I32))
         by_row = tab_scales.bitcast(I32).rearrange("a (q r) t -> r q a t", r=PACK)
         for r in range(PACK):
             nc.sync.dma_start(out=scale_window[r:P:SECOND_ROWS, 0:T].bitcast(I32), in_=by_row[r])
-        nc.sync.dma_start(out=word_window[:], in_=tab_words[0].rearrange("p t b -> p (t b)").bitcast(I32))
-        load_piece("wt0", QUARTER, QUARTER, pool=keep, tag="second")
-        load_piece("wt1", 0)
-        load_piece("wt0", HALF)
+        load_operand("wt0")
+        load_operand("wt1")
 
+        picked_words = keep.tile([P, J], U32, name="picked_words", align_bytes=64)
+        nc.vector.tensor_copy(picked_words[:], word_window[:].bitcast(U32).indirect(offsets[:]))
         nc.vector.tensor_copy(picked_scales[:], scale_window[:].indirect(offsets[:]))
         nc.gpsimd.memset(second_scales[:].bitcast(I32), 0)
         nc.sync.dma_start(out=second_scales[0 : P - SECOND_ROWS, :].bitcast(I32), in_=picked_scales[SECOND_ROWS:P, :].bitcast(I32))
 
-        load_piece("wt1", HALF)
-        load_piece("x", 0)
-        load_piece("x", HALF)
-        load_piece("wx", 0)
-        load_piece("wx", HALF)
+        load_operand("x")
+        load_operand("wx")
         for m in range(ROW_TILES):
             load_record(m)
 
@@ -106,11 +102,12 @@ def tile_list_tiert_resL_kernel(tc, tab_words, tab_scales, wt, x, wx, rT, offs, 
             words[key] = keep.tile([P, HALF], U32, name="words_%s_%d" % key, align_bytes=64)
 
         def quantise(name, first, interleaved, parts=1):
-            width = HALF // parts
+            width = interleaved.shape[1] // PACK // parts
+            key = (name, first // HALF * HALF)
             for part in range(parts):
-                cols = slice(part * width, (part + 1) * width)
+                cols = slice(first % HALF + part * width, first % HALF + (part + 1) * width)
                 nc.vector.quantize_mx(
-                    out=words[(name, first)][:, cols].bitcast(FP8X4), scales=scales[(name, first)][:, cols],
+                    out=words[key][:, cols].bitcast(FP8X4), scales=scales[key][:, cols],
                     in_=interleaved[:, part * width * PACK : (part + 1) * width * PACK],
                 )
 
@@ -120,57 +117,53 @@ def tile_list_tiert_resL_kernel(tc, tab_words, tab_scales, wt, x, wx, rT, offs, 
             keep.tile([P, HALF * PACK], BF16, name="stage%d" % i, tag="stage%d" % i, align_bytes=64)
             for i in range(STAGE_TILES)
         ]
-        results = [keep.tile([P, J], F32, name="result%d" % m) for m in range(ROW_TILES)]
+        results = [keep.tile([P, J], F32, name="result%d" % m) for m in range(ROW_TILES - 2)]
+        results = results + [keep.tile([P, J], F32, name="result", tag="stage%d" % i, align_bytes=64) for i in (2, 3)]
         banks = [psum.tile([P, HALF], F32, name="bank%d" % i) for i in range(8)]
 
-        def cast(name, first, tile):
-            piece = pieces[(name, first)]
-            lo = first % HALF * PACK
-            nc.scalar.copy(
-                out=tile[:, lo : lo + piece.shape[2] * PACK].rearrange("p (c i t) -> p c t i", i=RUN, t=PACK),
-                in_=piece[:].rearrange("p t (c i) -> p c t i", i=RUN),
+        def cast(name, first, interleaved, copy=nc.scalar.copy):
+            columns = operands[name][:, :, first : first + interleaved.shape[1] // PACK]
+            copy(
+                out=interleaved.rearrange("p (c i t) -> p c t i", i=RUN, t=PACK),
+                in_=columns.rearrange("p t (c i) -> p c t i", i=RUN),
             )
 
-        def decode(a, first, bank):
+        def decode(a, first, b, bank):
             key = ("wt%d" % a, first)
-            for b in range(HALF // P):
-                cols = slice(b * P, (b + 1) * P)
-                for t in range(PACK):
-                    sel = slice(t * P, (t + 1) * P)
-                    nc.tensor.matmul_mx(
-                        out=banks[bank + b][:, sel],
-                        lhsT=words[("eye", 0)][:, sel].bitcast(FP8X4), lhsT_scale=scales[("eye", 0)][:, sel],
-                        rhs=words[key][:, cols].bitcast(FP8X4), rhs_scale=scales[key][:, cols],
-                        start=True, stop=True,
-                    )
+            cols = slice(b * P, (b + 1) * P)
+            for t in range(PACK):
+                sel = slice(t * P, (t + 1) * P)
+                nc.tensor.matmul_mx(
+                    out=bank[:, sel],
+                    lhsT=words[("eye", 0)][:, sel].bitcast(FP8X4), lhsT_scale=scales[("eye", 0)][:, sel],
+                    rhs=words[key][:, cols].bitcast(FP8X4), rhs_scale=scales[key][:, cols],
+                    start=True, stop=True,
+                )
 
-        def leftover(a, first, tile):
+        def leftover(a, first, tile, places=DECODE_BANKS):
             name = "wt%d" % a
-            bank = DECODE_BANKS * (1 - a)
-            decode(a, first, bank)
             for b in range(HALF // P):
+                bank = banks[places[b]]
+                decode(a, first, b, bank)
                 col = first + b * P
-                start = max(s for n, s in pieces if n == name and s <= col)
-                weights = pieces[(name, start)][:, :, col - start : col - start + P]
+                weights = operands[name][:, :, col : col + P]
                 nc.vector.tensor_tensor(
                     out=tile[:, b * K_PASS : (b + 1) * K_PASS].rearrange("p (c i t) -> p c t i", i=RUN, t=PACK),
                     in0=weights.rearrange("p t (c i) -> p c t i", i=RUN),
-                    in1=banks[bank + b][:].rearrange("p (t c i) -> p c t i", t=PACK, i=RUN),
+                    in1=bank[:].rearrange("p (t c i) -> p c t i", t=PACK, i=RUN),
                     op=ALU.subtract,
                 )
 
-        picked_words = keep.tile([P, J], U32, name="picked_words", align_bytes=64)
         table_words = keep.tile([P, 2 * 2 * J], U8, name="table_words", tag="stage0", align_bytes=64)
         halves = [slice(0, HALF), slice(HALF, J)]
 
         def sum_bank(m, column):
-            return banks[(DECODE_BANKS + 2 * m) % len(banks) + column // HALF]
+            return banks[2 * m % len(banks) + column // HALF]
 
         def products(m):
             first = m * P // HALF * HALF
             rows = slice(m * P - first, (m + 1) * P - first)
-            terms = TERMS if m < ROW_TILES // 2 else TERMS[1:] + TERMS[:1]
-            for s, name in enumerate(terms):
+            for s, name in enumerate(TERMS):
                 for half in halves:
                     if name == "wx":
                         rhs, rhs_scale = words[("x", half.start)][:].bitcast(FP8X4), scales[("x", half.start)][:]
@@ -188,32 +181,38 @@ def tile_list_tiert_resL_kernel(tc, tab_words, tab_scales, wt, x, wx, rT, offs, 
             queue = nc.scalar if m == ROW_TILES - 1 else nc.sync
             queue.dma_start(out=out[m * P : (m + 1) * P, part], in_=source[:, part])
 
-        nc.vector.tensor_copy(picked_words[:], word_window[:].bitcast(U32).indirect(offsets[:]))
-        cast("wt0", 0, stage[0])
-        cast("wt0", QUARTER, stage[0])
-        quantise("wt0", 0, stage[0][:])
+        cast("wt0", 0, stage[0][:], copy=nc.vector.tensor_copy)
+        quantise("wt0", 0, stage[0][:], parts=2)
         nc.vector.tensor_copy(
             out=table_words[:].bitcast(U16).rearrange("p (d j) -> p d j", d=2),
             in_=picked_words[:].bitcast(U16).rearrange("p (j d) -> p d j", d=2),
         )
         leftover(0, 0, stage[5])
-        cast("wt1", 0, stage[1])
-        quantise("wt1", 0, stage[1][:])
+        cast("wt0", HALF, stage[1][:])
+        quantise("wt0", HALF, stage[1][:])
         quantise("wr0", 0, stage[5][:], parts=2)
 
-        following = [("wt1", 0), ("wt0", HALF), ("wt1", HALF), ("x", 0)]
+        following = [("wt0", HALF), ("wt1", 0), ("wt1", HALF)]
         for i in range(1, len(following)):
             name, first = following[i]
             tile = stage[i + 1]
-            cast(name, first, tile)
+            cast(name, first, tile[:])
             quantise(name, first, tile[:], parts=2)
             before, before_first = following[i - 1]
             leftover(int(before[2]), before_first, tile)
             quantise("wr" + before[2], before_first, tile[:], parts=2)
 
-        for name, first, tile in (("x", HALF, stage[1]), ("wx", 0, stage[5]), ("wx", HALF, stage[2])):
-            cast(name, first, tile)
-            quantise(name, first, tile[:])
+        upper = slice(QUARTER * PACK, HALF * PACK)
+        cast("x", 0, stage[4][:])
+        quantise("x", 0, stage[4][:], parts=2)
+        cast("x", HALF, stage[1][:])
+        quantise("x", HALF, stage[1][:])
+        cast("wx", 0, stage[4][:, upper])
+        quantise("wx", 0, stage[4][:, upper])
+        leftover(1, HALF, stage[4], LAST_DECODE_BANKS)
+        cast("wx", QUARTER, stage[5][:, upper])
+        quantise("wx", QUARTER, stage[5][:, upper])
+        quantise("wr1", HALF, stage[4][:], parts=2)
 
         last = ROW_TILES - 1
         for m in range(ROW_TILES):
@@ -235,3 +234,7 @@ def tile_list_tiert_resL_kernel(tc, tab_words, tab_scales, wt, x, wx, rT, offs, 
                     store(m, part, results[m])
             if m < last:
                 store(m, slice(0, J), results[m])
+            if m < 2:
+                cast("wx", HALF + m * QUARTER, stage[1][:, m * QUARTER * PACK : (m + 1) * QUARTER * PACK])
+            if m == 1:
+                quantise("wx", HALF, stage[1][:])

@@ -26,7 +26,7 @@ RUN = 2
 ROW_TILES = N // P
 LOAD_SLOTS = 8
 SUM_SLOTS = 3
-STAGE_TILES = 6
+STAGE_TILES = 7
 SECOND_ROWS = 16
 DECODE_BANKS = (4, 5, 6, 7)
 LAST_DECODE_BANKS = (6, 7, 6, 7)
@@ -63,11 +63,17 @@ def tile_list_tiert_resL_kernel(tc, tab_words, tab_scales, wt, x, wx, rT, offs, 
             )
 
         sources = {"wt0": wt[0:K_PASS, :], "wt1": wt[K_PASS:K, :], "x": x, "wx": wx}
-        operands, records = {}, {}
+        pieces, records = {}, {}
 
-        def load_operand(name):
-            operands[name] = keep.tile([P, PACK, N], F32, name="operand_" + name, align_bytes=64)
-            nc.sync.dma_start(out=operands[name][:], in_=sources[name].rearrange("(p t) n -> p t n", t=PACK))
+        def load_piece(name, first=0, width=N):
+            piece = keep.tile([P, PACK, width], F32, name="piece_%s_%d" % (name, first), align_bytes=64)
+            rows = sources[name].rearrange("(p t) n -> p t n", t=PACK)
+            nc.sync.dma_start(out=piece[:], in_=rows[:, :, first : first + width])
+            pieces[(name, first)] = piece
+
+        def columns(name, first, width):
+            start = max(s for n, s in pieces if n == name and s <= first)
+            return pieces[(name, start)][:, :, first - start : first - start + width]
 
         def load_record(m):
             records[m] = loads.tile([P, T], F32, name="record", tag="load", align_bytes=64)
@@ -82,8 +88,9 @@ def tile_list_tiert_resL_kernel(tc, tab_words, tab_scales, wt, x, wx, rT, offs, 
         by_row = tab_scales.bitcast(I32).rearrange("a (q r) t -> r q a t", r=PACK)
         for r in range(PACK):
             nc.sync.dma_start(out=scale_window[r:P:SECOND_ROWS, 0:T].bitcast(I32), in_=by_row[r])
-        load_operand("wt0")
-        load_operand("wt1")
+        load_piece("wt0", 0, HALF)
+        load_piece("wt0", HALF, HALF)
+        load_piece("wt1")
 
         picked_words = keep.tile([P, J], U32, name="picked_words", align_bytes=64)
         nc.vector.tensor_copy(picked_words[:], word_window[:].bitcast(U32).indirect(offsets[:]))
@@ -91,15 +98,17 @@ def tile_list_tiert_resL_kernel(tc, tab_words, tab_scales, wt, x, wx, rT, offs, 
         nc.gpsimd.memset(second_scales[:].bitcast(I32), 0)
         nc.sync.dma_start(out=second_scales[0 : P - SECOND_ROWS, :].bitcast(I32), in_=picked_scales[SECOND_ROWS:P, :].bitcast(I32))
 
-        load_operand("x")
-        load_operand("wx")
+        load_piece("x")
+        load_piece("wx")
         for m in range(ROW_TILES):
             load_record(m)
 
+        held = {("wr0", 0): 1, ("wr0", HALF): 2, ("wr1", 0): 3}
         words, scales = {}, {}
         for key in [("eye", 0)] + [(name, first) for name in TERMS + ("x",) for first in (0, HALF)]:
             scales[key] = keep.tile([P, HALF], U8, name="scales_%s_%d" % key, align_bytes=64)
-            words[key] = keep.tile([P, HALF], U32, name="words_%s_%d" % key, align_bytes=64)
+            if key not in held:
+                words[key] = keep.tile([P, HALF], U32, name="words_%s_%d" % key, align_bytes=64)
 
         def quantise(name, first, interleaved, parts=1):
             width = interleaved.shape[1] // PACK // parts
@@ -118,14 +127,13 @@ def tile_list_tiert_resL_kernel(tc, tab_words, tab_scales, wt, x, wx, rT, offs, 
             for i in range(STAGE_TILES)
         ]
         results = [keep.tile([P, J], F32, name="result%d" % m) for m in range(ROW_TILES - 2)]
-        results = results + [keep.tile([P, J], F32, name="result", tag="stage%d" % i, align_bytes=64) for i in (2, 3)]
+        results = results + [keep.tile([P, J], F32, name="result", tag="stage%d" % i, align_bytes=64) for i in (4, 5)]
         banks = [psum.tile([P, HALF], F32, name="bank%d" % i) for i in range(8)]
 
-        def cast(name, first, interleaved, copy=nc.scalar.copy):
-            columns = operands[name][:, :, first : first + interleaved.shape[1] // PACK]
-            copy(
+        def cast(name, first, interleaved):
+            nc.scalar.copy(
                 out=interleaved.rearrange("p (c i t) -> p c t i", i=RUN, t=PACK),
-                in_=columns.rearrange("p t (c i) -> p c t i", i=RUN),
+                in_=columns(name, first, interleaved.shape[1] // PACK).rearrange("p t (c i) -> p c t i", i=RUN),
             )
 
         def decode(a, first, b, bank):
@@ -146,7 +154,7 @@ def tile_list_tiert_resL_kernel(tc, tab_words, tab_scales, wt, x, wx, rT, offs, 
                 bank = banks[places[b]]
                 decode(a, first, b, bank)
                 col = first + b * P
-                weights = operands[name][:, :, col : col + P]
+                weights = columns(name, col, P)
                 nc.vector.tensor_tensor(
                     out=tile[:, b * K_PASS : (b + 1) * K_PASS].rearrange("p (c i t) -> p c t i", i=RUN, t=PACK),
                     in0=weights.rearrange("p t (c i) -> p c t i", i=RUN),
@@ -154,7 +162,9 @@ def tile_list_tiert_resL_kernel(tc, tab_words, tab_scales, wt, x, wx, rT, offs, 
                     op=ALU.subtract,
                 )
 
-        table_words = keep.tile([P, 2 * 2 * J], U8, name="table_words", tag="stage0", align_bytes=64)
+        table_words = keep.tile([P, 2 * 2 * J], U8, name="table_words", tag="stage6", align_bytes=64)
+        for key in held:
+            words[key] = keep.tile([P, HALF], U32, name="words_held", tag="stage%d" % held[key], align_bytes=64)
         halves = [slice(0, HALF), slice(HALF, J)]
 
         def sum_bank(m, column):
@@ -181,32 +191,32 @@ def tile_list_tiert_resL_kernel(tc, tab_words, tab_scales, wt, x, wx, rT, offs, 
             queue = nc.scalar if m == ROW_TILES - 1 else nc.sync
             queue.dma_start(out=out[m * P : (m + 1) * P, part], in_=source[:, part])
 
-        cast("wt0", 0, stage[0][:], copy=nc.vector.tensor_copy)
-        quantise("wt0", 0, stage[0][:], parts=2)
+        lower, upper = slice(0, QUARTER * PACK), slice(QUARTER * PACK, HALF * PACK)
+        cast("wt0", 0, stage[6][:, lower])
+        quantise("wt0", 0, stage[6][:, lower])
         nc.vector.tensor_copy(
             out=table_words[:].bitcast(U16).rearrange("p (d j) -> p d j", d=2),
             in_=picked_words[:].bitcast(U16).rearrange("p (j d) -> p d j", d=2),
         )
+        cast("wt0", QUARTER, stage[5][:, upper])
+        quantise("wt0", QUARTER, stage[5][:, upper])
         leftover(0, 0, stage[5])
         cast("wt0", HALF, stage[1][:])
         quantise("wt0", HALF, stage[1][:])
-        quantise("wr0", 0, stage[5][:], parts=2)
+        quantise("wr0", 0, stage[5][:])
+        leftover(0, HALF, stage[0])
+        cast("wt1", 0, stage[2][:])
+        quantise("wt1", 0, stage[2][:])
+        quantise("wr0", HALF, stage[0][:])
+        leftover(1, 0, stage[5])
+        cast("wt1", HALF, stage[3][:])
+        quantise("wt1", HALF, stage[3][:])
+        quantise("wr1", 0, stage[5][:])
 
-        following = [("wt0", HALF), ("wt1", 0), ("wt1", HALF)]
-        for i in range(1, len(following)):
-            name, first = following[i]
-            tile = stage[i + 1]
-            cast(name, first, tile[:])
-            quantise(name, first, tile[:], parts=2)
-            before, before_first = following[i - 1]
-            leftover(int(before[2]), before_first, tile)
-            quantise("wr" + before[2], before_first, tile[:], parts=2)
-
-        upper = slice(QUARTER * PACK, HALF * PACK)
         cast("x", 0, stage[4][:])
         quantise("x", 0, stage[4][:], parts=2)
-        cast("x", HALF, stage[1][:])
-        quantise("x", HALF, stage[1][:])
+        cast("x", HALF, stage[0][:])
+        quantise("x", HALF, stage[0][:])
         cast("wx", 0, stage[4][:, upper])
         quantise("wx", 0, stage[4][:, upper])
         leftover(1, HALF, stage[4], LAST_DECODE_BANKS)
@@ -235,6 +245,6 @@ def tile_list_tiert_resL_kernel(tc, tab_words, tab_scales, wt, x, wx, rT, offs, 
             if m < last:
                 store(m, slice(0, J), results[m])
             if m < 2:
-                cast("wx", HALF + m * QUARTER, stage[1][:, m * QUARTER * PACK : (m + 1) * QUARTER * PACK])
+                cast("wx", HALF + m * QUARTER, stage[0][:, m * QUARTER * PACK : (m + 1) * QUARTER * PACK])
             if m == 1:
-                quantise("wx", HALF, stage[1][:])
+                quantise("wx", HALF, stage[0][:])

@@ -24,31 +24,34 @@ HALF = 512
 QUARTER = HALF // 2
 RUN = 2
 ROW_TILES = N // P
-LOAD_SLOTS = 8
-SUM_SLOTS = 3
-STAGE_TILES = 7
+SUM_SLOTS = 4
 SECOND_ROWS = 16
 DECODE_BANKS = (4, 5, 6, 7)
 LAST_DECODE_BANKS = (6, 7, 6, 7)
-TERMS = ("wt0", "wr0", "wt1", "wr1", "wx")
+TABLE_TERMS = ("wt0", "wr0", "wt1", "wr1")
+ORDER = (0, 1, 2, 4, 5, 6, 7, 3)
+WX_GROUPS = ((0,), (1,), (2,), (4, 5), (6, 7), (3,))
 
 
 def tile_list_tiert_resL_kernel(tc, tab_words, tab_scales, wt, x, wx, rT, offs, out):
     nc = tc.nc
     with ExitStack() as ctx:
         keep = ctx.enter_context(tc.tile_pool(name="keep", bufs=1))
-        loads = ctx.enter_context(tc.tile_pool(name="loads", bufs=LOAD_SLOTS))
-        sum_pool = ctx.enter_context(tc.tile_pool(name="sums", bufs=SUM_SLOTS))
         psum = ctx.enter_context(tc.psum_pool(name="psum", bufs=1))
 
+        def place(name, shape, dtype, slot=None):
+            return keep.tile(shape, dtype, name=name, tag=slot or name, align_bytes=64)
+
         offsets = keep.tile([P, J // LIST_ROWS], U16, name="offsets")
+        word_window = place("word_window", [P, T], I32, "record%d" % (ROW_TILES - 1))
+        nc.sync.dma_start(out=word_window[:], in_=tab_words[0].rearrange("p t b -> p (t b)").bitcast(I32))
         nc.sync.dma_start(offsets[:], offs)
 
-        scale_window = keep.tile([P, T + 4], U8, name="scale_window", align_bytes=64)
-        eye = keep.tile([P, PACK * (K_PASS + 1)], BF16, name="eye", align_bytes=64)
-        ones = keep.tile([P, P], F32, name="ones")
-        ramp = keep.tile([P, P], F32, name="ramp", align_bytes=64)
-        turned = keep.tile([P, QUAD], F32, name="turned", align_bytes=64)
+        scale_window = place("scale_window", [P, T + 4], U8)
+        eye = place("eye", [P, PACK * (K_PASS + 1)], BF16)
+        ones = place("ones", [P, P], F32)
+        ramp = place("ramp", [P, P], F32)
+        turned = place("turned", [P, QUAD], F32)
         nc.vector.memset(scale_window[:].bitcast(I32), 0)
         nc.gpsimd.memset(ones[:], 1.0)
         nc.gpsimd.memset(eye[:].bitcast(I32), 0)
@@ -63,188 +66,180 @@ def tile_list_tiert_resL_kernel(tc, tab_words, tab_scales, wt, x, wx, rT, offs, 
             )
 
         sources = {"wt0": wt[0:K_PASS, :], "wt1": wt[K_PASS:K, :], "x": x, "wx": wx}
-        pieces, records = {}, {}
+        loaded = {}
 
-        def load_piece(name, first=0, width=N):
-            piece = keep.tile([P, PACK, width], F32, name="piece_%s_%d" % (name, first), align_bytes=64)
+        def load(name, first=0, width=N):
+            raw = place("raw_%s_%d" % (name, first), [P, PACK, width], F32)
             rows = sources[name].rearrange("(p t) n -> p t n", t=PACK)
-            nc.sync.dma_start(out=piece[:], in_=rows[:, :, first : first + width])
-            pieces[(name, first)] = piece
+            nc.sync.dma_start(out=raw[:], in_=rows[:, :, first : first + width])
+            loaded[(name, first)] = raw
 
         def columns(name, first, width):
-            start = max(s for n, s in pieces if n == name and s <= first)
-            return pieces[(name, start)][:, :, first - start : first - start + width]
+            start = max(s for n, s in loaded if n == name and s <= first)
+            return loaded[(name, start)][:, :, first - start : first - start + width]
 
-        def load_record(m):
-            records[m] = loads.tile([P, T], F32, name="record", tag="load", align_bytes=64)
-            nc.sync.dma_start(out=records[m][:], in_=rT[m * P : (m + 1) * P, :])
-
-        word_window = loads.tile([P, T], I32, name="word_window", tag="load", align_bytes=64)
-        picked_scales = keep.tile([P, J], U8, name="picked_scales", align_bytes=64)
-        second_scales = keep.tile([P, J], U8, name="second_scales", align_bytes=64)
-        table_scales = [picked_scales, second_scales]
-
-        nc.sync.dma_start(out=word_window[:], in_=tab_words[0].rearrange("p t b -> p (t b)").bitcast(I32))
         by_row = tab_scales.bitcast(I32).rearrange("a (q r) t -> r q a t", r=PACK)
         for r in range(PACK):
             nc.sync.dma_start(out=scale_window[r:P:SECOND_ROWS, 0:T].bitcast(I32), in_=by_row[r])
-        load_piece("wt0", 0, HALF)
-        load_piece("wt0", HALF, HALF)
-        load_piece("wt1")
+        load("wt0", 0, HALF)
+        load("wt0", HALF, HALF)
+        load("wt1")
 
-        picked_words = keep.tile([P, J], U32, name="picked_words", align_bytes=64)
+        picked_words = place("picked_words", [P, J], U32)
+        picked_scales = place("picked_scales", [P, J], U8)
+        second_scales = place("second_scales", [P, J], U8)
+        table_scales = [picked_scales, second_scales]
         nc.vector.tensor_copy(picked_words[:], word_window[:].bitcast(U32).indirect(offsets[:]))
         nc.vector.tensor_copy(picked_scales[:], scale_window[:].indirect(offsets[:]))
         nc.gpsimd.memset(second_scales[:].bitcast(I32), 0)
         nc.sync.dma_start(out=second_scales[0 : P - SECOND_ROWS, :].bitcast(I32), in_=picked_scales[SECOND_ROWS:P, :].bitcast(I32))
 
-        load_piece("x")
-        load_piece("wx")
-        for m in range(ROW_TILES):
-            load_record(m)
+        load("x")
+        load("wx")
+        records = []
+        for i, m in enumerate(ORDER):
+            records.append(place("record%d" % i, [P, T], F32))
+            nc.sync.dma_start(out=records[i][:], in_=rT[m * P : (m + 1) * P, :])
 
-        held = {("wr0", 0): 1, ("wr0", HALF): 2, ("wr1", 0): 3}
-        words, scales = {}, {}
-        for key in [("eye", 0)] + [(name, first) for name in TERMS + ("x",) for first in (0, HALF)]:
-            scales[key] = keep.tile([P, HALF], U8, name="scales_%s_%d" % key, align_bytes=64)
-            if key not in held:
-                words[key] = keep.tile([P, HALF], U32, name="words_%s_%d" % key, align_bytes=64)
-
-        def quantise(name, first, interleaved, parts=1):
-            width = interleaved.shape[1] // PACK // parts
-            key = (name, first // HALF * HALF)
-            for part in range(parts):
-                cols = slice(first % HALF + part * width, first % HALF + (part + 1) * width)
-                nc.vector.quantize_mx(
-                    out=words[key][:, cols].bitcast(FP8X4), scales=scales[key][:, cols],
-                    in_=interleaved[:, part * width * PACK : (part + 1) * width * PACK],
-                )
-
-        quantise("eye", 0, eye[:, 0 : PACK * K_PASS])
-
-        stage = [
-            keep.tile([P, HALF * PACK], BF16, name="stage%d" % i, tag="stage%d" % i, align_bytes=64)
-            for i in range(STAGE_TILES)
-        ]
-        results = [keep.tile([P, J], F32, name="result%d" % m) for m in range(ROW_TILES - 2)]
-        results = results + [keep.tile([P, J], F32, name="result", tag="stage%d" % i, align_bytes=64) for i in (4, 5)]
         banks = [psum.tile([P, HALF], F32, name="bank%d" % i) for i in range(8)]
+        words, scales = {}, {}
 
-        def cast(name, first, interleaved):
-            nc.scalar.copy(
-                out=interleaved.rearrange("p (c i t) -> p c t i", i=RUN, t=PACK),
-                in_=columns(name, first, interleaved.shape[1] // PACK).rearrange("p t (c i) -> p c t i", i=RUN),
-            )
+        def planes(key, width, slot=None):
+            words[key] = place("words_%s_%d" % key, [P, width], U32, slot)
+            scales[key] = place("scales_%s_%d" % key, [P, width], U8)
 
-        def decode(a, first, b, bank):
-            key = ("wt%d" % a, first)
-            cols = slice(b * P, (b + 1) * P)
-            for t in range(PACK):
-                sel = slice(t * P, (t + 1) * P)
-                nc.tensor.matmul_mx(
-                    out=bank[:, sel],
-                    lhsT=words[("eye", 0)][:, sel].bitcast(FP8X4), lhsT_scale=scales[("eye", 0)][:, sel],
-                    rhs=words[key][:, cols].bitcast(FP8X4), rhs_scale=scales[key][:, cols],
-                    start=True, stop=True,
-                )
+        def quantise(key, first, interleaved):
+            cols = slice(first, first + interleaved.shape[1] // PACK)
+            nc.vector.quantize_mx(out=words[key][:, cols].bitcast(FP8X4), scales=scales[key][:, cols], in_=interleaved)
 
-        def leftover(a, first, tile, places=DECODE_BANKS):
-            name = "wt%d" % a
+        def walks(name, first, width, slot):
+            tile = place("cast_%s_%d" % (name, first), [P, width * PACK], BF16, slot)
+            written = tile[:].rearrange("p (c i t) -> p c t i", i=RUN, t=PACK)
+            return tile, written, columns(name, first, width).rearrange("p t (c i) -> p c t i", i=RUN)
+
+        def cast(name, first, width, slot=None):
+            tile, written, read = walks(name, first, width, slot)
+            nc.scalar.copy(out=written, in_=read)
+            return tile
+
+        def leftover(name, first, slot, places=DECODE_BANKS):
+            tile = place("left_%s_%d" % (name, first), [P, HALF * PACK], BF16, slot)
+            key, identity = (name, first), ("eye", 0)
             for b in range(HALF // P):
                 bank = banks[places[b]]
-                decode(a, first, b, bank)
-                col = first + b * P
-                weights = columns(name, col, P)
+                cols = slice(b * P, (b + 1) * P)
+                for t in range(PACK):
+                    sel = slice(t * P, (t + 1) * P)
+                    nc.tensor.matmul_mx(
+                        out=bank[:, sel],
+                        lhsT=words[identity][:, sel].bitcast(FP8X4), lhsT_scale=scales[identity][:, sel],
+                        rhs=words[key][:, cols].bitcast(FP8X4), rhs_scale=scales[key][:, cols],
+                        start=True, stop=True,
+                    )
                 nc.vector.tensor_tensor(
                     out=tile[:, b * K_PASS : (b + 1) * K_PASS].rearrange("p (c i t) -> p c t i", i=RUN, t=PACK),
-                    in0=weights.rearrange("p t (c i) -> p c t i", i=RUN),
+                    in0=columns(name, first + b * P, P).rearrange("p t (c i) -> p c t i", i=RUN),
                     in1=bank[:].rearrange("p (t c i) -> p c t i", t=PACK, i=RUN),
                     op=ALU.subtract,
                 )
+            return tile
 
-        table_words = keep.tile([P, 2 * 2 * J], U8, name="table_words", tag="stage6", align_bytes=64)
-        for key in held:
-            words[key] = keep.tile([P, HALF], U32, name="words_held", tag="stage%d" % held[key], align_bytes=64)
-        halves = [slice(0, HALF), slice(HALF, J)]
+        planes(("eye", 0), HALF)
+        quantise(("eye", 0), 0, eye[:, 0 : PACK * K_PASS])
 
-        def sum_bank(m, column):
-            return banks[2 * m % len(banks) + column // HALF]
-
-        def products(m):
-            first = m * P // HALF * HALF
-            rows = slice(m * P - first, (m + 1) * P - first)
-            for s, name in enumerate(TERMS):
-                for half in halves:
-                    if name == "wx":
-                        rhs, rhs_scale = words[("x", half.start)][:].bitcast(FP8X4), scales[("x", half.start)][:]
-                    else:
-                        a = int(name[2])
-                        rhs = table_words[:, 2 * (a * J + half.start) : 2 * (a * J + half.stop)].bitcast(FP4X4)
-                        rhs_scale = table_scales[a][:, half]
-                    nc.tensor.matmul_mx(
-                        out=sum_bank(m, half.start)[:],
-                        lhsT=words[(name, first)][:, rows].bitcast(FP8X4), lhsT_scale=scales[(name, first)][:, rows],
-                        rhs=rhs, rhs_scale=rhs_scale, start=(s == 0), stop=(s == len(TERMS) - 1),
-                    )
-
-        def store(m, part, source):
-            queue = nc.scalar if m == ROW_TILES - 1 else nc.sync
-            queue.dma_start(out=out[m * P : (m + 1) * P, part], in_=source[:, part])
-
-        lower, upper = slice(0, QUARTER * PACK), slice(QUARTER * PACK, HALF * PACK)
-        cast("wt0", 0, stage[6][:, lower])
-        quantise("wt0", 0, stage[6][:, lower])
+        planes(("wt0", 0), HALF)
+        quantise(("wt0", 0), 0, cast("wt0", 0, QUARTER, "first_cast")[:])
+        table_words = place("table_words", [P, 2 * 2 * J], U8, "first_cast")
         nc.vector.tensor_copy(
             out=table_words[:].bitcast(U16).rearrange("p (d j) -> p d j", d=2),
             in_=picked_words[:].bitcast(U16).rearrange("p (j d) -> p d j", d=2),
         )
-        cast("wt0", QUARTER, stage[5][:, upper])
-        quantise("wt0", QUARTER, stage[5][:, upper])
-        leftover(0, 0, stage[5])
-        cast("wt0", HALF, stage[1][:])
-        quantise("wt0", HALF, stage[1][:])
-        quantise("wr0", 0, stage[5][:])
-        leftover(0, HALF, stage[0])
-        cast("wt1", 0, stage[2][:])
-        quantise("wt1", 0, stage[2][:])
-        quantise("wr0", HALF, stage[0][:])
-        leftover(1, 0, stage[5])
-        cast("wt1", HALF, stage[3][:])
-        quantise("wt1", HALF, stage[3][:])
-        quantise("wr1", 0, stage[5][:])
+        quantise(("wt0", 0), QUARTER, cast("wt0", QUARTER, QUARTER)[:])
 
-        cast("x", 0, stage[4][:])
-        quantise("x", 0, stage[4][:], parts=2)
-        cast("x", HALF, stage[0][:])
-        quantise("x", HALF, stage[0][:])
-        cast("wx", 0, stage[4][:, upper])
-        quantise("wx", 0, stage[4][:, upper])
-        leftover(1, HALF, stage[4], LAST_DECODE_BANKS)
-        cast("wx", QUARTER, stage[5][:, upper])
-        quantise("wx", QUARTER, stage[5][:, upper])
-        quantise("wr1", HALF, stage[4][:], parts=2)
+        pieces = [("wt0", 0), ("wt0", HALF), ("wt1", 0), ("wt1", HALF)]
+        left = leftover("wt0", 0, "left0")
+        for i in range(1, len(pieces)):
+            name, first = pieces[i]
+            planes(pieces[i], HALF)
+            quantise(pieces[i], 0, cast(name, first, HALF, "cast%d" % i)[:])
+            before = ("wr" + pieces[i - 1][0][2], pieces[i - 1][1])
+            planes(before, HALF, "cast%d" % i)
+            quantise(before, 0, left[:])
+            left = leftover(name, first, "left%d" % (i % 2), LAST_DECODE_BANKS if i == len(pieces) - 1 else DECODE_BANKS)
+
+        group_of = {m: g for g, group in enumerate(WX_GROUPS) for m in group}
+        wx_cast = {}
+
+        def cast_wx(g, slot=None):
+            wx_cast[g] = cast("wx", WX_GROUPS[g][0] * P, len(WX_GROUPS[g]) * P, slot)
+
+        def quantise_wx(g, slot):
+            planes(("wx", g), len(WX_GROUPS[g]) * P, slot)
+            quantise(("wx", g), 0, wx_cast[g][:])
+
+        for first in (0, HALF):
+            planes(("x", first), HALF)
+            quantise(("x", first), 0, cast("x", first, HALF)[:])
+        cast_wx(0, "wx_cast0")
+        quantise_wx(0, "wx_group0")
+        planes(("wr1", HALF), HALF, "wx_cast0")
+        quantise(("wr1", HALF), 0, left[:])
+        cast_wx(1)
+        quantise_wx(1, "wx_group1")
+
+        halves = [slice(0, HALF), slice(HALF, J)]
+
+        def sum_bank(i, half):
+            return banks[2 * i % len(banks) + half.start // HALF]
+
+        def products(i):
+            m = ORDER[i]
+            terms = TABLE_TERMS[::-1] if i == 3 else TABLE_TERMS
+            for s in range(len(terms) + 1):
+                for half in halves:
+                    if s < len(terms):
+                        a = int(terms[s][2])
+                        key = (terms[s], m * P // HALF * HALF)
+                        first = m * P - key[1]
+                        rhs = table_words[:, 2 * (a * J + half.start) : 2 * (a * J + half.stop)].bitcast(FP4X4)
+                        rhs_scale = table_scales[a][:, half]
+                    else:
+                        key = ("wx", group_of[m])
+                        first = (m - WX_GROUPS[group_of[m]][0]) * P
+                        rhs, rhs_scale = words[("x", half.start)][:].bitcast(FP8X4), scales[("x", half.start)][:]
+                    rows = slice(first, first + P)
+                    nc.tensor.matmul_mx(
+                        out=sum_bank(i, half)[:],
+                        lhsT=words[key][:, rows].bitcast(FP8X4), lhsT_scale=scales[key][:, rows],
+                        rhs=rhs, rhs_scale=rhs_scale, start=(s == 0), stop=(s == len(TABLE_TERMS)),
+                    )
+
+        shared = [place("results01", [P, 2, J], F32, "raw_wt0_0"), place("results23", [P, 2, J], F32, "raw_wt0_%d" % HALF)]
+        shared.append(place("results4567", [P, 4, J], F32, "raw_wt1_0"))
+        results = [shared[0][:, 0, :], shared[0][:, 1, :], shared[1][:, 0, :], shared[1][:, 1, :]]
+        results = results + [shared[2][:, i, :] for i in range(4)]
 
         last = ROW_TILES - 1
-        for m in range(ROW_TILES):
-            parts = [slice(0, J)]
-            if m == 0:
-                parts = halves
-            if m == last:
-                parts = [slice(0, HALF), slice(HALF, HALF + QUARTER), slice(HALF + QUARTER, J)]
-            products(m)
-            summed = sum_pool.tile([P, J], F32, name="summed", align_bytes=64)
+        cast_slots = {0: (2, "wx_group0"), 1: (3, "wx_group1"), 2: (4, "sum0_0"), 3: (5, "wx_group1")}
+        for i, m in enumerate(ORDER):
+            products(i)
             for half in halves:
-                nc.scalar.copy(out=summed[:, half], in_=sum_bank(m, half.start)[:])
-            for part in parts:
-                listed = offsets[:, part.start // LIST_ROWS : part.stop // LIST_ROWS]
-                nc.vector.tensor_tensor(
-                    out=results[m][:, part], in0=records[m][:].indirect(listed), in1=summed[:, part], op=ALU.add,
-                )
-                if m == last:
-                    store(m, part, results[m])
-            if m < last:
-                store(m, slice(0, J), results[m])
-            if m < 2:
-                cast("wx", HALF + m * QUARTER, stage[0][:, m * QUARTER * PACK : (m + 1) * QUARTER * PACK])
-            if m == 1:
-                quantise("wx", HALF, stage[0][:])
+                summed = place("summed", [P, HALF], F32, "sum%d_%d" % (i % SUM_SLOTS, half.start))
+                nc.scalar.copy(out=summed[:], in_=sum_bank(i, half)[:])
+                parts = [half]
+                if i == last and half.stop == J:
+                    parts = [slice(HALF, HALF + QUARTER), slice(HALF + QUARTER, J)]
+                for part in parts:
+                    listed = offsets[:, part.start // LIST_ROWS : part.stop // LIST_ROWS]
+                    nc.vector.tensor_tensor(
+                        out=results[m][:, part], in0=records[i][:].indirect(listed),
+                        in1=summed[:, part.start - half.start : part.stop - half.start], op=ALU.add,
+                    )
+                    if i == last:
+                        nc.scalar.dma_start(out=out[m * P : (m + 1) * P, part], in_=results[m][:, part])
+            if i < last:
+                nc.sync.dma_start(out=out[m * P : (m + 1) * P, :], in_=results[m])
+            if i in cast_slots:
+                group, slot = cast_slots[i]
+                cast_wx(group, slot)
+                quantise_wx(group, "sum%d_0" % (i % SUM_SLOTS))

@@ -24,13 +24,15 @@ HALF = 512
 QUARTER = HALF // 2
 RUN = 2
 ROW_TILES = N // P
-SUM_SLOTS = 4
+SUM_SLOTS = 3
 SECOND_ROWS = 16
 DECODE_BANKS = (4, 5, 6, 7)
 LAST_DECODE_BANKS = (6, 7, 6, 7)
 TABLE_TERMS = ("wt0", "wr0", "wt1", "wr1")
-ORDER = (0, 1, 2, 4, 5, 6, 7, 3)
-WX_GROUPS = ((0,), (1,), (2,), (4, 5), (6, 7), (3,))
+WX_GROUPS = ((0,), (1,), (2,), (3, 4), (5, 6, 7))
+LEAD = T // 4
+PAD = 16
+HALVED = 3
 
 
 def tile_list_tiert_resL_kernel(tc, tab_words, tab_scales, wt, x, wx, rT, offs, out):
@@ -44,26 +46,38 @@ def tile_list_tiert_resL_kernel(tc, tab_words, tab_scales, wt, x, wx, rT, offs, 
 
         offsets = keep.tile([P, J // LIST_ROWS], U16, name="offsets")
         word_window = place("word_window", [P, T], I32, "record%d" % (ROW_TILES - 1))
-        nc.sync.dma_start(out=word_window[:], in_=tab_words[0].rearrange("p t b -> p (t b)").bitcast(I32))
+        word_rows = tab_words[0].rearrange("p t b -> p (t b)").bitcast(I32)
+        nc.sync.dma_start(out=word_window[:, 0:LEAD], in_=word_rows[:, 0:LEAD])
         nc.sync.dma_start(offsets[:], offs)
 
         scale_window = place("scale_window", [P, T + 4], U8)
-        eye = place("eye", [P, PACK * (K_PASS + 1)], BF16)
+        eye = place("eye", [P, K_PASS], BF16)
+        eye_words = place("eye_words", [P, PAD + HALF], U32)
+        eye_scales = place("eye_scales", [P, P], U8)
         ones = place("ones", [P, P], F32)
         ramp = place("ramp", [P, P], F32)
         turned = place("turned", [P, QUAD], F32)
-        nc.vector.memset(scale_window[:].bitcast(I32), 0)
+        nc.gpsimd.memset(scale_window[:, 0 : T // 2].bitcast(I32), 0)
+        nc.vector.memset(scale_window[:, T // 2 : T + 4].bitcast(I32), 0)
         nc.gpsimd.memset(ones[:], 1.0)
         nc.gpsimd.memset(eye[:].bitcast(I32), 0)
+        nc.gpsimd.memset(eye_words[:, PAD - 1 : PAD].bitcast(I32), 0)
         nc.vector.tensor_tensor_scan(out=ramp[:], data0=ones[:], data1=ones[:], initial=-1.0, op0=ALU.mult, op1=ALU.add)
         nc.vector.transpose(out=turned[:], in_=ramp[:, 0:QUAD])
         for q in range(P // QUAD):
             quadrant = slice(QUAD * q, QUAD * (q + 1))
             nc.vector.tensor_scalar(
-                out=eye[quadrant, :].rearrange("p (t u) -> p t u", t=PACK)[:, :, P * q : P * (q + 1)],
-                in0=ramp[quadrant, :].unsqueeze(1).to_broadcast([QUAD, PACK, P]),
+                out=eye[quadrant, P * q : P * (q + 1)], in0=ramp[quadrant, :],
                 scalar1=1.0 / PACK, scalar2=turned[quadrant, 0:1], op0=ALU.mult, op1=ALU.is_equal,
             )
+        nc.vector.quantize_mx(out=eye_words[:, PAD : PAD + P].bitcast(FP8X4), scales=eye_scales[:], in_=eye[:])
+        eye_bytes, eye_pairs = eye_words[:].bitcast(U8), eye_words[:].bitcast(U16)
+        nc.gpsimd.tensor_copy(
+            out=eye_bytes[:, 4 * (PAD + P) : 4 * (PAD + 2 * P)], in_=eye_bytes[:, 4 * PAD - 1 : 4 * (PAD + P) - 1],
+        )
+        nc.scalar.copy(
+            out=eye_pairs[:, 2 * (PAD + 2 * P) : 2 * (PAD + 4 * P)], in_=eye_pairs[:, 2 * PAD - 1 : 2 * (PAD + 2 * P) - 1],
+        )
 
         sources = {"wt0": wt[0:K_PASS, :], "wt1": wt[K_PASS:K, :], "x": x, "wx": wx}
         loaded = {}
@@ -81,6 +95,7 @@ def tile_list_tiert_resL_kernel(tc, tab_words, tab_scales, wt, x, wx, rT, offs, 
         by_row = tab_scales.bitcast(I32).rearrange("a (q r) t -> r q a t", r=PACK)
         for r in range(PACK):
             nc.sync.dma_start(out=scale_window[r:P:SECOND_ROWS, 0:T].bitcast(I32), in_=by_row[r])
+        nc.sync.dma_start(out=word_window[:, LEAD:T], in_=word_rows[:, LEAD:T])
         load("wt0", 0, HALF)
         load("wt0", HALF, HALF)
         load("wt1")
@@ -89,129 +104,120 @@ def tile_list_tiert_resL_kernel(tc, tab_words, tab_scales, wt, x, wx, rT, offs, 
         picked_scales = place("picked_scales", [P, J], U8)
         second_scales = place("second_scales", [P, J], U8)
         table_scales = [picked_scales, second_scales]
-        nc.vector.tensor_copy(picked_words[:], word_window[:].bitcast(U32).indirect(offsets[:]))
         nc.vector.tensor_copy(picked_scales[:], scale_window[:].indirect(offsets[:]))
+        nc.vector.tensor_copy(picked_words[:], word_window[:].bitcast(U32).indirect(offsets[:]))
         nc.gpsimd.memset(second_scales[:].bitcast(I32), 0)
         nc.sync.dma_start(out=second_scales[0 : P - SECOND_ROWS, :].bitcast(I32), in_=picked_scales[SECOND_ROWS:P, :].bitcast(I32))
 
         load("x")
         load("wx")
         records = []
-        for i, m in enumerate(ORDER):
-            records.append(place("record%d" % i, [P, T], F32))
-            nc.sync.dma_start(out=records[i][:], in_=rT[m * P : (m + 1) * P, :])
+        for m in range(ROW_TILES):
+            records.append(place("record%d" % m, [P, T], F32))
+            nc.sync.dma_start(out=records[m][:], in_=rT[m * P : (m + 1) * P, :])
 
         banks = [psum.tile([P, HALF], F32, name="bank%d" % i) for i in range(8)]
-        words, scales = {}, {}
+        planes = {}
 
-        def planes(key, width, slot=None):
-            words[key] = place("words_%s_%d" % key, [P, width], U32, slot)
-            scales[key] = place("scales_%s_%d" % key, [P, width], U8)
+        def plane_tiles(name, width, slot=None):
+            return place("words_" + name, [P, width], U32, slot), place("scales_" + name, [P, width], U8)
 
-        def quantise(key, first, interleaved):
+        def quantise(tiles, first, interleaved):
             cols = slice(first, first + interleaved.shape[1] // PACK)
-            nc.vector.quantize_mx(out=words[key][:, cols].bitcast(FP8X4), scales=scales[key][:, cols], in_=interleaved)
+            nc.vector.quantize_mx(out=tiles[0][:, cols].bitcast(FP8X4), scales=tiles[1][:, cols], in_=interleaved)
 
-        def walks(name, first, width, slot):
-            tile = place("cast_%s_%d" % (name, first), [P, width * PACK], BF16, slot)
-            written = tile[:].rearrange("p (c i t) -> p c t i", i=RUN, t=PACK)
-            return tile, written, columns(name, first, width).rearrange("p t (c i) -> p c t i", i=RUN)
+        def enter(name, first, width, tiles, at=0):
+            for b in range(width // P):
+                planes[(name, first + b * P)] = (tiles, at + b * P)
 
-        def cast(name, first, width, slot=None):
-            tile, written, read = walks(name, first, width, slot)
-            nc.scalar.copy(out=written, in_=read)
-            return tile
+        def operand(name, first, width):
+            tiles, at = planes[(name, first)]
+            return tiles[0][:, at : at + width].bitcast(FP8X4), tiles[1][:, at : at + width]
 
-        def leftover(name, first, slot, places=DECODE_BANKS):
-            tile = place("left_%s_%d" % (name, first), [P, HALF * PACK], BF16, slot)
-            key, identity = (name, first), ("eye", 0)
-            for b in range(HALF // P):
+        def staged(name, width, slot=None):
+            return place("staged_" + name, [P, width * PACK], BF16, slot)
+
+        def cast(name, first, interleaved):
+            nc.scalar.copy(
+                out=interleaved.rearrange("p (c i t) -> p c t i", i=RUN, t=PACK),
+                in_=columns(name, first, interleaved.shape[1] // PACK).rearrange("p t (c i) -> p c t i", i=RUN),
+            )
+
+        def leftover(name, first, interleaved, places):
+            for b in range(interleaved.shape[1] // K_PASS):
                 bank = banks[places[b]]
-                cols = slice(b * P, (b + 1) * P)
+                codes, bytes_of_scale = operand(name, first + b * P, P)
                 for t in range(PACK):
-                    sel = slice(t * P, (t + 1) * P)
                     nc.tensor.matmul_mx(
-                        out=bank[:, sel],
-                        lhsT=words[identity][:, sel].bitcast(FP8X4), lhsT_scale=scales[identity][:, sel],
-                        rhs=words[key][:, cols].bitcast(FP8X4), rhs_scale=scales[key][:, cols],
-                        start=True, stop=True,
+                        out=bank[:, t * P : (t + 1) * P],
+                        lhsT=eye_words[:, PAD + t * P : PAD + (t + 1) * P].bitcast(FP8X4), lhsT_scale=eye_scales[:],
+                        rhs=codes, rhs_scale=bytes_of_scale, start=True, stop=True,
                     )
                 nc.vector.tensor_tensor(
-                    out=tile[:, b * K_PASS : (b + 1) * K_PASS].rearrange("p (c i t) -> p c t i", i=RUN, t=PACK),
+                    out=interleaved[:, b * K_PASS : (b + 1) * K_PASS].rearrange("p (c i t) -> p c t i", i=RUN, t=PACK),
                     in0=columns(name, first + b * P, P).rearrange("p t (c i) -> p c t i", i=RUN),
                     in1=bank[:].rearrange("p (t c i) -> p c t i", t=PACK, i=RUN),
                     op=ALU.subtract,
                 )
-            return tile
 
-        planes(("eye", 0), HALF)
-        quantise(("eye", 0), 0, eye[:, 0 : PACK * K_PASS])
+        def cast_and_quantise(name, first, width, cast_slot=None, word_slot=None):
+            label = "%s_%d" % (name, first)
+            tile = staged(label, width, cast_slot)
+            cast(name, first, tile[:])
+            tiles = plane_tiles(label, width, word_slot)
+            enter(name, first, width, tiles)
+            quantise(tiles, 0, tile[:])
 
-        planes(("wt0", 0), HALF)
-        quantise(("wt0", 0), 0, cast("wt0", 0, QUARTER, "first_cast")[:])
+        cast_and_quantise("wt0", 0, QUARTER, "first_cast")
         table_words = place("table_words", [P, 2 * 2 * J], U8, "first_cast")
         nc.vector.tensor_copy(
             out=table_words[:].bitcast(U16).rearrange("p (d j) -> p d j", d=2),
             in_=picked_words[:].bitcast(U16).rearrange("p (j d) -> p d j", d=2),
         )
-        quantise(("wt0", 0), QUARTER, cast("wt0", QUARTER, QUARTER)[:])
+        cast_and_quantise("wt0", QUARTER, QUARTER)
 
         pieces = [("wt0", 0), ("wt0", HALF), ("wt1", 0), ("wt1", HALF)]
-        left = leftover("wt0", 0, "left0")
-        for i in range(1, len(pieces)):
+        for i in range(len(pieces) - 1):
             name, first = pieces[i]
-            planes(pieces[i], HALF)
-            quantise(pieces[i], 0, cast(name, first, HALF, "cast%d" % i)[:])
-            before = ("wr" + pieces[i - 1][0][2], pieces[i - 1][1])
-            planes(before, HALF, "cast%d" % i)
-            quantise(before, 0, left[:])
-            left = leftover(name, first, "left%d" % (i % 2), LAST_DECODE_BANKS if i == len(pieces) - 1 else DECODE_BANKS)
+            left = staged("left%d" % i, HALF, "left%d" % (i % 2))
+            leftover(name, first, left[:], DECODE_BANKS)
+            cast_and_quantise(pieces[i + 1][0], pieces[i + 1][1], HALF, "cast%d" % i)
+            tiles = plane_tiles("left%d" % i, HALF, "cast%d" % i)
+            enter("wr" + name[2], first, HALF, tiles)
+            quantise(tiles, 0, left[:])
 
-        group_of = {m: g for g, group in enumerate(WX_GROUPS) for m in group}
-        wx_cast = {}
-
-        def cast_wx(g, slot=None):
-            wx_cast[g] = cast("wx", WX_GROUPS[g][0] * P, len(WX_GROUPS[g]) * P, slot)
-
-        def quantise_wx(g, slot):
-            planes(("wx", g), len(WX_GROUPS[g]) * P, slot)
-            quantise(("wx", g), 0, wx_cast[g][:])
-
+        with_x = staged("with_x", QUARTER + J)
+        tiles = plane_tiles("with_x", QUARTER + J)
+        enter("wr1", HALF, QUARTER, tiles)
+        enter("x", 0, J, tiles, QUARTER)
+        leftover("wt1", HALF, with_x[:, 0 : QUARTER * PACK], LAST_DECODE_BANKS)
         for first in (0, HALF):
-            planes(("x", first), HALF)
-            quantise(("x", first), 0, cast("x", first, HALF)[:])
-        cast_wx(0, "wx_cast0")
-        quantise_wx(0, "wx_group0")
-        planes(("wr1", HALF), HALF, "wx_cast0")
-        quantise(("wr1", HALF), 0, left[:])
-        cast_wx(1)
-        quantise_wx(1, "wx_group1")
+            cast("x", first, with_x[:, (QUARTER + first) * PACK : (QUARTER + first + HALF) * PACK])
+        for first, width in ((0, HALF), (HALF, QUARTER), (HALF + QUARTER, HALF)):
+            quantise(tiles, first, with_x[:, first * PACK : (first + width) * PACK])
+        cast_and_quantise("wx", 0, P, "wx_cast0", "wx_group0")
+        with_wx = staged("with_wx", QUARTER + P, "wx_cast0")
+        leftover("wt1", HALF + QUARTER, with_wx[:, 0 : QUARTER * PACK], LAST_DECODE_BANKS)
+        cast_and_quantise("wx", P, P, None, "wx_group1")
 
         halves = [slice(0, HALF), slice(HALF, J)]
 
-        def sum_bank(i, half):
-            return banks[2 * i % len(banks) + half.start // HALF]
+        def sum_bank(m, half):
+            return banks[2 * m % len(banks) + half.start // HALF]
 
-        def products(i):
-            m = ORDER[i]
-            terms = TABLE_TERMS[::-1] if i == 3 else TABLE_TERMS
-            for s in range(len(terms) + 1):
+        def products(m):
+            for s, name in enumerate(TABLE_TERMS + ("wx",)):
+                codes, bytes_of_scale = operand(name, m * P, P)
                 for half in halves:
-                    if s < len(terms):
-                        a = int(terms[s][2])
-                        key = (terms[s], m * P // HALF * HALF)
-                        first = m * P - key[1]
+                    if name == "wx":
+                        rhs, rhs_scale = operand("x", half.start, HALF)
+                    else:
+                        a = int(name[2])
                         rhs = table_words[:, 2 * (a * J + half.start) : 2 * (a * J + half.stop)].bitcast(FP4X4)
                         rhs_scale = table_scales[a][:, half]
-                    else:
-                        key = ("wx", group_of[m])
-                        first = (m - WX_GROUPS[group_of[m]][0]) * P
-                        rhs, rhs_scale = words[("x", half.start)][:].bitcast(FP8X4), scales[("x", half.start)][:]
-                    rows = slice(first, first + P)
                     nc.tensor.matmul_mx(
-                        out=sum_bank(i, half)[:],
-                        lhsT=words[key][:, rows].bitcast(FP8X4), lhsT_scale=scales[key][:, rows],
-                        rhs=rhs, rhs_scale=rhs_scale, start=(s == 0), stop=(s == len(TABLE_TERMS)),
+                        out=sum_bank(m, half)[:], lhsT=codes, lhsT_scale=bytes_of_scale,
+                        rhs=rhs, rhs_scale=rhs_scale, start=(s == 0), stop=(name == "wx"),
                     )
 
         shared = [place("results01", [P, 2, J], F32, "raw_wt0_0"), place("results23", [P, 2, J], F32, "raw_wt0_%d" % HALF)]
@@ -220,26 +226,36 @@ def tile_list_tiert_resL_kernel(tc, tab_words, tab_scales, wt, x, wx, rT, offs, 
         results = results + [shared[2][:, i, :] for i in range(4)]
 
         last = ROW_TILES - 1
-        cast_slots = {0: (2, "wx_group0"), 1: (3, "wx_group1"), 2: (4, "sum0_0"), 3: (5, "wx_group1")}
-        for i, m in enumerate(ORDER):
-            products(i)
-            for half in halves:
-                summed = place("summed", [P, HALF], F32, "sum%d_%d" % (i % SUM_SLOTS, half.start))
-                nc.scalar.copy(out=summed[:], in_=sum_bank(i, half)[:])
-                parts = [half]
-                if i == last and half.stop == J:
-                    parts = [slice(HALF, HALF + QUARTER), slice(HALF + QUARTER, J)]
-                for part in parts:
-                    listed = offsets[:, part.start // LIST_ROWS : part.stop // LIST_ROWS]
-                    nc.vector.tensor_tensor(
-                        out=results[m][:, part], in0=records[i][:].indirect(listed),
-                        in1=summed[:, part.start - half.start : part.stop - half.start], op=ALU.add,
-                    )
-                    if i == last:
-                        nc.scalar.dma_start(out=out[m * P : (m + 1) * P, part], in_=results[m][:, part])
-            if i < last:
+        for m in range(ROW_TILES):
+            products(m)
+            sums = []
+            if m < HALVED:
+                for half in halves:
+                    sums.append((half, place("summed", [P, HALF], F32, "sum%d_%d" % (m, half.start))[:]))
+                parts = sums
+            else:
+                whole = place("summed", [P, J], F32, "sum%d" % (m % SUM_SLOTS))
+                sums = [(half, whole[:, half]) for half in halves]
+                cuts = [slice(0, J)]
+                if m == last:
+                    cuts = [slice(0, HALF), slice(HALF, HALF + QUARTER), slice(HALF + QUARTER, J)]
+                parts = [(cut, whole[:, cut]) for cut in cuts]
+            for half, summed in sums:
+                nc.scalar.copy(out=summed, in_=sum_bank(m, half)[:])
+            for part, summed in parts:
+                listed = offsets[:, part.start // LIST_ROWS : part.stop // LIST_ROWS]
+                nc.vector.tensor_tensor(out=results[m][:, part], in0=records[m][:].indirect(listed), in1=summed, op=ALU.add)
+                if m == last:
+                    nc.scalar.dma_start(out=out[m * P : (m + 1) * P, part], in_=results[m][:, part])
+            if m < last:
                 nc.sync.dma_start(out=out[m * P : (m + 1) * P, :], in_=results[m])
-            if i in cast_slots:
-                group, slot = cast_slots[i]
-                cast_wx(group, slot)
-                quantise_wx(group, "sum%d_0" % (i % SUM_SLOTS))
+            if m == 0:
+                cast("wx", 2 * P, with_wx[:, QUARTER * PACK : (QUARTER + P) * PACK])
+                tiles = plane_tiles("with_wx", QUARTER + P, "sum0_0")
+                enter("wr1", HALF + QUARTER, QUARTER, tiles)
+                enter("wx", 2 * P, P, tiles, QUARTER)
+                quantise(tiles, 0, with_wx[:])
+            if m == 1:
+                cast_and_quantise("wx", 3 * P, 2 * P, "wx_group1", "sum1_0")
+            if m == 2:
+                cast_and_quantise("wx", 5 * P, 3 * P, "wx_group1", "sum2_0")

@@ -32,6 +32,7 @@ TABLE_TERMS = ("wt0", "wr0", "wt1", "wr1")
 WX_GROUPS = ((0,), (1,), (2,), (3, 4), (5, 6, 7))
 LEAD = T // 4
 PAD = 16
+STORE_GROUPS = ((0, 1, 2, 3), (4, 5), (6,), (7,))
 HALVED = 3
 
 
@@ -220,10 +221,13 @@ def tile_list_tiert_resL_kernel(tc, tab_words, tab_scales, wt, x, wx, rT, offs, 
                         rhs=rhs, rhs_scale=rhs_scale, start=(s == 0), stop=(name == "wx"),
                     )
 
-        shared = [place("results01", [P, 2, J], F32, "raw_wt0_0"), place("results23", [P, 2, J], F32, "raw_wt0_%d" % HALF)]
-        shared.append(place("results4567", [P, 4, J], F32, "raw_wt1_0"))
-        results = [shared[0][:, 0, :], shared[0][:, 1, :], shared[1][:, 0, :], shared[1][:, 1, :]]
-        results = results + [shared[2][:, i, :] for i in range(4)]
+        slots = ("raw_wt1_0", "raw_wt0_0", "raw_wt0_%d" % HALF, "raw_x_0")
+        results, closes = {}, {}
+        for group, slot in zip(STORE_GROUPS, slots):
+            shared = place("results%d" % group[0], [P, len(group), J], F32, slot)
+            closes[group[-1]] = (group, shared)
+            for i, m in enumerate(group):
+                results[m] = shared[:, i, :]
 
         last = ROW_TILES - 1
         for m in range(ROW_TILES):
@@ -238,7 +242,7 @@ def tile_list_tiert_resL_kernel(tc, tab_words, tab_scales, wt, x, wx, rT, offs, 
                 sums = [(half, whole[:, half]) for half in halves]
                 cuts = [slice(0, J)]
                 if m == last:
-                    cuts = [slice(0, HALF), slice(HALF, HALF + QUARTER), slice(HALF + QUARTER, J)]
+                    cuts = [slice(0, J - QUARTER), slice(J - QUARTER, J)]
                 parts = [(cut, whole[:, cut]) for cut in cuts]
             for half, summed in sums:
                 nc.scalar.copy(out=summed, in_=sum_bank(m, half)[:])
@@ -247,8 +251,10 @@ def tile_list_tiert_resL_kernel(tc, tab_words, tab_scales, wt, x, wx, rT, offs, 
                 nc.vector.tensor_tensor(out=results[m][:, part], in0=records[m][:].indirect(listed), in1=summed, op=ALU.add)
                 if m == last:
                     nc.scalar.dma_start(out=out[m * P : (m + 1) * P, part], in_=results[m][:, part])
-            if m < last:
-                nc.sync.dma_start(out=out[m * P : (m + 1) * P, :], in_=results[m])
+            if m < last and m in closes:
+                group, shared = closes[m]
+                rows = out[group[0] * P : (m + 1) * P, :].rearrange("(m p) j -> p m j", p=P)
+                nc.sync.dma_start(out=rows, in_=shared[:])
             if m == 0:
                 cast("wx", 2 * P, with_wx[:, QUARTER * PACK : (QUARTER + P) * PACK])
                 tiles = plane_tiles("with_wx", QUARTER + P, "sum0_0")

@@ -144,6 +144,14 @@ def tile_list_tiert_resL_kernel(tc, tab_words, tab_scales, wt, x, wx, rT, offs, 
                 in_=columns(name, first, interleaved.shape[1] // PACK).rearrange("p t (c i) -> p c t i", i=RUN),
             )
 
+        def cast_aside(name, first, width, slot):
+            tile = staged("aside_%s_%d" % (name, first), width, slot)
+            nc.gpsimd.tensor_scalar(
+                out=tile[:].rearrange("p (c t) -> p c t", t=PACK), in0=columns(name, first, width).rearrange("p t c -> p c t"),
+                scalar1=1.0, scalar2=0.0, op0=ALU.mult, op1=ALU.add,
+            )
+            return tile
+
         def leftover(name, first, interleaved, places):
             for b in range(interleaved.shape[1] // K_PASS):
                 bank = banks[places[b]]
@@ -182,19 +190,29 @@ def tile_list_tiert_resL_kernel(tc, tab_words, tab_scales, wt, x, wx, rT, offs, 
             name, first = pieces[i]
             left = staged("left%d" % i, HALF, "left%d" % (i % 2))
             leftover(name, first, left[:], DECODE_BANKS)
-            cast_and_quantise(pieces[i + 1][0], pieces[i + 1][1], HALF, "cast%d" % i)
+            if pieces[i + 1] == ("wt1", 0):
+                aside = cast_aside("wt1", QUARTER, QUARTER, "left0")
+                cast_and_quantise("wt1", 0, QUARTER, "cast%d" % i)
+                tiles = plane_tiles("aside", QUARTER)
+                enter("wt1", QUARTER, QUARTER, tiles)
+                quantise(tiles, 0, aside[:])
+            else:
+                cast_and_quantise(pieces[i + 1][0], pieces[i + 1][1], HALF, "cast%d" % i)
             tiles = plane_tiles("left%d" % i, HALF, "cast%d" % i)
             enter("wr" + name[2], first, HALF, tiles)
             quantise(tiles, 0, left[:])
 
-        with_x = staged("with_x", QUARTER + J)
+        aside = cast_aside("x", J - P, P, "left0")
+        with_x = staged("with_x", QUARTER + J - P)
         tiles = plane_tiles("with_x", QUARTER + J)
         enter("wr1", HALF, QUARTER, tiles)
         enter("x", 0, J, tiles, QUARTER)
         leftover("wt1", HALF, with_x[:, 0 : QUARTER * PACK], LAST_DECODE_BANKS)
-        for first in (0, HALF):
-            cast("x", first, with_x[:, (QUARTER + first) * PACK : (QUARTER + first + HALF) * PACK])
-        for first, width in ((0, HALF), (HALF, QUARTER), (HALF + QUARTER, HALF)):
+        for first, width in ((0, HALF), (HALF, HALF - P)):
+            cast("x", first, with_x[:, (QUARTER + first) * PACK : (QUARTER + first + width) * PACK])
+        quantise(tiles, 0, with_x[:, 0 : HALF * PACK])
+        quantise(tiles, QUARTER + J - P, aside[:])
+        for first, width in ((HALF, QUARTER), (HALF + QUARTER, HALF - P)):
             quantise(tiles, first, with_x[:, first * PACK : (first + width) * PACK])
         cast_and_quantise("wx", 0, P, "wx_cast0", "wx_group0")
         with_wx = staged("with_wx", QUARTER + P, "wx_cast0")

@@ -33,6 +33,8 @@ WX_GROUPS = ((0,), (1,), (2,), (3, 4), (5, 6, 7))
 LEAD = T // 4
 PAD = 16
 STORE_GROUPS = ((0, 1, 2, 3), (4, 5), (6,), (7,))
+DMA_ALIGN = 256
+DMA_SLOTS = ("record", "raw_", "scale_window", "picked_scales", "second_scales")
 HALVED = 3
 
 
@@ -43,7 +45,8 @@ def tile_list_tiert_resL_kernel(tc, tab_words, tab_scales, wt, x, wx, rT, offs, 
         psum = ctx.enter_context(tc.psum_pool(name="psum", bufs=1))
 
         def place(name, shape, dtype, slot=None):
-            return keep.tile(shape, dtype, name=name, tag=slot or name, align_bytes=64)
+            tag = slot or name
+            return keep.tile(shape, dtype, name=name, tag=tag, align_bytes=DMA_ALIGN if tag.startswith(DMA_SLOTS) else 64)
 
         offsets = keep.tile([P, J // LIST_ROWS], U16, name="offsets")
         word_window = place("word_window", [P, T], I32, "record%d" % (ROW_TILES - 1))
@@ -152,22 +155,32 @@ def tile_list_tiert_resL_kernel(tc, tab_words, tab_scales, wt, x, wx, rT, offs, 
             )
             return tile
 
+        def decode(name, first, bank):
+            codes, bytes_of_scale = operand(name, first, P)
+            for t in range(PACK):
+                nc.tensor.matmul_mx(
+                    out=bank[:, t * P : (t + 1) * P],
+                    lhsT=eye_words[:, PAD + t * P : PAD + (t + 1) * P].bitcast(FP8X4), lhsT_scale=eye_scales[:],
+                    rhs=codes, rhs_scale=bytes_of_scale, start=True, stop=True,
+                )
+
         def leftover(name, first, interleaved, places):
             for b in range(interleaved.shape[1] // K_PASS):
                 bank = banks[places[b]]
-                codes, bytes_of_scale = operand(name, first + b * P, P)
-                for t in range(PACK):
-                    nc.tensor.matmul_mx(
-                        out=bank[:, t * P : (t + 1) * P],
-                        lhsT=eye_words[:, PAD + t * P : PAD + (t + 1) * P].bitcast(FP8X4), lhsT_scale=eye_scales[:],
-                        rhs=codes, rhs_scale=bytes_of_scale, start=True, stop=True,
-                    )
+                decode(name, first + b * P, bank)
                 nc.vector.tensor_tensor(
                     out=interleaved[:, b * K_PASS : (b + 1) * K_PASS].rearrange("p (c i t) -> p c t i", i=RUN, t=PACK),
                     in0=columns(name, first + b * P, P).rearrange("p t (c i) -> p c t i", i=RUN),
                     in1=bank[:].rearrange("p (t c i) -> p c t i", t=PACK, i=RUN),
                     op=ALU.subtract,
                 )
+
+        def hand_over(name, first):
+            bank = banks[DECODE_BANKS[-2]]
+            decode(name, first, bank)
+            copied = place("copied", [P, P, PACK], F32)
+            nc.scalar.copy(out=copied[:], in_=bank[:].rearrange("p (t c) -> p c t", t=PACK))
+            return name, first, copied
 
         def cast_and_quantise(name, first, width, cast_slot=None, word_slot=None):
             label = "%s_%d" % (name, first)
@@ -186,20 +199,33 @@ def tile_list_tiert_resL_kernel(tc, tab_words, tab_scales, wt, x, wx, rT, offs, 
         cast_and_quantise("wt0", QUARTER, QUARTER)
 
         pieces = [("wt0", 0), ("wt0", HALF), ("wt1", 0), ("wt1", HALF)]
+        handed = None
         for i in range(len(pieces) - 1):
             name, first = pieces[i]
-            left = staged("left%d" % i, HALF, "left%d" % (i % 2))
+            width = HALF - P if i == 0 else HALF
+            left = staged("left%d" % i, width, "left%d" % (i % 2))
+            if i == 2:
+                late = staged("late", P, "left1")
+                nc.gpsimd.tensor_tensor(
+                    out=late[:].rearrange("p (c t) -> p c t", t=PACK),
+                    in0=columns(handed[0], handed[1], P).rearrange("p t c -> p c t"), in1=handed[2][:], op=ALU.subtract,
+                )
             leftover(name, first, left[:], DECODE_BANKS)
-            if pieces[i + 1] == ("wt1", 0):
+            if i == 0:
+                handed = hand_over(name, width)
+            if i == 1:
                 aside = cast_aside("wt1", QUARTER, QUARTER, "left0")
                 cast_and_quantise("wt1", 0, QUARTER, "cast%d" % i)
                 tiles = plane_tiles("aside", QUARTER)
                 enter("wt1", QUARTER, QUARTER, tiles)
                 quantise(tiles, 0, aside[:])
             else:
-                cast_and_quantise(pieces[i + 1][0], pieces[i + 1][1], HALF, "cast%d" % i)
-            tiles = plane_tiles("left%d" % i, HALF, "cast%d" % i)
-            enter("wr" + name[2], first, HALF, tiles)
+                cast_and_quantise(pieces[i + 1][0], pieces[i + 1][1], HALF, "cast%d" % i, "copied" if i == 2 else None)
+            tiles = plane_tiles("left%d" % i, width + P if i == 2 else width, "cast%d" % i)
+            enter("wr" + name[2], first, width, tiles)
+            if i == 2:
+                enter("wr0", handed[1], P, tiles, width)
+                quantise(tiles, width, late[:])
             quantise(tiles, 0, left[:])
 
         aside = cast_aside("x", J - P, P, "left0")

@@ -30,7 +30,7 @@ DECODE_BANKS = (4, 5, 6, 7)
 LAST_DECODE_BANKS = (6, 7, 6, 7)
 TABLE_TERMS = ("wt0", "wr0", "wt1", "wr1")
 WX_GROUPS = ((0,), (1,), (2,), (3, 4), (5, 6, 7))
-LEAD = T // 4
+LEAD = 3 * T // 8
 PAD = 16
 STORE_GROUPS = ((0, 1, 2, 3), (4, 5), (6,), (7,))
 DMA_ALIGN = 256
@@ -147,14 +147,6 @@ def tile_list_tiert_resL_kernel(tc, tab_words, tab_scales, wt, x, wx, rT, offs, 
                 in_=columns(name, first, interleaved.shape[1] // PACK).rearrange("p t (c i) -> p c t i", i=RUN),
             )
 
-        def cast_aside(name, first, width, slot):
-            tile = staged("aside_%s_%d" % (name, first), width, slot)
-            nc.gpsimd.tensor_scalar(
-                out=tile[:].rearrange("p (c t) -> p c t", t=PACK), in0=columns(name, first, width).rearrange("p t c -> p c t"),
-                scalar1=1.0, scalar2=0.0, op0=ALU.mult, op1=ALU.add,
-            )
-            return tile
-
         def decode(name, first, bank):
             codes, bytes_of_scale = operand(name, first, P)
             for t in range(PACK):
@@ -213,14 +205,7 @@ def tile_list_tiert_resL_kernel(tc, tab_words, tab_scales, wt, x, wx, rT, offs, 
             leftover(name, first, left[:], DECODE_BANKS)
             if i == 0:
                 handed = hand_over(name, width)
-            if i == 1:
-                aside = cast_aside("wt1", QUARTER, QUARTER, "left0")
-                cast_and_quantise("wt1", 0, QUARTER, "cast%d" % i)
-                tiles = plane_tiles("aside", QUARTER)
-                enter("wt1", QUARTER, QUARTER, tiles)
-                quantise(tiles, 0, aside[:])
-            else:
-                cast_and_quantise(pieces[i + 1][0], pieces[i + 1][1], HALF, "cast%d" % i, "copied" if i == 2 else None)
+            cast_and_quantise(pieces[i + 1][0], pieces[i + 1][1], HALF, "cast%d" % i, "copied" if i == 2 else None)
             tiles = plane_tiles("left%d" % i, width + P if i == 2 else width, "cast%d" % i)
             enter("wr" + name[2], first, width, tiles)
             if i == 2:
@@ -228,17 +213,14 @@ def tile_list_tiert_resL_kernel(tc, tab_words, tab_scales, wt, x, wx, rT, offs, 
                 quantise(tiles, width, late[:])
             quantise(tiles, 0, left[:])
 
-        aside = cast_aside("x", J - P, P, "left0")
-        with_x = staged("with_x", QUARTER + J - P)
+        with_x = staged("with_x", QUARTER + J)
         tiles = plane_tiles("with_x", QUARTER + J)
         enter("wr1", HALF, QUARTER, tiles)
         enter("x", 0, J, tiles, QUARTER)
         leftover("wt1", HALF, with_x[:, 0 : QUARTER * PACK], LAST_DECODE_BANKS)
-        for first, width in ((0, HALF), (HALF, HALF - P)):
-            cast("x", first, with_x[:, (QUARTER + first) * PACK : (QUARTER + first + width) * PACK])
-        quantise(tiles, 0, with_x[:, 0 : HALF * PACK])
-        quantise(tiles, QUARTER + J - P, aside[:])
-        for first, width in ((HALF, QUARTER), (HALF + QUARTER, HALF - P)):
+        for first in (0, HALF):
+            cast("x", first, with_x[:, (QUARTER + first) * PACK : (QUARTER + first + HALF) * PACK])
+        for first, width in ((0, HALF), (HALF, QUARTER), (HALF + QUARTER, HALF)):
             quantise(tiles, first, with_x[:, first * PACK : (first + width) * PACK])
         cast_and_quantise("wx", 0, P, "wx_cast0", "wx_group0")
         with_wx = staged("with_wx", QUARTER + P, "wx_cast0")

from contextlib import ExitStack

import concourse.mybir as mybir

K, L, N, T, J = 1024, 512, 1024, 2048, 1024
FLOPS = 2 * (2 * K + L) * N * J + 2 * 512 * K * N

F32 = mybir.dt.float32
BF16 = mybir.dt.bfloat16
I32 = mybir.dt.int32
U32 = mybir.dt.uint32
U16 = mybir.dt.uint16
U8 = mybir.dt.uint8
FP8X4 = mybir.dt.float8_e4m3fn_x4
FP4X4 = mybir.dt.float4_e2m1fn_x4
ALU = mybir.AluOpType

P = 128
PACK = 4
K_PASS = P * PACK
QUAD = 32
LIST_ROWS = 16
HALF = 512
QUARTER = HALF // 2
RUN = 2
ROW_TILES = N // P
SUM_SLOTS = 3
SECOND_ROWS = 16
DECODE_BANKS = (4, 5, 6, 7)
LAST_DECODE_BANKS = (6, 7, 6, 7)
TABLE_TERMS = ("wt0", "wr0", "wt1", "wr1")
WX_GROUPS = ((0,), (1,), (2,), (3, 4), (5, 6, 7))
LEAD = 3 * T // 8
PAD = 16
STORE_GROUPS = ((0, 1, 2, 3), (4, 5), (6,), (7,))
DMA_ALIGN = 256
DMA_SLOTS = ("record", "raw_", "scale_window", "picked_scales", "second_scales")
HALVED = 3


def tile_list_tiert_resL_kernel(tc, tab_words, tab_scales, wt, x, wx, rT, offs, out):
    nc = tc.nc
    with ExitStack() as ctx:
        keep = ctx.enter_context(tc.tile_pool(name="keep", bufs=1))
        psum = ctx.enter_context(tc.psum_pool(name="psum", bufs=1))

        def place(name, shape, dtype, slot=None):
            tag = slot or name
            return keep.tile(shape, dtype, name=name, tag=tag, align_bytes=DMA_ALIGN if tag.startswith(DMA_SLOTS) else 64)

        offsets = keep.tile([P, J // LIST_ROWS], U16, name="offsets")
        word_window = place("word_window", [P, T], I32, "record%d" % (ROW_TILES - 1))
        word_rows = tab_words[0].rearrange("p t b -> p (t b)").bitcast(I32)
        nc.sync.dma_start(out=word_window[:, 0:LEAD], in_=word_rows[:, 0:LEAD])
        nc.sync.dma_start(offsets[:], offs)

        scale_window = place("scale_window", [P, T + 4], U8)
        eye = place("eye", [P, K_PASS], BF16)
        eye_words = place("eye_words", [P, PAD + HALF], U32)
        eye_scales = place("eye_scales", [P, P], U8)
        ones = place("ones", [P, P], F32)
        ramp = place("ramp", [P, P], F32)
        turned = place("turned", [P, QUAD], F32)
        nc.gpsimd.memset(scale_window[:, 0 : T // 2].bitcast(I32), 0)
        nc.vector.memset(scale_window[:, T // 2 : T + 4].bitcast(I32), 0)
        nc.gpsimd.memset(ones[:], 1.0)
        nc.gpsimd.memset(eye[:].bitcast(I32), 0)
        nc.gpsimd.memset(eye_words[:, PAD - 1 : PAD].bitcast(I32), 0)
        nc.vector.tensor_tensor_scan(out=ramp[:], data0=ones[:], data1=ones[:], initial=-1.0, op0=ALU.mult, op1=ALU.add)
        nc.vector.transpose(out=turned[:], in_=ramp[:, 0:QUAD])
        for q in range(P // QUAD):
            quadrant = slice(QUAD * q, QUAD * (q + 1))
            nc.vector.tensor_scalar(
                out=eye[quadrant, P * q : P * (q + 1)], in0=ramp[quadrant, :],
                scalar1=1.0 / PACK, scalar2=turned[quadrant, 0:1], op0=ALU.mult, op1=ALU.is_equal,
            )
        nc.vector.quantize_mx(out=eye_words[:, PAD : PAD + P].bitcast(FP8X4), scales=eye_scales[:], in_=eye[:])
        eye_bytes, eye_pairs = eye_words[:].bitcast(U8), eye_words[:].bitcast(U16)
        nc.gpsimd.tensor_copy(
            out=eye_bytes[:, 4 * (PAD + P) : 4 * (PAD + 2 * P)], in_=eye_bytes[:, 4 * PAD - 1 : 4 * (PAD + P) - 1],
        )
        nc.scalar.copy(
            out=eye_pairs[:, 2 * (PAD + 2 * P) : 2 * (PAD + 4 * P)], in_=eye_pairs[:, 2 * PAD - 1 : 2 * (PAD + 2 * P) - 1],
        )

        sources = {"wt0": wt[0:K_PASS, :], "wt1": wt[K_PASS:K, :], "x": x, "wx": wx}
        loaded = {}

        def load(name, first=0, width=N):
            raw = place("raw_%s_%d" % (name, first), [P, PACK, width], F32)
            rows = sources[name].rearrange("(p t) n -> p t n", t=PACK)
            nc.sync.dma_start(out=raw[:], in_=rows[:, :, first : first + width])
            loaded[(name, first)] = raw

        def columns(name, first, width):
            start = max(s for n, s in loaded if n == name and s <= first)
            return loaded[(name, start)][:, :, first - start : first - start + width]

        by_row = tab_scales.bitcast(I32).rearrange("a (q r) t -> r q a t", r=PACK)
        for r in range(PACK):
            nc.sync.dma_start(out=scale_window[r:P:SECOND_ROWS, 0:T].bitcast(I32), in_=by_row[r])
        nc.sync.dma_start(out=word_window[:, LEAD:T], in_=word_rows[:, LEAD:T])
        load("wt0", 0, HALF)
        load("wt0", HALF, HALF)
        load("wt1")

        picked_words = place("picked_words", [P, J], U32)
        picked_scales = place("picked_scales", [P, J], U8)
        second_scales = place("second_scales", [P, J], U8)
        table_scales = [picked_scales, second_scales]
        nc.vector.tensor_copy(picked_scales[:], scale_window[:].indirect(offsets[:]))
        nc.vector.tensor_copy(picked_words[:], word_window[:].bitcast(U32).indirect(offsets[:]))
        nc.gpsimd.memset(second_scales[:].bitcast(I32), 0)
        nc.sync.dma_start(out=second_scales[0 : P - SECOND_ROWS, :].bitcast(I32), in_=picked_scales[SECOND_ROWS:P, :].bitcast(I32))

        load("x")
        load("wx")
        records = []
        for m in range(ROW_TILES):
            records.append(place("record%d" % m, [P, T], F32))
            nc.sync.dma_start(out=records[m][:], in_=rT[m * P : (m + 1) * P, :])

        banks = [psum.tile([P, HALF], F32, name="bank%d" % i) for i in range(8)]
        planes = {}

        def plane_tiles(name, width, slot=None):
            return place("words_" + name, [P, width], U32, slot), place("scales_" + name, [P, width], U8)

        def quantise(tiles, first, interleaved):
            cols = slice(first, first + interleaved.shape[1] // PACK)
            nc.vector.quantize_mx(out=tiles[0][:, cols].bitcast(FP8X4), scales=tiles[1][:, cols], in_=interleaved)

        def enter(name, first, width, tiles, at=0):
            for b in range(width // P):
                planes[(name, first + b * P)] = (tiles, at + b * P)

        def operand(name, first, width):
            tiles, at = planes[(name, first)]
            return tiles[0][:, at : at + width].bitcast(FP8X4), tiles[1][:, at : at + width]

        def staged(name, width, slot=None):
            return place("staged_" + name, [P, width * PACK], BF16, slot)

        def cast(name, first, interleaved):
            nc.scalar.copy(
                out=interleaved.rearrange("p (c i t) -> p c t i", i=RUN, t=PACK),
                in_=columns(name, first, interleaved.shape[1] // PACK).rearrange("p t (c i) -> p c t i", i=RUN),
            )

        def decode(name, first, bank):
            codes, bytes_of_scale = operand(name, first, P)
            for t in range(PACK):
                nc.tensor.matmul_mx(
                    out=bank[:, t * P : (t + 1) * P],
                    lhsT=eye_words[:, PAD + t * P : PAD + (t + 1) * P].bitcast(FP8X4), lhsT_scale=eye_scales[:],
                    rhs=codes, rhs_scale=bytes_of_scale, start=True, stop=True,
                )

        def leftover(name, first, interleaved, places):
            for b in range(interleaved.shape[1] // K_PASS):
                bank = banks[places[b]]
                decode(name, first + b * P, bank)
                nc.vector.tensor_tensor(
                    out=interleaved[:, b * K_PASS : (b + 1) * K_PASS].rearrange("p (c i t) -> p c t i", i=RUN, t=PACK),
                    in0=columns(name, first + b * P, P).rearrange("p t (c i) -> p c t i", i=RUN),
                    in1=bank[:].rearrange("p (t c i) -> p c t i", t=PACK, i=RUN),
                    op=ALU.subtract,
                )

        def hand_over(name, first):
            bank = banks[DECODE_BANKS[-2]]
            decode(name, first, bank)
            copied = place("copied", [P, P, PACK], F32)
            nc.scalar.copy(out=copied[:], in_=bank[:].rearrange("p (t c) -> p c t", t=PACK))
            return name, first, copied

        def cast_and_quantise(name, first, width, cast_slot=None, word_slot=None):
            label = "%s_%d" % (name, first)
            tile = staged(label, width, cast_slot)
            cast(name, first, tile[:])
            tiles = plane_tiles(label, width, word_slot)
            enter(name, first, width, tiles)
            quantise(tiles, 0, tile[:])

        cast_and_quantise("wt0", 0, QUARTER, "first_cast")
        table_words = place("table_words", [P, 2 * 2 * J], U8, "first_cast")
        nc.vector.tensor_copy(
            out=table_words[:].bitcast(U16).rearrange("p (d j) -> p d j", d=2),
            in_=picked_words[:].bitcast(U16).rearrange("p (j d) -> p d j", d=2),
        )
        cast_and_quantise("wt0", QUARTER, QUARTER)

        pieces = [("wt0", 0), ("wt0", HALF), ("wt1", 0), ("wt1", HALF)]
        handed = None
        for i in range(len(pieces) - 1):
            name, first = pieces[i]
            width = HALF - P if i == 0 else HALF
            left = staged("left%d" % i, width, "left%d" % (i % 2))
            if i == 2:
                late = staged("late", P, "left1")
                nc.gpsimd.tensor_tensor(
                    out=late[:].rearrange("p (c t) -> p c t", t=PACK),
                    in0=columns(handed[0], handed[1], P).rearrange("p t c -> p c t"), in1=handed[2][:], op=ALU.subtract,
                )
            leftover(name, first, left[:], DECODE_BANKS)
            if i == 0:
                handed = hand_over(name, width)
            cast_and_quantise(pieces[i + 1][0], pieces[i + 1][1], HALF, "cast%d" % i, "copied" if i == 2 else None)
            tiles = plane_tiles("left%d" % i, width + P if i == 2 else width, "cast%d" % i)
            enter("wr" + name[2], first, width, tiles)
            if i == 2:
                enter("wr0", handed[1], P, tiles, width)
                quantise(tiles, width, late[:])
            quantise(tiles, 0, left[:])

        with_x = staged("with_x", QUARTER + J)
        tiles = plane_tiles("with_x", QUARTER + J)
        enter("wr1", HALF, QUARTER, tiles)
        enter("x", 0, J, tiles, QUARTER)
        leftover("wt1", HALF, with_x[:, 0 : QUARTER * PACK], LAST_DECODE_BANKS)
        for first in (0, HALF):
            cast("x", first, with_x[:, (QUARTER + first) * PACK : (QUARTER + first + HALF) * PACK])
        for first, width in ((0, HALF), (HALF, QUARTER), (HALF + QUARTER, HALF)):
            quantise(tiles, first, with_x[:, first * PACK : (first + width) * PACK])
        cast_and_quantise("wx", 0, P, "wx_cast0", "wx_group0")
        with_wx = staged("with_wx", QUARTER + P, "wx_cast0")
        leftover("wt1", HALF + QUARTER, with_wx[:, 0 : QUARTER * PACK], LAST_DECODE_BANKS)
        cast_and_quantise("wx", P, P, None, "wx_group1")

        halves = [slice(0, HALF), slice(HALF, J)]

        def sum_bank(m, half):
            return banks[2 * m % len(banks) + half.start // HALF]

        def products(m):
            for s, name in enumerate(TABLE_TERMS + ("wx",)):
                codes, bytes_of_scale = operand(name, m * P, P)
                for half in halves:
                    if name == "wx":
                        rhs, rhs_scale = operand("x", half.start, HALF)
                    else:
                        a = int(name[2])
                        rhs = table_words[:, 2 * (a * J + half.start) : 2 * (a * J + half.stop)].bitcast(FP4X4)
                        rhs_scale = table_scales[a][:, half]
                    nc.tensor.matmul_mx(
                        out=sum_bank(m, half)[:], lhsT=codes, lhsT_scale=bytes_of_scale,
                        rhs=rhs, rhs_scale=rhs_scale, start=(s == 0), stop=(name == "wx"),
                    )

        slots = ("raw_wt1_0", "raw_wt0_0", "raw_wt0_%d" % HALF, "raw_x_0")
        results, closes = {}, {}
        for group, slot in zip(STORE_GROUPS, slots):
            shared = place("results%d" % group[0], [P, len(group), J], F32, slot)
            closes[group[-1]] = (group, shared)
            for i, m in enumerate(group):
                results[m] = shared[:, i, :]

        last = ROW_TILES - 1
        for m in range(ROW_TILES):
            products(m)
            sums = []
            if m < HALVED:
                for half in halves:
                    sums.append((half, place("summed", [P, HALF], F32, "sum%d_%d" % (m, half.start))[:]))
                parts = sums
            else:
                whole = place("summed", [P, J], F32, "sum%d" % (m % SUM_SLOTS))
                sums = [(half, whole[:, half]) for half in halves]
                cuts = [slice(0, J)]
                if m == last:
                    cuts = [slice(0, J - QUARTER), slice(J - QUARTER, J)]
                parts = [(cut, whole[:, cut]) for cut in cuts]
            for half, summed in sums:
                nc.scalar.copy(out=summed, in_=sum_bank(m, half)[:])
            for part, summed in parts:
                listed = offsets[:, part.start // LIST_ROWS : part.stop // LIST_ROWS]
                nc.vector.tensor_tensor(out=results[m][:, part], in0=records[m][:].indirect(listed), in1=summed, op=ALU.add)
                if m == last:
                    nc.scalar.dma_start(out=out[m * P : (m + 1) * P, part], in_=results[m][:, part])
            if m < last and m in closes:
                group, shared = closes[m]
                rows = out[group[0] * P : (m + 1) * P, :].rearrange("(m p) j -> p m j", p=P)
                nc.sync.dma_start(out=rows, in_=shared[:])
            if m == 0:
                cast("wx", 2 * P, with_wx[:, QUARTER * PACK : (QUARTER + P) * PACK])
                tiles = plane_tiles("with_wx", QUARTER + P, "sum0_0")
                enter("wr1", HALF + QUARTER, QUARTER, tiles)
                enter("wx", 2 * P, P, tiles, QUARTER)
                quantise(tiles, 0, with_wx[:])
            if m == 1:
                cast_and_quantise("wx", 3 * P, 2 * P, "wx_group1", "sum1_0")
            if m == 2:
                cast_and_quantise("wx", 5 * P, 3 * P, "wx_group1", "sum2_0")
